import numpy as np, ml_dtypes
CORES = [6,15,38,47]
N = 4
BF = ml_dtypes.bfloat16
def gentries(a):
    return np.ascontiguousarray(a.reshape(8, 16, -1).transpose(0, 2, 1)).reshape(8, -1)
def gtable(e):
    e = np.asarray(e); return np.ascontiguousarray(e.reshape(8, -1, 16).transpose(0, 2, 1)).reshape(128, -1).astype(np.int32)
W, C, M, V, E = 4096, 256, 16, 6, 3
def parts(rng):
    u = rng.random((N, 8, 16, W), dtype=np.float32); z = rng.random((N, 8, 16, W), dtype=np.float32); ty = rng.integers(0, 3, (N, 8, 1, W))
    u = np.where(ty == 0, np.minimum(u, z), np.where(ty == 1, u, np.maximum(u, z)))
    here = rng.random((N, 8, 16, W)) < 0.35 + 0.65 * rng.random((N, 8, 1, W))
    x = np.where(here, np.minimum(1 + (255 * u).astype(np.int64), 255), 0)
    L = rng.integers(0, W, (N, 8, C, 16)); k = (rng.random((N, 8, C, 16)) < 0.25).astype(np.int64)
    o = np.argsort(rng.random((N, 8, W)), axis=-1)[..., :M * C]
    t = rng.integers(0, 256, (N, 8, 16, C)); w = rng.integers(0, 4096, (N, 8, 16)); th = rng.integers(3, 10, (N, 8, V))
    return x, L, k, np.ascontiguousarray(o), t, w, th
def deep(rng, x, L, k, o, th, g):
    n = C // 4; z = n * (M // 4); slots = np.concatenate([np.array([0]), 1 + rng.permutation(C - 2)[:n - 2], np.array([C - 1])])
    p = rng.permutation(W); u, d, full, none, half = p[:3], p[3:6], p[6:10], p[10:12], p[12:14]; used = p[14:14 + N * z].reshape(N, z)
    y = x[:, g]; y[..., u] = 1; y[..., used.reshape(-1)] = 1; y[..., full] = 255; y[..., none] = 0
    y[..., d] = np.where(np.argsort(rng.random((N, 16, 3)), axis=1) < 2, 255, 1)
    y[..., half] = np.where(np.argsort(rng.random((N, 16, 2)), axis=1) < 8, 255, 1)
    for r in range(N):
        a = np.zeros((C, M), np.int64); rest = np.ones((C, M), bool); rest[slots, ::4] = False
        a[~rest] = rng.permutation(used[r]); a[rest] = rng.permutation(np.setdiff1d(p, used[r]))[:M * C - z]
        o[r, g] = a.reshape(-1)
    kind = rng.integers(0, 3, (N, C, 1)); ff = rng.choice(full, (N, C, 16)); fe = rng.choice(np.concatenate([full, none]), (N, C, 16))
    a = np.where(kind < 2, fe, ff); a[..., 0] = np.where(kind[..., 0] == 2, rng.choice(u, (N, C)), a[..., 0]); b = np.where(kind < 2, rng.integers(0, 2, (N, C, 16)), 0)
    q = ff[:, slots]; q[..., 0] = rng.choice(u, (N, n)); q[..., 1:3] = rng.choice(d, (N, n, 2)); q[..., 3] = rng.choice(half, (N, n)); a[:, slots] = q; b[:, slots] = 1
    L[:, g] = a; k[:, g] = b; th[:, g] = rng.choice(np.array([8, 15]), (N, V)); th[:, g, :2] = 1
    if g == 7:
        th[:, g, 2:5] = 15; th[:, g, 5:] = 8
def pack(x, L, k, o, t, w, th):
    return {"dep": np.ascontiguousarray(x.reshape(N, 128, W)).astype(np.float32).astype(BF), "nam": np.stack([gtable(a.reshape(8, -1)) for a in L]), "mrk": np.stack([gtable(a.reshape(8, -1)) for a in k]),
            "own": np.stack([gtable(a) for a in o]), "pic": np.ascontiguousarray(t.reshape(N, 128, C)).astype(np.float32).astype(BF), "wt": w.reshape(N, 128, 1).astype(np.int32), "thr": np.ascontiguousarray(th).astype(np.int32)}
def setup_inputs(rng):
    return pack(*parts(rng))
def setup_inputs_spread(rng):
    x, L, k, o, t, w, th = parts(rng)
    x = np.minimum(np.exp2(8 * np.sqrt(rng.random((N, 8, 1, W))) * rng.random((N, 8, 16, W))).astype(np.int64) - 1, 255)
    t = np.minimum(np.exp2(8 * rng.random((N, 8, 16, C))).astype(np.int64) - 1, 255); w = np.minimum(np.exp2(12 * rng.random((N, 8, 16))).astype(np.int64) - 1, 4095)
    L = np.minimum((W * rng.random((N, 8, C, 16)) ** 3).astype(np.int64), W - 1); k = (rng.random((N, 8, C, 16)) < rng.random((N, 8, C, 1))).astype(np.int64)
    th = 1 + (14 * rng.random((N, 8, V)) ** 2).astype(np.int64)
    return pack(x, L, k, o, t, w, th)
def setup_inputs_ends(rng):
    x, L, k, o, t, w, th = parts(rng); lane = np.arange(16)[:, None]
    b = 255 * rng.integers(0, 2, (N, 8, 16, W)); q = rng.random((N, 8, 1, W))
    x = np.where(q < 0.2, b, np.where(q < 0.42, 255, np.where(q < 0.65, 1, np.where(q < 0.75, np.maximum(b, 1), np.where(q < 0.9, np.where(lane == 15, 1, 255), 0)))))
    for g in range(8):
        if g % 2 == 0 or g == 7:
            x[:, g, :, 0] = 1; x[:, g, :, W - 1] = 255
        else:
            x[:, g, :, 0] = 255; x[:, g, 15, 0] = 1; x[:, g, :, W - 1] = 1
    u = rng.random((N, 8, C, 16)); L = np.where(u < 0.36, 0, np.where(u < 0.72, W - 1, L)); k = rng.integers(0, 2, (N, 8, C, 16))
    L[:, 7, 0] = W - 1; L[:, 7, C - 1] = W - 1
    L[:, 7, 1] = 0; L[:, 7, C - 2] = 0; L[:, 7, 1, 15] = W - 1; L[:, 7, C - 2, 15] = W - 1; k[:, 7, 1] = 0; k[:, 7, C - 2] = 1
    h = (M * C) // 2; mid = np.concatenate([np.arange(1, M * C - h), np.arange(W - h, W - 1)]); c = (C - 1) * M
    for r in range(N):
        for g in range(8):
            p = rng.permutation(mid); o[r, g] = np.concatenate([p[:c], np.array([0]), p[c:c + M // 2 - 1], np.array([W - 1]), p[c + M // 2 - 1:]])
    t = 255 * rng.integers(0, 2, (N, 8, 16, C)); t[:, 7] = 255; w = 4095 * rng.integers(0, 2, (N, 8, 16)); w[:, 7] = 4095; w[:, 6, 0] = 4095; w[:, 3] = 0
    th = np.where(rng.random((N, 8, V)) < 0.6, 1, 15)
    return pack(x, L, k, o, t, w, th)
def setup_inputs_corners(rng):
    x, L, k, o, t, w, th = parts(rng); lane = np.arange(16)
    pal = [np.full(16, 100), np.full(16, 255), np.where(lane < 8, 200, 50), np.where((lane >= 8) & (lane < 8 + E), 10, 0), np.where((lane >= 8) & (lane < 7 + E), 10, 0),
           np.zeros(16, np.int64), np.full(16, 1), np.where(lane < 8, 101, 100), np.where(lane < 7, 101, 100), np.full(16, 200)]
    f = rng.choice(np.array([0, 5]), (N, 8, C, 16)); f[..., 0] = 0
    s = (np.arange(C) + rng.integers(0, 12, (N, 8, 1))) % 12
    f[s == 1, 15] = 2
    f[s == 2, 1] = 2
    f[s == 3, 1] = 2; f[s == 3, 15] = 3
    f[s == 4, 15] = 2; f[s == 4, 14] = 3; f[s == 4, 13] = 4
    f[s == 5, 2] = 2; f[s == 5, 1] = 3
    f[s == 6] = 3; f[s == 6, 0] = 0; f[s == 6, 1] = 2
    f[s == 7, 1] = 8; f[s == 7, 2] = 7; f[s == 7, 3] = 1
    f[s == 8, 0] = 5; f[s == 8, 1] = 1
    f[s == 9] = 1; f[s == 9, 0] = 6
    f[s == 10] = 0
    f[s == 11] = rng.integers(0, 10, (int(np.count_nonzero(s == 11)), 16))
    for g in range(8):
        if g == 3 or g == 6: continue
        q = rng.permutation(W)[:10]
        for i in range(10): x[:, g, :, int(q[i])] = pal[i]
        L[:, g] = q[f[:, g]]
    m = rng.integers(0, 3, (N, 8, C, 1)); k = np.where(m == 0, 1, np.where(m == 1, 0, k))
    th = rng.choice(np.array([1, 7, 8, 8, 9, 15]), (N, 8, V)); th[..., 0] = np.array([8, 7, 8, 1, 8, 7, 15, 8])
    k[:, 3] = 1; th[:, 3] = 1; k[:, 6] = 0; th[:, 6] = 15
    t[:, 0] = 0; t[:, 6] = 255; t[:, 2, :, ::2] = 255; w[:, 5] = 4095; w[:, 0, ::2] = 0
    deep(rng, x, L, k, o, th, 4); deep(rng, x, L, k, o, th, 7)
    return pack(x, L, k, o, t, w, th)
def setup_inputs_crowd(rng):
    x, L, k, o, t, w, th = parts(rng); lane = np.arange(16)
    pal = [np.full(16, 1), np.full(16, 255), np.where(lane == 15, 1, 255), np.where(lane < 8, 200, 120), np.where(lane < 8, 1, 0), np.full(16, 150)]
    for g in range(8):
        z = rng.permutation(W)[:6]
        for i in range(6): x[:, g, :, int(z[i])] = pal[i]
        if g % 4 == 0:
            odd = rng.integers(0, 16, (N, C, 1)) == np.arange(16); L[:, g] = np.where(odd, z[rng.integers(1, 3, (N, C, 1))], z[0])
        elif g % 4 == 1: L[:, g] = z[rng.integers(0, 6, (N, C, 16))]
        elif g % 4 == 2:
            L[:, g] = z[rng.integers(0, 6, (1, 1, 16))]; L[:, g, :, 0] = z[0]; L[:, g, :, 9] = z[2]
        else: L[:, g] = z[3]
        rest = np.setdiff1d(np.arange(W), z)
        for r in range(N): o[r, g] = rng.permutation(np.concatenate([z, rng.permutation(rest)[:M * C - 6]]))
    k = (rng.random((N, 8, C, 16)) < 0.5).astype(np.int64); th = rng.choice(np.array([1, 8, 14, 15]), (N, 8, V)); th[:, 1, 0] = 14; th[:, 5, 0] = 15; th[:, 0, 0] = 15; th[:, 2, 0] = 1
    return pack(x, L, k, o, t, w, th)
def setup_inputs_ranks(rng):
    x, L, k, o, t, w, th = parts(rng); q = rng.permutation(N)
    for i in (0, 2, 3):
        r = int(q[i]); th[r, :, 0] = 1; k[r] = 0 if i == 3 else 1
        for g in range(8):
            z = rng.permutation(W)[:2]; x[r, g, :, int(z[0])] = 1; x[r, g, :, int(z[1])] = 255
            a = L[r, g]; a[:, 0] = z[0]; a[np.arange(C), rng.integers(1, 16, C)] = z[1]
    k[int(q[2]), 7, C - 1] = 0; k[int(q[3]), 7, C - 1] = 1
    b = int(q[1]); th[b] = 15
    for g in range(8):
        e = rng.permutation(16)[:2]; y = x[b, g]; y[e] = rng.integers(1, 256, (2, 1))
        if g == 2 or g == 7:
            y[int(e[0])] = 2 * (2 * int(rng.integers(0, 64)) + 1); w[b, g] = 0; w[b, g, int(e[0])] = W // 2
    return pack(x, L, k, o, t, w, th)
def check_inputs(d):
    bad = []
    for a, lo, hi in (("dep", 0, 255), ("nam", 0, W - 1), ("mrk", 0, 1), ("own", 0, W - 1), ("pic", 0, 255), ("wt", 0, 4095), ("thr", 1, 15)):
        v = np.asarray(d[a]).astype(np.float64)
        if not (np.min(v) >= lo and np.max(v) <= hi): bad.append("range of " + a)
        elif np.any(v != np.floor(v)): bad.append("whole numbers of " + a)
    s = np.sort(np.stack([gentries(np.asarray(a)) for a in d["own"]]), axis=-1)
    if np.any(s[..., 1:] == s[..., :-1]): bad.append("distinct numbers of own")
    return bad
def reference(dep, nam, mrk, own, pic, wt, thr):
    X = dep.astype(np.float32).astype(np.int32).reshape(N, 8, 16, W)
    L = np.stack([gentries(a) for a in nam]).astype(np.int64).reshape(N, 8, C, 16); K = np.stack([gentries(a) for a in mrk]).astype(np.int64).reshape(N, 8, C, 16)
    O = np.stack([gentries(a) for a in own]).astype(np.int64).reshape(N, 8, C, M)
    T = pic.astype(np.float32).astype(np.int64).reshape(N, 8, 16, C); A = np.zeros((N, 8, C), np.int64); wv = wt.astype(np.int64).reshape(N, 8, 16, 1)
    row = np.arange(16)
    for v in range(V):
        G = np.take_along_axis(X, L.reshape(N, 8, 1, 16 * C), 3).reshape(N, 8, 16, C, 16)
        P = G[..., 0]
        cnt = np.add.reduce((P > 0)[..., None] & (G > P[..., None]), axis=2, dtype=np.int64)
        clash = cnt >= (thr[:, :, v].astype(np.int64)[..., None] + (A & 1))[..., None]
        some = np.any(clash, axis=3); k = np.argmax(clash, axis=3)
        km = np.take_along_axis(K, k[..., None], 3)[..., 0]
        none = ~some; turn = some & (km == 0); cut = some & (km == 1)
        T = np.where(none[:, :, None, :] & (P > 0), P, T)
        h = np.add.reduce(wv * T, axis=2) & (W - 1)
        xk = np.take_along_axis(G, k[:, :, None, :, None], 4)[..., 0]
        n = np.add.reduce(xk, axis=2, dtype=np.int64) & (M - 1)
        na = np.take_along_axis(O, n[..., None], 3)[..., 0]; nb = np.take_along_axis(O, (n ^ (M // 2))[..., None], 3)[..., 0]
        far = np.where(xk > P, xk, 0); near = np.where(xk <= P, xk, 0)
        enter = np.add.reduce((G > 0) & (G < near[..., None]), axis=2, dtype=np.int64) >= E
        j = np.where(np.any(enter, axis=3), np.argmax(enter, axis=3), 16)
        isk = row == k[..., None]; key = np.broadcast_to(4 * row, (N, 8, C, 16))
        key = np.where(none[..., None] & (row == 0), 999, key); key = np.where(turn[..., None] & isk, -1, key); key = np.where(cut[..., None] & isk, 999, key)
        ka = np.where(none, 100, np.where(cut, -1, 999)); kb = np.where(cut, 4 * j - 1, 999)
        order = np.argsort(np.concatenate([key, ka[..., None], kb[..., None]], axis=3), axis=3, kind="stable")[..., :16]
        L = np.take_along_axis(np.concatenate([L, np.where(none, h, na)[..., None], nb[..., None]], axis=3), order, 3)
        K = np.take_along_axis(np.concatenate([np.where(turn[..., None] & isk, 1, K), np.zeros((N, 8, C, 2), np.int64)], axis=3), order, 3)
        A = A + cut
        for r in range(N):
            for g in range(8):
                i = np.flatnonzero(cut[r, g])
                X[r, g][:, na[r, g, i]] = far[r, g][:, i]; X[r, g][:, nb[r, g, i]] = near[r, g][:, i]
        if v < V - 1: L, K, T, A = np.roll(L, 1, axis=0), np.roll(K, 1, axis=0), np.roll(T, 1, axis=0), np.roll(A, 1, axis=0)
    return {"ydep": X.reshape(N, 128, W).astype(np.float32).astype(BF), "ynam": np.stack([gtable(a.reshape(8, -1)) for a in L]).astype(np.float32), "ymrk": np.stack([gtable(a.reshape(8, -1)) for a in K]).astype(np.float32),
            "ypic": T.reshape(N, 128, C).astype(np.float32).astype(BF), "ycut": A.astype(np.float32)}

@@ -1,0 +1,788 @@
+from concourse.bass import DstId, RemoteDMATransfer
+from concourse.mybir import dt, AluOpType, AxisListType, ActivationFunctionType
+
+AL = AluOpType
+AF = ActivationFunctionType
+V = 6
+W = 4096
+NS = 128
+F32, BF, F16, I32, U16 = "float32", "bfloat16", "float16", "int32", "uint16"
+
+CFG = dict(
+    pb_bf16=True,
+    fused_le=True,
+    gp=4,
+    ns=128, tp=1, pc="s", fbi=1, he=1, late=0, dup="f", rnd="v", y="s", to="s",
+    gv=(10, 0, 0, 0),
+    nzp=4, nzs=(4, 4),
+    clash="s", cum="s", ent="s", cp="v", z="v", gate="s",
+    gam=1.56, sig=3.8, tau=0.5, tau2=1.0, pe=0.5, hop=100.0, shop=60.0, fix=30.0, rissue=900.0, rlat=2600.0,
+    slack=40.0, gt="v", xor="v", fmn="p", mk="vvv", off={},
+)
+CFG.update({'fused_le': False, 'gp': 4, 'ns': 128, 'tp': 1, 'pc': 's', 'fbi': 2, 'he': 0, 'dup': 'v', 'rnd': 's', 'y': 's', 'to': 's', 'gv': (10, 4, 1, 12), 'nzp': 8, 'nzs': (3, 8), 'clash': 's', 'cum': 's', 'ent': 's', 'cp': 'v', 'z': 'v', 'gate': 's', 'slack': 40, 'gt': 's', 'xor': 's', 'fmn': 'v', 'mk': 'ssv',
+            'off': {'a1': 4900, 's1': 22500, 'k1': 5300, 'a0': 39900, 'l0': 4400, 'g0': 3300, 'g1': -700, 'k0': -5800, 't1': -31900, 'e1': -12600, 'e0': 21400, 's0': -1400, 'm0': 1000, 'd1': 49900, 'z1': -18600, 'd0': 6600, 'l1': -21600, 'p1': -2400, 'm1': 600, 'z0': 6800, 't0': 5000, 'p0': 300}})
+
+MATS_BF = ["I", "NI", "BO", "D1", "Ub", "Lin", "M2", "R15", "Ma", "Mf", "BOd", "R150", "Cm", "Ch", "Big", "Wh", "Wl", "DIb", "IUb", "Zr", "R15n", "In"]
+MATS_H = ["U", "DI", "IU", "T0I", "T0M", "NT0", "BOh", "BOc", "BOg", "E15", "Sw", "Ih"]
+COLS = ["pm", "p", "pp", "pg", "pi", "c16", "m15", "nl15", "n0", "wk", "cm", "ch", "big", "e15", "p8", "t1", "a16", "t2",
+        "bcum", "bcp", "wa", "whs", "wls"]
+
+SCRATCH = {
+    "win": ("sbuf", [128, W + 256], BF),
+    "G0": ("sbuf", [128, 32 * NS], BF), "G1": ("sbuf", [128, 16 * NS], BF),
+    "NZ": ("sbuf", [128, 32 * NS], BF), "IND": ("sbuf", [128, 32 * NS], BF),
+    "ofs": ("sbuf", [128, V * 256], U16), "snd": ("sbuf", [128, V * 256], U16),
+    "rM": ("sbuf", [128, V * 256], BF), "sM": ("sbuf", [128, V * 256], BF),
+    "rST": ("sbuf", [128, V * 512], BF), "sST": ("sbuf", [128, V * 512], BF),
+    "hh": ("sbuf", [128, 2 * 16 * NS], F16), "bb": ("sbuf", [128, 2 * 16 * NS], BF),
+    "ii": ("sbuf", [128, 4 * NS], I32), "ff": ("sbuf", [128, 512], F32), "I32": ("sbuf", [128, 128], F32),
+    "ko": ("sbuf", [128, 16], U16), "so": ("sbuf", [128, 32], U16), "l3": ("sbuf", [128, 48], F32),
+    "inN": ("sbuf", [128, 256], I32), "inM": ("sbuf", [128, 256], I32), "inO": ("sbuf", [128, 256], I32),
+    "inW": ("sbuf", [128, 4], I32), "inT": ("sbuf", [128, 8], I32), "ic": ("sbuf", [128, 8], I32),
+    "ownN": ("sbuf", [128, 256], F16), "ownP": ("sbuf", [128, 256], F16),
+    "X": ("sbuf", [128, 144], F32), "QB": ("sbuf", [128, 128], F32), "col": ("sbuf", [128, 32], F32),
+    "Zo": ("sbuf", [128, 144], BF), "Zk": ("sbuf", [128, 144], BF), "Zh": ("sbuf", [128, 144], F16),
+    "mb": ("sbuf", [128, 128 * len(MATS_BF)], BF), "mh": ("sbuf", [128, 128 * len(MATS_H)], F16),
+    "ones": ("sbuf", [128, 256], BF), "sm": ("sbuf", [128, 80], BF), "k1": ("sbuf", [128, 32], F32),
+    "thb": ("sbuf", [128, 8], BF), "Gm": ("sbuf", [128, 128], BF), "thc": ("sbuf", [128, 16], F32),
+    "oN": ("sbuf", [128, 256], F32), "oM": ("sbuf", [128, 256], F32), "oA": ("sbuf", [128, 256], F32),
+    "K0": ("psum", [128, 1024], BF) if CFG["pb_bf16"] else ("psum", [128, 512], F32),
+}
+for _k in range(1, 8):
+    SCRATCH["K%d" % _k] = ("psum", [128, 512], F32)
+
+DMAS = ["dN", "dD", "dM", "dO", "dP0", "dP1", "dW", "dT", "oD", "oN0", "oN1", "oM0", "oM1", "oP0", "oP1", "oA0", "oA1"]
+SEMAPHORES = ["sv", "ss", "st", "sg", "ls"] + DMAS + ["r%s%d%d" % (k, v, c) for k in "NMS" for v in range(1, V) for c in range(2)]
+DRAM = ("dep", "nam", "mrk", "own", "pic", "wt", "thr", "ydep", "ynam", "ymrk", "ypic", "ycut")
+
+
+def R(buf, c0, c1, st=1, p0=0, p1=128):
+    return (buf, p0, p1, c0, c1, st)
+
+
+def width(r):
+    return (r[4] - r[3] + r[5] - 1) // r[5]
+
+
+def dtype_of(r):
+    return SCRATCH[r[0]][2]
+
+
+def is_ps(r):
+    return r[0][0] == "K" and len(r[0]) == 2
+
+
+def build(cfg):
+    ops = []
+    n = cfg["ns"]
+    nc, nb = 256 // n, n // 16
+    lab = ["0"]
+
+    def add(eng, cost, ins, outs, call, **kw):
+        o = dict(eng=eng, cost=cost, ins=[r for r in ins if isinstance(r, tuple)], outs=outs, call=call, k=len(ops), lat=0.0, kind="c", lab=lab[0])
+        o.update(kw)
+        ops.append(o)
+        return o
+
+    def two(*rs):
+        return all(dtype_of(r) in (BF, F16, U16) for r in rs)
+
+    def ts(out, a, s1, s2, o0, o1=None, ind=None):
+        c = max(64.0, width(out) * (0.5 if two(out, a) else 1.0)) + cfg["fix"]
+        if ind is not None:
+            c = 50 + width(out) * cfg["gam"]
+        add("v", c, [a, s1, s2, ind], [out], ("ts", out, a, s1, s2, o0, o1, ind))
+
+    def tt(out, a, b, op, ind=None, sct=None):
+        if ind is not None:
+            c = 50 + width(out) * cfg["gam"]
+        elif sct is not None:
+            c = 50 + width(a) * cfg["sig"]
+        else:
+            ps = is_ps(a) or is_ps(b)
+            f = (cfg["tau"] if ps else cfg["tau2"]) if two(out, a, b) else (1.0 if ps else 2.0)
+            c = max(64.0, width(out) * f) + cfg["fix"]
+        add("v", c, [a, b, ind, sct], [out], ("tt", out, a, b, op, ind, sct))
+
+    def cp(out, a, ind=None):
+        c = max(64.0, width(out) * (0.5 if two(out, a) else 1.0)) + cfg["fix"]
+        if ind is not None:
+            c = 50 + width(out) * cfg["gam"]
+        add("v", c, [a, ind], [out], ("cp", out, a, ind))
+
+    def act(out, a, f, bias=0.0, scale=1.0, ind=None):
+        c = max(64.0, width(out)) + cfg["fix"]
+        if ind is not None:
+            c = 65 + width(out) * cfg["gam"]
+        add("s", c, [a, bias, scale, ind], [out], ("act", out, a, f, bias, scale, ind))
+
+    def mm(out, l, r, start, stop):
+        add("t", max(64.0, width(r)) * cfg["pe"] * (4 if dtype_of(r) == F32 else 1) + 5, [l, r], [out], ("mm", out, l, r, start, stop), start=start)
+
+    def grp(out, terms, first=True, end=True):
+        for i, (l, r) in enumerate(terms):
+            mm(out, l, r, first and i == 0, end and i == len(terms) - 1)
+
+    def dma(q, sem, out, a, nbytes):
+        add(q, 60.0, [a], [out], ("dma", out, a), kind="d", sem=sem, lat=2000.0 + nbytes / 180.0)
+
+    def send(sem, dst, src):
+        s = add("g", cfg["rissue"], [src], [], ("send", dst, src, sem), kind="r")
+        add("x", 0.0, [], [dst], None, kind="a", sem=sem, src=s["k"], lat=cfg["rlat"] + width(src) * 2)
+
+    def mb(name):
+        i = MATS_BF.index(name)
+        return R("mb", 128 * i, 128 * i + 128)
+
+    def mh(name):
+        i = MATS_H.index(name)
+        return R("mh", 128 * i, 128 * i + 128)
+
+    def col(name, p1=128):
+        i = COLS.index(name)
+        return R("col", i, i + 1, 1, 0, p1)
+
+    def zs(buf, a):
+        return R(buf, 16 - a, 144 - a)
+
+    dma("y", "dN", R("inN", 0, 256), R("nam", 0, 256), 131072)
+    dma("y", "dD", R("win", 0, W), R("dep", 0, W), 1 << 20)
+    dma("s", "dT", R("inT", 0, 6, 1, 0, 8), R("thr", 0, 6, 1, 0, 8), 200)
+    dma("s", "dW", R("inW", 0, 1), ("wt",), 500)
+    dma("y", "dM", R("inM", 0, 256), R("mrk", 0, 256), 1200000)
+    dma("y", "dO", R("inO", 0, 256), R("own", 0, 256), 1300000)
+    for c in range(nc):
+        dma("y", "dP%d" % c, R("rST", 2 * n * c + n, 2 * n * c + 2 * n), R("pic", n * c, n * c + n), 1300000)
+        add("v", 94.0, [], [R("rST", 2 * n * c, 2 * n * c + n)], ("ms", R("rST", 2 * n * c, 2 * n * c + n), 0.0))
+    add("g", 130 + 2 * 144, [], [R("X", 0, 144)], ("iota", R("X", 0, 144), [[1, 144]], 0, 0))
+    add("g", 140, [], [R("ic", 0, 1)], ("iota", R("ic", 0, 1), [[1, 1]], 0, 1))
+    add("g", 140, [], [R("col", 0, 3)], ("iota", R("col", 0, 3), [[1, 3]], -1, 1))
+    add("g", 130 + 256, [], [R("QB", 0, 128)], ("iota", R("QB", 0, 128), [[1, 8], [0, 16]], 0, 0))
+    for r, val in ((R("ones", 0, n), 1.0), (R("win", W, W + n), 0.0), (R("sm", 16 + 2 * nb, 16 + 3 * nb), 0.0)):
+        add("v", 94.0, [], [r], ("ms", r, val))
+    cp(R("ofs", 0, 128), R("inN", 0, 128))
+    cp(R("ofs", 128, 256), R("inN", 128, 256))
+    X = R("X", 0, 128)
+    ts(R("ic", 1, 2), R("ic", 0, 1), 4, None, AL.arith_shift_right)
+    ts(R("ic", 2, 3), R("ic", 0, 1), 15, None, AL.bitwise_and)
+    cp(R("col", 3, 5), R("ic", 1, 3))
+    ts(col("c16"), col("pg"), 16.0, 16.0, AL.mult, AL.add)
+    ts(col("m15"), col("pi"), 15.0, None, AL.is_equal)
+    ts(col("nl15"), col("pi"), 15.0, None, AL.is_lt)
+    ts(col("n0"), col("pi"), 0.0, None, AL.is_gt)
+    act(col("wk"), col("m15"), AF.Identity, -1.0, 16.0)
+    act(col("cm"), col("pi"), AF.Identity, 1.0 / 32, -1.0 / 16)
+    act(col("ch"), col("m15"), AF.Copy, 0.0, -0.5)
+    act(col("big"), col("m15"), AF.Copy, 0.0, 3.0 * 2 ** 22)
+    act(col("e15"), col("m15"), AF.Copy, 0.0, 4096.0)
+    ts(col("t1"), col("pi"), 8.0, -16.0, AL.is_ge, AL.mult)
+    ts(col("p8"), col("p"), col("t1"), 8.0, AL.add, AL.add)
+    ts(col("t2"), col("pi"), 6.0, None, AL.is_le)
+    tt(col("a16"), col("t2"), col("n0"), AL.mult)
+    k1 = 1.0 if cfg["clash"] == "s" else 0.0
+    if cfg["cum"] == "s":
+        act(col("bcum"), col("pi"), AF.Identity, k1, k1)
+    else:
+        act(col("bcum"), col("pi"), AF.Identity, 1.0 - k1, -k1)
+    k2 = 1.0 if cfg["ent"] == "s" else 0.0
+    if cfg["cp"] == "s":
+        act(col("bcp"), col("pi"), AF.Identity, 0.5 * k2 - 1.0, k2)
+    else:
+        act(col("bcp"), col("pi"), AF.Identity, 2.0 - 0.5 * k2, -k2)
+    ts(R("Zo", 0, 144), R("X", 0, 144), col("c16"), None, AL.is_equal)
+    ts(mb("I"), X, col("p"), None, AL.is_equal)
+    ts(mb("BO"), R("QB", 0, 128), col("pg"), None, AL.is_equal)
+    ts(mb("D1"), X, col("pp"), col("nl15"), AL.is_equal, AL.mult)
+    ts(mb("Ub"), X, col("pm"), col("n0"), AL.is_equal, AL.mult)
+    act(R("Zk", 0, 144), R("Zo", 0, 144), AF.Copy, 0.0, col("wk"))
+    cp(R("Zh", 0, 144), R("Zo", 0, 144))
+    ts(mb("M2"), X, col("p"), None, AL.is_ge)
+    tt(mb("Lin"), mb("M2"), mb("BO"), AL.mult)
+    ts(mb("M2"), mb("Lin"), 2.0, None, AL.mult)
+    tt(mb("M2"), mb("M2"), mb("I"), AL.subtract)
+    if k2:
+        act(mb("M2"), mb("M2"), AF.Copy, 0.0, 0.5)
+    act(mb("NI"), mb("I"), AF.Copy, 0.0, -1.0)
+    if cfg["dup"] == "f":
+        act(R("I32", 0, 128), mb("I"), AF.Copy)
+    if cfg["dup"] == "v":
+        cp(mh("Ih"), mb("I"))
+    act(mb("R15"), mb("BO"), AF.Copy, 0.0, col("m15"))
+    act(mb("R15n"), mb("R15"), AF.Copy, 0.0, -256.0)
+    act(mb("In"), mb("I"), AF.Copy, 0.0, -256.0)
+    tt(mb("Ma"), mb("R15"), mb("I"), AL.subtract)
+    tt(mb("Mf"), mb("I"), mb("D1"), AL.subtract)
+    act(mb("BOd"), mb("BO"), AF.Copy, 0.0, 1.0 / 16)
+    act(mb("R150"), zs("Zo", 0), AF.Copy, 0.0, col("m15"))
+    act(mb("Cm"), mb("I"), AF.Copy, 0.0, col("cm"))
+    act(mb("Ch"), mb("I"), AF.Copy, 0.0, col("ch"))
+    act(mb("Big"), mb("I"), AF.Copy, 0.0, col("big"))
+    ts(R("ic", 4, 5), R("inW", 0, 1), 6, None, AL.arith_shift_right)
+    ts(R("ic", 5, 6), R("inW", 0, 1), 63, None, AL.bitwise_and)
+    ts(col("wa"), R("ic", 4, 5), 32.0, -64.0, AL.is_ge, AL.mult)
+    ts(col("whs"), R("ic", 4, 5), col("wa"), 1.0 / 64, AL.add, AL.mult)
+    ts(col("wls"), R("ic", 5, 6), 1.0 / 4096, None, AL.mult)
+    act(mb("Wh"), zs("Zo", 15), AF.Copy, 0.0, col("whs"))
+    act(mb("Wl"), zs("Zo", 15), AF.Copy, 0.0, col("wls"))
+    cp(mh("U"), mb("Ub"))
+    ts(mh("DI"), mb("Mf"), -1.0, None, AL.mult)
+    act(mb("DIb"), mb("Mf"), AF.Copy, 0.0, -1.0)
+    tt(mb("IUb"), mb("I"), mb("Ub"), AL.subtract)
+    cp(mh("IU"), mb("IUb"))
+    tt(mh("T0I"), zs("Zo", 0), mb("I"), AL.subtract)
+    ts(mh("NT0"), zs("Zo", 0), -1.0, None, AL.mult)
+    tt(mh("T0M"), mh("NT0"), mb("I"), AL.subtract)
+    cp(mh("BOh"), mb("BO"))
+    ts(mh("BOc"), mb("BO"), -1.0 / 32, None, AL.mult)
+    ts(mh("BOg"), mb("BO"), -100.0, None, AL.mult)
+    ts(mh("E15"), mb("I"), col("e15"), None, AL.mult)
+    ts(mh("Sw"), X, col("p8"), None, AL.is_equal)
+    jj = R("k1", 16, 16 + nb)
+    ts(jj, R("X", 0, nb), 16.0, col("pi"), AL.mult, AL.add)
+    act(R("sm", 0, nb), jj, AF.Copy, 0.0, 16.0)
+    act(R("sm", 16, 16 + nb), jj, AF.Copy, 0.0, -1.0)
+    act(R("sm", 16 + nb, 16 + 2 * nb), jj, AF.Copy, 0.0, -1.0)
+    act(R("k1", 0, nb), jj, AF.Identity, -2048.0, -1.0)
+    ts(R("sm", 64, 72), R("X", 0, 8), col("pg"), col("a16"), AL.is_equal, AL.mult)
+    Mpar = R("Gm", 0, 128)
+    cp(R("thb", 0, 6, 1, 0, 8), R("inT", 0, 6, 1, 0, 8))
+    ts(R("IND", 0, 128, 1, 0, 8), R("QB", 0, 128, 1, 0, 8), col("p", 8), None, AL.is_equal)
+    mm(R("K7", 0, 6), R("IND", 0, 128, 1, 0, 8), R("thb", 0, 6, 1, 0, 8), True, True)
+    if cfg["clash"] == "s":
+        act(R("thc", 0, 6), R("K7", 0, 6), AF.Identity, 0.5, -1.0)
+    else:
+        act(R("thc", 0, 6), R("K7", 0, 6), AF.Copy)
+    ts(col("t1"), col("n0"), -1.0, None, AL.add)
+    act(Mpar, mb("BO"), AF.Copy, 0.0, col("t1"))
+    ts(R("ownN", 0, 256), R("inO", 0, 256), -1.0, 2048.0, AL.mult, AL.add)
+    mm(R("K7", 256, 512), mh("Sw"), R("ownN", 0, 256), True, True)
+    cp(R("ownP", 0, 256), R("K7", 256, 512))
+    act_or = cp
+    act_or(R("rM", 0, 256), R("inM", 0, 256))
+    ones = R("ones", 0, n)
+
+    for v in range(V):
+        last = v == V - 1
+        gp = cfg["gp"]
+        for c in range(nc):
+            gv = cfg["gv"][c if v == 0 else 2 + c]
+            s = n // gp
+            lab[0] = "g%d" % c
+            for i in range(gp):
+                o = v * 256 + c * n + i * s
+                out = R("G%d" % c, 16 * i * s, 16 * (i + 1) * s)
+                if gv >> i & 1:
+                    cp(out, R("win", 0, W), ind=R("ofs", o, o + s))
+                else:
+                    act(out, R("win", 0, W), AF.Copy, ind=R("ofs", o, o + s))
+        for c in range(nc):
+            G = "G%d" % c
+            Gw = R(G, 0, 16 * n)
+            K1, K2, K3 = "K%d" % (1 + 3 * c), "K%d" % (2 + 3 * c), "K%d" % (3 + 3 * c)
+
+            def ps(ka, kb, i):
+                return R(ka, i * n, (i + 1) * n) if (i + 1) * n <= 512 else R(kb, i * n - 512, (i + 1) * n - 512)
+
+            def cut(r, i, s):
+                return R(r[0], r[3] + i * s * r[5], r[3] - r[3] % r[5] + (i + 1) * s * r[5], r[5])
+
+            def h(i, k=1):
+                return R("hh", (16 * c + i) * n, (16 * c + i + k) * n)
+
+            def b(i):
+                return R("bb", (16 * c + i) * n, (16 * c + i + 1) * n)
+
+            def row(r, buf=G, o=0):
+                return R(buf, o + r, o + 16 * n, 16)
+
+            Nh, aN, sN, FN, FMN, Qn, Qp, FM, hd, cN, cP = [h(i) for i in range(11)]
+            aM, sM, cM = b(13), b(14), b(15)
+            clash, cum, ent, cpm, z, le, gt, xk, xk1, gate, y, cpr = [b(i) for i in range(12)]
+            PB, BB = R("K0", 2 * c * n, (2 * c + 1) * n), R("K0", (2 * c + 1) * n, (2 * c + 2) * n)
+            cnt1, cnt2 = R(K1, 0, n), R(K1, n, 2 * n)
+            pre1, koff, l3p, um, pre2 = R(K2, 0, n), R(K2, n, n + nb), R(K2, n + 16, n + 16 + 3 * nb), ps(K2, "K4", 2), ps(K2, "K4", 3)
+            oh = pre1
+            ma, mf, ms, mx = [ps(K3, "K5", i) for i in range(4)]
+            midN, midM, npr = ma, mf, ms
+            pd, pg_, pt, uh = [ps("K7", "K6", i) for i in range(4)]
+            o = v * 256 + c * n
+            Min = R("rM", o, o + n)
+            Sin, Tin = R("rST", 2 * o, 2 * o + n), R("rST", 2 * o + n, 2 * o + 2 * n)
+            Sout, Tout = R("sST", 2 * o, 2 * o + n), R("sST", 2 * o + n, 2 * o + 2 * n)
+            P = row(0)
+            nzo = 16 * n * c
+            lab[0] = "a%d" % c
+            Pc = b(12)
+            s = n // cfg["tp"]
+            for i in range(cfg["tp"]):
+                if cfg["pc"] == "s":
+                    act(cut(Pc, i, s), cut(P, i, s), AF.Copy)
+                else:
+                    cp(cut(Pc, i, s), cut(P, i, s))
+                if cfg["z"] == "s":
+                    act(cut(z, i, s), cut(P, i, s), AF.Relu, 256.0, -256.0)
+                else:
+                    ts(cut(z, i, s), cut(P, i, s), 0.0, 256.0, AL.is_equal, AL.mult)
+                tt(cut(PB, i, s), cut(Pc, i, s), cut(z, i, s), AL.add)
+                for r in range(1, 16):
+                    ind = cut(R("IND", nzo + r * n, nzo + (r + 1) * n), i, s)
+                    tt(ind, cut(row(r), i, s), cut(PB, i, s), AL.is_gt)
+                    mm(cut(cnt1, i, s), zs("Zo", r), ind, r == 1, v == 0 and r == 15)
+                if v > 0:
+                    mm(cut(cnt1, i, s), Mpar, cut(Sin, i, s), False, True)
+            s = 16 * n // cfg["nzp"]
+            lab[0] = "z%d" % c
+            for i in range(cfg["nzp"]):
+                if i < cfg["nzs"][c]:
+                    act(R("NZ", nzo + i * s, nzo + (i + 1) * s), R(G, i * s, (i + 1) * s), AF.Sign, 0.0, -1.0)
+                else:
+                    ts(R("NZ", nzo + i * s, nzo + (i + 1) * s), R(G, i * s, (i + 1) * s), 1.0, -1.0, AL.min, AL.mult)
+            lab[0] = "l%d" % c
+            ts(Nh, R("ofs", o, o + n), -2048.0, None, AL.add)
+            lab[0] = "d%d" % c
+            th = R("thc", v, v + 1)
+            if cfg["clash"] == "s":
+                act(clash, cnt1, AF.Sign, th)
+            else:
+                ts(clash, cnt1, th, None, AL.is_ge)
+            grp(pre1, [(mb("Lin"), clash)])
+            if cfg["cum"] == "s":
+                act(cum, pre1, AF.Sign, col("bcum"))
+            else:
+                ts(cum, pre1, col("bcum"), None, AL.is_ge)
+            grp(koff, [(mb("I"), R("sm", 0, nb))] + [(zs("Zk", a), R("bb", cum[3] + a, cum[4], 16)) for a in range(16)])
+            grp(mf, [(mb("Mf"), cum)])
+            grp(ma, [(mb("Ma"), cum)])
+            grp(ms, [(mb("R15"), cum)])
+            ko = R("ko", nb * c, nb * c + nb)
+            cp(ko, koff)
+            act(xk1, Gw, AF.Relu, -1.0, ind=ko)
+            act(xk, Gw, AF.Copy, ind=ko)
+            if cfg["fused_le"]:
+                tt(le, Gw, Pc, AL.is_le, ind=ko)
+            else:
+                tt(le, xk, Pc, AL.is_le)
+            tt(BB, xk1, le, AL.mult)
+            tt(FM, mf, Min, AL.mult)
+            lab[0] = "t%d" % c
+            for r in range(1, 16):
+                mm(cnt2, zs("Zo", r), row(r, "NZ", nzo), r == 1, False)
+            mm(cnt2, mh("BOg"), FM, False, False)
+            for r in range(1, 16):
+                ind = R("IND", nzo + r * n, nzo + (r + 1) * n)
+                tt(ind, row(r), BB, AL.is_gt)
+                mm(cnt2, zs("Zo", r), ind, False, r == 15)
+            lab[0] = "m%d" % c
+            grp(um, [(mb("Cm"), ones), (mh("BOc"), FM), (mb("BOd"), xk)])
+            rm, rh = R("ii", 2 * c * n, (2 * c + 1) * n), R("ii", (2 * c + 1) * n, (2 * c + 2) * n)
+            if cfg["rnd"] == "s":
+                rm = R("ff", c * n, c * n + n)
+                act(rm, um, AF.Identity, 3.0 * 2 ** 22)
+                act(rm, rm, AF.Identity, -3.0 * 2 ** 22)
+            else:
+                cp(rm, um)
+            tt(oh, um, rm, AL.is_equal)
+            tt(Qn, oh, R("ownN", c * n, c * n + n), AL.mult)
+            tt(Qp, oh, R("ownP", c * n, c * n + n), AL.mult)
+            mark = len(ops)
+            grp(l3p, [(mb("I"), R("sm", 16, 16 + 3 * nb))] + [(zs("Zh", a), R("hh", Qn[3] + a, FM[4], 16)) for a in range(16)])
+            t3, o3 = R("l3", 24 * c, 24 * c + nb), 24 * c + nb
+            tt(t3, cut(l3p, 2, nb), R("k1", 0, nb), AL.mult)
+            tt(R("l3", o3, o3 + nb), t3, cut(l3p, 0, nb), AL.subtract)
+            tt(R("l3", o3 + nb, o3 + 2 * nb), t3, cut(l3p, 1, nb), AL.subtract)
+            so = R("so", 16 * c, 16 * c + 2 * nb)
+            ts(so, R("l3", o3, o3 + 2 * nb), 4096.0, None, AL.add)
+            lab[0] = "s%d" % c
+            if cfg["gt"] == "s":
+                act(gt, le, AF.Identity, 1.0, -1.0)
+            else:
+                ts(gt, le, -1.0, 1.0, AL.mult, AL.add)
+            tt(R("win", 0, W + n), xk, gt, AL.mult, sct=cut(so, 0, nb))
+            tt(R("win", 0, W + n), xk, le, AL.mult, sct=cut(so, 1, nb))
+            held = []
+            if cfg["late"] >> c & 1:
+                held = ops[mark:]
+                del ops[mark:]
+            lab[0] = "l%d" % c
+            tt(FN, mf, Nh, AL.mult)
+            tt(aN, ma, Nh, AL.mult)
+            tt(sN, ms, Nh, AL.mult)
+            for i, (dst, msk) in enumerate(((aM, ma), (sM, ms))):
+                if cfg["mk"][i] == "s":
+                    grp(mx, [(mb("I"), Min), (mb(("Ma", "R15")[i]), cum)])
+                    act(dst, mx, AF.Relu, -1.0)
+                else:
+                    tt(dst, msk, Min, AL.mult)
+            if cfg["fmn"] == "p":
+                grp(mf, [(mh("BOh"), FM)])
+                tt(FMN, mf, FN, AL.mult)
+            else:
+                tt(FMN, FM, Nh, AL.mult)
+            lab[0] = "p%d" % c
+            if cfg["xor"] == "s":
+                grp(mx, [(mb("NI"), Sin), (zs("Zh", 0), FM), (zs("Zh", v + 1), FM)])
+                act(Sout, mx, AF.Abs)
+            else:
+                grp(mx, [(zs("Zh", 0), FM), (zs("Zh", v + 1), FM)])
+                tt(Sout, mx, Sin, AL.not_equal)
+            if cfg["he"]:
+                lab[0] = "h%d" % c
+                grp(pt, [(mb("I"), Tin), (mb("In"), Pc)])
+                act(cpr, pt, AF.Relu)
+                grp(uh, [(mb("Ch"), ones), (mb("Wh"), Pc), (mb("Wl"), Pc), (mb("Wh"), cpr), (mb("Wl"), cpr), (mb("Big"), cum)])
+                ts(rh, uh, 2.0 ** -13, None, AL.add)
+                tt(hd, uh, rh, AL.subtract)
+                lab[0] = "p%d" % c
+            grp(pd, [(mb("I"), Pc), (mb("R15n"), cum)])
+            if cfg["gate"] == "s":
+                act(gate, pd, AF.Relu)
+            else:
+                ts(gate, pd, 0.0, None, AL.max)
+            grp(pg_, [(mb("I"), Tin), (mb("In"), gate)])
+            if cfg["y"] == "s":
+                act(y, pg_, AF.Relu)
+            else:
+                ts(y, pg_, 0.0, None, AL.max)
+            if cfg["to"] == "s":
+                grp(pt, [(mb("I"), gate), (mb("I"), y)])
+                act(Tout, pt, AF.Copy)
+            else:
+                tt(Tout, gate, y, AL.add)
+            if not last:
+                send("rS%d%d" % (v + 1, c), R("rST", 2 * (o + 256), 2 * (o + 256) + 2 * n), R("sST", 2 * o, 2 * o + 2 * n))
+            else:
+                dma("y", "oP%d" % c, R("ypic", c * n, c * n + n), Tout, 32768)
+            if not cfg["he"]:
+                grp(uh, [(mb("Ch"), ones), (mb("Wh"), Tout), (mb("Wl"), Tout), (mb("Big"), cum)])
+                ts(rh, uh, 2.0 ** -13, None, AL.add)
+                tt(hd, uh, rh, AL.subtract)
+            if last:
+                grp(R("K7", 0, n, 1, 0, 8), [(R("sm", 64, 72), Sout)])
+                act(R("oA", c * n, c * n + n, 1, 0, 8), R("K7", 0, n, 1, 0, 8), AF.Copy)
+                dma("y", "oA%d" % c, R("ycut", c * n, c * n + n, 1, 0, 8), R("oA", c * n, c * n + n, 1, 0, 8), 4096)
+            lab[0] = "l%d" % c
+            grp(npr, [(mh("BOh"), Qp)])
+            grp(midM, [(mb("Ub"), Min), (mb("R150"), cum), (mh("T0M"), FM), (mb("DIb"), aM), (mb("IUb"), sM)])
+            terms = [(mh("U"), Nh), (mh("T0I"), FN), (mh("DI"), aN), (mh("IU"), sN), (mh("NT0"), FMN), (mh("NT0"), Qn), (mh("E15"), hd)]
+            grp(midN, terms)
+            act(aM, midM, AF.Copy)
+            if cfg["dup"] == "f":
+                act(R("ff", 256 + c * n, 256 + c * n + n), midN, AF.Copy)
+                terms = [(R("I32", 0, 128), R("ff", 256 + c * n, 256 + c * n + n))]
+            elif cfg["dup"] == "v":
+                cp(Nh, midN)
+                terms = [(mh("Ih"), Nh)]
+            grp(mx, terms, True, False)
+            lab[0] = "e%d" % c
+            if cfg["ent"] == "s":
+                act(ent, cnt2, AF.Sign, -102.5, -1.0)
+            else:
+                ts(ent, cnt2, -103.0, None, AL.is_le)
+            grp(pre2, [(mb("D1"), cum), (mb("M2"), ent)])
+            if cfg["cp"] == "s":
+                act(cpr, pre2, AF.Relu, col("bcp"))
+                act(cpm, cpr, AF.Sign)
+            else:
+                ts(cpm, pre2, col("bcp"), None, AL.is_ge)
+            tt(cN, midN, cpm, AL.mult)
+            tt(cP, npr, cpm, AL.mult)
+            grp(mx, [(mh("DI"), cN), (mh("DI"), cP)], False)
+            midN = mx
+            if not last:
+                ts(R("snd", o, o + n), midN, 2048.0, None, AL.add)
+                send("rN%d%d" % (v + 1, c), R("ofs", o + 256, o + 256 + n), R("snd", o, o + n))
+            else:
+                ts(R("oN", c * n, c * n + n), midN, 2048.0, None, AL.add)
+                dma("y", "oN%d" % c, R("ynam", c * n, c * n + n), R("oN", c * n, c * n + n), 65536)
+            ops.extend(held)
+            lab[0] = "k%d" % c
+            if cfg["mk"][2] == "s":
+                grp(midM, [(mb("I"), aM), (mb("I"), cpm)])
+                act(cM, midM, AF.Relu, -1.0)
+            else:
+                tt(cM, midM, cpm, AL.mult)
+            grp(midM, [(mb("I"), aM), (mb("DIb"), cM)])
+            if not last:
+                act(R("sM", o, o + n), midM, AF.Copy)
+                send("rM%d%d" % (v + 1, c), R("rM", o + 256, o + 256 + n), R("sM", o, o + n))
+            else:
+                act(R("oM", c * n, c * n + n), midM, AF.Copy)
+                dma("s", "oM%d" % c, R("ymrk", c * n, c * n + n), R("oM", c * n, c * n + n), 65536)
+        if last:
+            dma("y", "oD", R("ydep", 0, W), R("win", 0, W), 1 << 20)
+    for k, o in enumerate(ops):
+        o["k"] = k
+        if o["kind"] == "a":
+            o["src"] = k - 1
+    return ops
+
+
+def overlap(a, b):
+    if a[0] != b[0] or len(a) == 1:
+        return False
+    if a[2] <= b[1] or b[2] <= a[1] or a[4] <= b[3] or b[4] <= a[3]:
+        return False
+    return True
+
+
+def place(ops, seq, pre, gap):
+    t0 = [0.0] * len(ops)
+    lines = {}
+
+    def clear(key, eng, t, c, m):
+        a = lines.get(key)
+        if not a:
+            return t
+        lo, hi = 0, len(a)
+        while lo < hi:
+            mid = (lo + hi) // 2
+            if a[mid][1] + m <= t:
+                lo = mid + 1
+            else:
+                hi = mid
+        while lo < len(a) and a[lo][0] < t + c + m:
+            if a[lo][2] != eng and a[lo][1] + m > t:
+                t = a[lo][1] + m
+            lo += 1
+        return t
+
+    for k in seq:
+        o = ops[k]
+        t = max([t0[d] + w for d, w in pre[k] if d >= 0] + [w for d, w in pre[k] if d < 0] + [0.0])
+        c = o["cost"]
+        if o["kind"] != "a":
+            while True:
+                t1 = clear(o["eng"], None, t, c, 0.0)
+                for bk in o["banks"]:
+                    t1 = clear(bk, o["eng"], t1, c, gap)
+                if t1 == t:
+                    break
+                t = t1
+            for key in [o["eng"]] + list(o["banks"]):
+                a = lines.setdefault(key, [])
+                i = len(a)
+                while i and a[i - 1][0] > t:
+                    i -= 1
+                a.insert(i, (t, t + c, o["eng"]))
+        t0[k] = t
+    return t0
+
+
+def tighten(ops, base, hop, cfg):
+    fw = [[(d, ops[d]["cost"] + ops[d]["lat"] + hop(ops[d], o)) for d in base[o["k"]]] for o in ops]
+    bw = [[(-1, o["lat"])] for o in ops]
+    for o in ops:
+        for d in base[o["k"]]:
+            bw[d].append((o["k"], o["cost"] + ops[d]["lat"] + hop(ops[d], o)))
+    t0 = [o["t0"] for o in ops]
+    best = (max(o["fin"] for o in ops), t0)
+    for _ in range(cfg["fbi"]):
+        u = place(ops, sorted(range(len(ops)), key=lambda k: (-(t0[k] + ops[k]["cost"]), -k)), bw, cfg["hop"])
+        t0 = place(ops, sorted(range(len(ops)), key=lambda k: (-(u[k] + ops[k]["cost"]), k)), fw, cfg["hop"])
+        end = max(t0[o["k"]] + o["cost"] + o["lat"] for o in ops)
+        if end < best[0]:
+            best = (end, t0)
+    order = sorted(ops, key=lambda o: (best[1][o["k"]], o["k"]))
+    bank = {}
+    for o in order:
+        o["t0"] = best[1][o["k"]]
+        o["fin"] = o["t0"] + o["cost"] + o["lat"]
+        o["deps"] = set(base[o["k"]])
+        for k in o["banks"]:
+            for e, q in bank.get(k, {}).items():
+                if e != o["eng"]:
+                    o["deps"].add(q["k"])
+            bank.setdefault(k, {})[o["eng"]] = o
+    return order
+
+
+def schedule(cfg):
+    ops = build(cfg)
+    touch = {}
+    lastmm = {}
+    for o in ops:
+        deps = set()
+        for r in o["ins"]:
+            for (k, w, q) in touch.get(r[0], ()):
+                if w and overlap(r, q):
+                    deps.add(k)
+        for r in o["outs"]:
+            lst = touch.setdefault(r[0], [])
+            for (k, w, q) in lst:
+                if overlap(r, q):
+                    deps.add(k)
+            if r[5] == 1:
+                lst[:] = [e for e in lst if not (r[1] <= e[2][1] and e[2][2] <= r[2] and r[3] <= e[2][3] and e[2][4] <= r[4])]
+        for r in o["ins"]:
+            if len(r) > 1:
+                touch.setdefault(r[0], []).append((o["k"], False, r))
+        for r in o["outs"]:
+            touch[r[0]].append((o["k"], True, r))
+        if o["eng"] == "t":
+            bank = o["outs"][0][0]
+            if bank in lastmm:
+                deps.add(lastmm[bank])
+            lastmm[bank] = o["k"]
+        if o["kind"] == "a":
+            deps = {o["src"]}
+        deps.discard(o["k"])
+        o["deps"] = deps
+        o["banks"] = {r[0] for r in o["ins"] + o["outs"] if is_ps(r)}
+    succ = [[] for _ in ops]
+    for o in ops:
+        for d in o["deps"]:
+            succ[d].append(o["k"])
+    base = [set(o["deps"]) for o in ops]
+
+    def hop(a, b):
+        if a["eng"] == b["eng"] and a["kind"] == "c":
+            return 0.0 if a["eng"] == "t" else cfg["shop"]
+        return 0.0 if b["kind"] == "a" else cfg["hop"]
+
+    for o in reversed(ops):
+        o["pri"] = o["cost"] + o["lat"] + max([hop(o, ops[s]) + ops[s]["pri"] for s in succ[o["k"]]] + [0.0])
+    for o in ops:
+        o["pri"] += cfg["off"].get(o["lab"], 0.0)
+    free = {e: 0.0 for e in "vstgyx"}
+    left = [len(o["deps"]) for o in ops]
+    ready = [o for o in ops if not o["deps"]]
+    for o in ready:
+        o["rt"] = 0.0
+    bank = {}
+    order = []
+    while ready:
+        best = None
+        for o in ready:
+            t = max(o["rt"], free[o["eng"]]) if o["kind"] != "a" else o["rt"]
+            for k in o["banks"]:
+                for e, q in bank.get(k, {}).items():
+                    if e != o["eng"]:
+                        t = max(t, q["fin"] + cfg["hop"])
+            o["est"] = t
+            if best is None or t < best["est"]:
+                best = o
+        t0, e0 = best["est"], best["eng"]
+        for o in ready:
+            if o["eng"] == e0 and o["est"] <= t0 + cfg["slack"] and o["pri"] > best["pri"]:
+                best = o
+        o = best
+        ready.remove(o)
+        for k in o["banks"]:
+            for e, q in bank.get(k, {}).items():
+                if e != o["eng"]:
+                    o["deps"].add(q["k"])
+            bank.setdefault(k, {})[o["eng"]] = o
+        o["t0"] = o["est"]
+        if o["kind"] != "a":
+            free[o["eng"]] = o["t0"] + o["cost"]
+        o["fin"] = o["t0"] + o["cost"] + o["lat"]
+        order.append(o)
+        for s in succ[o["k"]]:
+            left[s] -= 1
+            if left[s] == 0:
+                q = ops[s]
+                q["rt"] = max(ops[d]["fin"] + hop(ops[d], q) for d in q["deps"])
+                ready.append(q)
+    if cfg["fbi"]:
+        order = tighten(ops, base, hop, cfg)
+    cnt = {e: 0 for e in "vstg"}
+    known = {e: {} for e in "vstgy"}
+    for o in order:
+        if o["kind"] == "a":
+            o["sig"], o["clock"] = (o["sem"], 1), {}
+            continue
+        e = o["eng"]
+        waits = {}
+        for d in sorted(o["deps"], key=lambda d: -ops[d]["fin"]):
+            q = ops[d]
+            if q["kind"] == "r" or (e == "t" and q["eng"] == "t"):
+                continue
+            s, val = q["sig"]
+            if known[e].get(s, 0) >= val:
+                continue
+            waits[s] = max(waits.get(s, 0), val)
+            known[e][s] = val
+            for s2, v2 in q["clock"].items():
+                if known[e].get(s2, 0) < v2:
+                    known[e][s2] = v2
+        o["waits"] = waits
+        o["clock"] = dict(known[e])
+        if o["kind"] == "c":
+            cnt[e] += 1
+            o["sig"] = ("s" + e, cnt[e])
+        elif o["kind"] == "d":
+            o["sig"] = (o["sem"], 16)
+    return order, cnt
+
+
+PLAN = []
+
+
+def rank_program(g, core, T, topo):
+    rank = T.rank_of(core)
+    if rank is None:
+        return
+    if not PLAN:
+        PLAN.append(schedule(CFG))
+    order, cnt = PLAN[0]
+    nxt = T.cores[(rank + 1) % len(T.cores)]
+    prv = T.cores[(rank - 1) % len(T.cores)]
+    rid, pid = topo.addr(nxt)[:2]
+    mask = topo.mask(core, nxt)
+    nout = len(topo.engines(core, nxt))
+    nin = len(topo.engines(prv, core))
+    Q = {"v": g.vector, "s": g.scalar, "t": g.tensor, "g": g, "y": g.sync}
+
+    def A(r, ind=None):
+        if not isinstance(r, tuple):
+            return r
+        if len(r) == 1:
+            return T[r[0]][:]
+        a = T[r[0]][r[1]:r[2], r[3]:r[4]] if r[5] == 1 else T[r[0]][r[1]:r[2], r[3]:r[4]:r[5]]
+        return a if ind is None else a.indirect(A(ind))
+
+    sends = 0
+    for o in order:
+        if o["kind"] == "a":
+            continue
+        q = Q[o["eng"]]
+        for s, val in o["waits"].items():
+            q.wait_ge(T.sem[s], val * nin if s[0] == "r" else val)
+        c = o["call"]
+        if c[0] == "ts":
+            if c[6] is None:
+                i = q.tensor_scalar(A(c[1]), A(c[2], c[7]), A(c[3]), None, c[5])
+            else:
+                i = q.tensor_scalar(A(c[1]), A(c[2], c[7]), A(c[3]), A(c[4]), c[5], c[6])
+        elif c[0] == "tt":
+            i = q.tensor_tensor(A(c[1], c[6]), A(c[2], c[5]), A(c[3]), c[4])
+        elif c[0] == "cp":
+            i = q.tensor_copy(A(c[1]), A(c[2], c[3]))
+        elif c[0] == "act":
+            if c[3] == AF.Copy:
+                i = q.activation(A(c[1]), A(c[2], c[6]), c[3], scale=A(c[5]))
+            else:
+                i = q.activation(A(c[1]), A(c[2], c[6]), c[3], bias=A(c[4]), scale=A(c[5]))
+        elif c[0] == "mm":
+            i = q.matmul(A(c[1]), A(c[2]), A(c[3]), c[4], c[5])
+        elif c[0] == "ms":
+            i = q.memset(A(c[1]), c[2])
+        elif c[0] == "iota":
+            if dtype_of(c[1]) == I32:
+                i = q.iota(A(c[1]), c[2], c[3], c[4])
+            else:
+                i = q.iota(A(c[1]), c[2], c[3], c[4], allow_small_or_imprecise_dtypes=True)
+        elif c[0] == "dma":
+            q.dma_start(A(c[1]), A(c[2])).then_inc(T.sem[o["sem"]], 16)
+            continue
+        else:
+            q.remote_dma(A(c[1]), A(c[2]), T.sem[c[3]], T.sem.ls, pid, rid, mask)
+            sends += 1
+            continue
+        i.then_inc(T.sem[o["sig"][0]], 1)
+    g.wait_ge(T.sem.ls, sends * nout)
+    for e in "vstg":
+        g.wait_ge(T.sem["s" + e], cnt[e])
+    for o in order:
+        if o["kind"] == "d":
+            g.wait_ge(T.sem[o["sem"]], 16)

@@ -6,54 +6,70 @@ AF = ActivationFunctionType
 V = 6
 W = 4096
 NS = 128
+NB = NS // 16
 F32, BF, F16, I32, U16 = "float32", "bfloat16", "float16", "int32", "uint16"
+Z = 2.0 ** 18
+WW = W + 7680
+PA, PBS, PD = 1280.0, 2304.0, 256.0
+QSUM = 522240.0
+ALPHA, BETA, BETA2 = 10240.0, 3072.0, 6144.0
 
 CFG = dict(
-    pb_bf16=True,
-    fused_le=True,
-    gp=4,
-    ns=128, tp=1, pc="s", fbi=1, he=1, late=0, dup="f", rnd="v", y="s", to="s",
-    gv=(10, 0, 0, 0),
-    nzp=4, nzs=(4, 4),
-    clash="s", cum="s", ent="s", cp="v", z="v", gate="s",
-    gam=1.56, sig=3.8, tau=0.5, tau2=1.0, pe=0.5, hop=100.0, shop=60.0, fix=30.0, rissue=900.0, rlat=2600.0,
-    slack=40.0, gt="v", xor="v", fmn="p", mk="vvv", off={},
+    gp=(4, 4, 4, 4), gv=(10, 0, 2, 4), tp=2, enc="bbcbbbcb", dec="ssss", aux="sss", ndep=4, zr=(15, 15), pes="t", runs="gatw", period=0, cv="svvvv", kx="-", fl="sss", mg="11", ce="s", wire="nm", par=1, lq="old", oq="old", di=60.0, rf=0.0, rb=0.0, t2=2.0, ht=0.0, za=0, rh="v", pbs=0, mv=64.0,
+    cy=0.83, gam=1.56, sig=3.8, pe=0.5, fs=90.0, hop=110.0, shop=40.0, rissue=600.0, rlat=1800.0, dlat=1500.0, dbw=200.0,
+    slack=80.0, fbi=1, off={},
+    bank=dict(cnt1="C1", Pe="D1", FMp="C1", f="C2", um="C0", pen="C1", l="C3", ko="C3", pre="C0", uh="D0", Sg="D1", U="D2",
+              cI="C2", cD="D3", cE="A2", cN="B0", acc="D0", nu="A3", gp="B2", qp="B3"),
 )
-CFG.update({'fused_le': False, 'gp': 4, 'ns': 128, 'tp': 1, 'pc': 's', 'fbi': 2, 'he': 0, 'dup': 'v', 'rnd': 's', 'y': 's', 'to': 's', 'gv': (10, 4, 1, 12), 'nzp': 8, 'nzs': (3, 8), 'clash': 's', 'cum': 's', 'ent': 's', 'cp': 'v', 'z': 'v', 'gate': 's', 'slack': 40, 'gt': 's', 'xor': 's', 'fmn': 'v', 'mk': 'ssv',
-            'off': {'a1': 4900, 's1': 22500, 'k1': 5300, 'a0': 39900, 'l0': 4400, 'g0': 3300, 'g1': -700, 'k0': -5800, 't1': -31900, 'e1': -12600, 'e0': 21400, 's0': -1400, 'm0': 1000, 'd1': 49900, 'z1': -18600, 'd0': 6600, 'l1': -21600, 'p1': -2400, 'm1': 600, 'z0': 6800, 't0': 5000, 'p0': 300}})
 
-MATS_BF = ["I", "NI", "BO", "D1", "Ub", "Lin", "M2", "R15", "Ma", "Mf", "BOd", "R150", "Cm", "Ch", "Big", "Wh", "Wl", "DIb", "IUb", "Zr", "R15n", "In"]
-MATS_H = ["U", "DI", "IU", "T0I", "T0M", "NT0", "BOh", "BOc", "BOg", "E15", "Sw", "Ih"]
-COLS = ["pm", "p", "pp", "pg", "pi", "c16", "m15", "nl15", "n0", "wk", "cm", "ch", "big", "e15", "p8", "t1", "a16", "t2",
-        "bcum", "bcp", "wa", "whs", "wls"]
+CFG.update({'gp': (4, 4, 4, 4), 'gv': (5, 5, 10, 5), 'tp': 2, 'enc': 'bbcbbcab', 'dec': 'ssss', 'aux': 'sss', 'ndep': 4, 'zr': (15, 0), 'pes': 't', 'runs': 'gatwz', 'period': 15000, 'cv': 'ssssv', 'kx': 'v', 'slack': -1, 'fbi': 2, 'off': {'g0': -1000.0, 'b0': 800.0, 'a0': 300.0, 'z0': 400.0, 'c0': -4300.0, 'd0': -4700.0, 'f0': 3900.0, 'p0': -4000.0, 't0': 5300.0, 'm0': 3900.0, 'q0': 400.0, 's0': -100.0, 'h0': 5700.0, 'u0': 6100.0, 'l0': -2800.0, 'e0': 7300.0, 'k0': 5700.0, 'g1': 2600.0, 'b1': -500.0, 'a1': 500.0, 'z1': 5000.0, 'c1': 4000.0, 'd1': 3000.0, 'f1': 8500.0, 'p1': 5000.0, 't1': -300.0, 'm1': 7700.0, 'q1': -1000.0, 's1': 9600.0, 'h1': 5600.0, 'u1': 6000.0, 'l1': 12300.0, 'e1': -7900.0, 'k1': -1000.0, '0': -6400.0, 'w': -20400.0, 'n': -10900.0, 'o': 5400.0}})
+CFG.update({'gp': (4, 4, 4, 4), 'gv': (9, 2, 2, 1), 'tp': 1, 'enc': 'bbcbbcab', 'dec': 'ssss', 'aux': 'ssv', 'ndep': 4, 'zr': (15, 15), 'pes': 's', 'runs': 'gatwz', 'period': 16000, 'cv': 'ssvvv', 'kx': 'v', 'fl': 'vvs', 'mg': '11', 'ce': 's', 'fs': 90.0, 'slack': -1, 'fbi': 1, 'off': {'g0': -800.0, 'b0': 1300.0, 'a0': -1000.0, 'z0': -4700.0, 'c0': -6600.0, 'd0': -2100.0, 'f0': 5800.0, 'p0': -1500.0, 't0': 4600.0, 'm0': 3800.0, 'q0': -3800.0, 's0': 700.0, 'h0': 3000.0, 'u0': 4200.0, 'l0': -1000.0, 'e0': 7600.0, 'k0': 3000.0, 'g1': 2600.0, 'b1': 1800.0, 'a1': -2100.0, 'z1': 700.0, 'c1': 6300.0, 'd1': 7400.0, 'f1': 8600.0, 'p1': 4800.0, 't1': -1200.0, 'm1': 6700.0, 'q1': -500.0, 's1': 1400.0, 'h1': 2000.0, 'u1': 6300.0, 'l1': 9900.0, 'e1': -12500.0, 'k1': 4000.0, '0': -14700.0, 'w': -19400.0, 'n': -9200.0, 'o': 5400.0}})
+CFG.update(dict(pe=0.44, hop=120.0, shop=100.0, rissue=600.0, rlat=1200.0, fs=50.0, rf=600.0, rb=4.0, di=900.0, dbw=200.0))
+CFG.update({'gp': (4, 4, 4, 4), 'gv': (3, 2, 2, 1), 'tp': 2, 'enc': 'bbcbbcab', 'dec': 'ssss', 'aux': 'vss', 'ndep': 2, 'zr': (15, 15), 'pes': 't', 'runs': 'gatwz', 'period': 16000, 'cv': 'ssvvv', 'kx': 'v', 'fl': 'vvs', 'mg': '11', 'ce': 's', 'wire': '2', 'par': 15, 'lq': 'ysyggggg', 'oq': 'gggsyyg', 'di': 900.0, 'rf': 600.0, 'rb': 4.0, 'fs': 50.0, 'slack': -1, 'fbi': 1, 'off': {'g0': -1600.0, 'b0': 1500.0, 'a0': -1200.0, 'z0': -2600.0, 'c0': -4600.0, 'd0': -4500.0, 'f0': 6100.0, 'p0': -3600.0, 't0': 5500.0, 'm0': 2000.0, 'q0': -6100.0, 's0': -1100.0, 'h0': 2900.0, 'u0': 3400.0, 'l0': -4900.0, 'e0': 5800.0, 'k0': 6200.0, 'g1': 2600.0, 'b1': 4000.0, 'a1': -6000.0, 'z1': -400.0, 'c1': -2600.0, 'd1': 6800.0, 'f1': 9100.0, 'p1': 6300.0, 't1': -1600.0, 'm1': 7000.0, 'q1': -5200.0, 's1': 1100.0, 'h1': 4700.0, 'u1': 6000.0, 'l1': 8500.0, 'e1': -17600.0, 'k1': 5400.0, '0': -11800.0, 'w': -18100.0, 'n': -7900.0, 'o': 6800.0}})
+CFG.update(dict(pe=0.44, hop=160.0, shop=160.0, rissue=500.0, rlat=2900.0, fs=70.0, rf=0.0, rb=2.0, di=60.0, dbw=400.0, gam=1.38, sig=2.8, t2=1.0, kx="-"))
+CFG.update({'gp': (4, 4, 4, 4), 'gv': (10, 2, 3, 1), 'tp': 1, 'aux': 'gss', 'pes': 's', 'period': 17000, 'cv': 'sssvv', 'fl': 'vvs', 'mg': '01', 'ce': 's', 'wire': '3', 'par': 8, 'slack': 40, 'fbi': 1, 'off': {'g0': -5000.0, 'b0': 2200.0, 'a0': -1500.0, 'z0': -1600.0, 'c0': -4100.0, 'd0': -5400.0, 'f0': 4800.0, 'p0': -3200.0, 't0': 7000.0, 'm0': 2600.0, 'q0': -8400.0, 's0': -3300.0, 'h0': 4600.0, 'u0': 4100.0, 'l0': -6600.0, 'e0': 4900.0, 'k0': 9200.0, 'g1': 3100.0, 'b1': 4800.0, 'a1': -1000.0, 'z1': 1500.0, 'c1': -4900.0, 'd1': 700.0, 'f1': 8000.0, 'p1': 7300.0, 't1': 2900.0, 'm1': 7000.0, 'q1': -6500.0, 's1': 6100.0, 'h1': 4200.0, 'u1': 4300.0, 'l1': 6000.0, 'e1': -24400.0, 'k1': 5400.0, '0': -9700.0, 'w': -17800.0, 'n': -6400.0, 'o': 4400.0}})
+CFG.update({'lq': 'ysysyyyy', 'oq': 'yyysyys', 'di': 200.0, 'dbw': 330.0, 'gv': (9, 2, 3, 4), 'fbi': 2, 'off': {'g0': -4200.0, 'b0': 2200.0, 'a0': -4300.0, 'z0': -4900.0, 'c0': 1000.0, 'd0': -300.0, 'f0': 4300.0, 'p0': -5900.0, 't0': 5600.0, 'm0': 5600.0, 'q0': -11500.0, 's0': -2500.0, 'h0': -1900.0, 'u0': 2800.0, 'l0': -1900.0, 'e0': -1200.0, 'k0': 8000.0, 'g1': 3100.0, 'b1': 3600.0, 'a1': -3400.0, 'z1': 2000.0, 'c1': -5400.0, 'd1': 1700.0, 'f1': 7500.0, 'p1': 3800.0, 't1': 1900.0, 'm1': 9100.0, 'q1': -7000.0, 's1': 5700.0, 'h1': 4400.0, 'u1': 2700.0, 'l1': 7900.0, 'e1': -23700.0, 'k1': 3000.0, '0': -8200.0, 'w': -14900.0, 'n': -9600.0, 'o': 9300.0}})
+CFG.update(dict(hop=90.0, shop=100.0, ht=50.0, fs=66.0, rlat=3000.0, pe=0.46, rissue=650.0, gam=1.22, sig=2.0, cy=0.96, dbw=200.0, dlat=400.0, di=60.0))
+CFG.update({'gp': (4, 4, 4, 4), 'gv': (5, 0, 3, 0), 'tp': 2, 'enc': 'babbabba', 'aux': 'vvs', 'ndep': 4, 'zr': (15, 15), 'pes': 't', 'period': 16000, 'cv': 'svsvv', 'fl': 'vvs', 'mg': '11', 'ce': 's', 'wire': '3', 'par': 1, 'lq': 'ysysysyyyy', 'za': 2, 'slack': 0, 'fbi': 1, 'off': {'g0': 0.0, 'b0': -2900.0, 'a0': 2400.0, 'z0': 300.0, 'c0': -1000.0, 'd0': -2100.0, 'f0': 4700.0, 'p0': 5200.0, 't0': 4900.0, 'm0': 4100.0, 'q0': 4200.0, 's0': 11300.0, 'h0': 7100.0, 'u0': 9800.0, 'l0': 3800.0, 'e0': 5600.0, 'k0': 11700.0, 'g1': 6000, 'b1': 7900.0, 'a1': 6200.0, 'z1': 11100.0, 'c1': 10200.0, 'd1': 11500.0, 'f1': 10800.0, 'p1': 10200.0, 't1': 10700.0, 'm1': 12800.0, 'q1': 13700.0, 's1': 19100.0, 'h1': 13800.0, 'u1': 8400.0, 'l1': 11700.0, 'e1': 15100.0, 'k1': 13000.0, '0': -4600.0, 'w': -14100.0, 'n': -18700.0, 'o': 6600.0}})
+CFG.update(pbs=1)
+CFG.update(dict(hop=120.0, shop=120.0, ht=130.0, fs=20.0, rlat=2050.0, pe=0.49, rissue=400.0, gam=1.6, sig=3.6, cy=0.84, dbw=220.0, dlat=400.0, di=60.0, mv=85.0))
+CFG.update({'gp': (4, 4, 4, 4), 'gv': (10, 2, 10, 8), 'tp': 1, 'enc': 'babbabba', 'dec': 'vsss', 'pes': 'v', 'period': 15500, 'cv': 'ssssv', 'fl': 'vss', 'mg': '11', 'ce': 's', 'wire': 'nm', 'par': 1, 'slack': 0, 'fbi': 1, 'off': {'g0': 200.0, 'b0': 700.0, 'a0': -2100.0, 'z0': 1200.0, 'c0': 700.0, 'd0': 1700.0, 'f0': 5000.0, 'p0': 5500.0, 't0': 4700.0, 'm0': 2100.0, 'q0': 7300.0, 's0': 11200.0, 'h0': 4600.0, 'u0': 6300.0, 'l0': 5200.0, 'e0': 7600.0, 'k0': 10900.0, 'g1': 5900.0, 'b1': 5500.0, 'a1': 7700.0, 'z1': 7600.0, 'c1': 6100.0, 'd1': 10000.0, 'f1': 9800.0, 'p1': 11200.0, 't1': 12400.0, 'm1': 9300.0, 'q1': 10200.0, 's1': 17000.0, 'h1': 9300.0, 'u1': 8400.0, 'l1': 11600.0, 'e1': 12000.0, 'k1': 11200.0, '0': -4700.0, 'w': -9400.0, 'n': -13500.0, 'o': 9000.0}, 'bank': {'cnt1': 'C1', 'Pe': 'D1', 'FMp': 'C1', 'f': 'C2', 'um': 'A0', 'pen': 'C1', 'l': 'C3', 'ko': 'C3', 'pre': 'C0', 'uh': 'D0', 'Sg': 'D1', 'U': 'A1', 'cI': 'C2', 'cD': 'D3', 'cE': 'A2', 'cN': 'B0', 'acc': 'C0', 'nu': 'A3', 'gp': 'B2', 'qp': 'B3'}})
+
+MATS_BF = ["I", "NI", "BO", "Mpar", "Lin", "Mf2", "RZ", "I255", "IZ", "BOb", "BOf", "Cp", "BOg", "D1", "M2", "Ls2", "DQ",
+           "RU", "CI", "CD", "CE", "GI", "GE", "GD", "QD", "GN", "T0a", "T0w", "Wh", "Wl", "Ch", "SS", "SF",
+           "X0", "X15", "XD", "t1", "t2", "t3", "t4", "t5", "t6", "t7", "Ub", "D2b", "I2b"]
+MATS_H = ["U", "Ih", "D", "D2", "E15", "Rh", "I2", "BO2", "Sw"]
+COLS = ["p", "pg", "pi", "c16", "m0", "m15", "n0", "nl15", "nl14", "bc", "bg", "bq", "cm", "cp", "a2", "aq",
+        "wq", "wcd", "wce", "wgi", "wgd", "wqd", "wss", "wa", "whs", "wls", "p8", "t1", "t2", "t3", "ch", "e15", "ka"]
 
 SCRATCH = {
-    "win": ("sbuf", [128, W + 256], BF),
-    "G0": ("sbuf", [128, 32 * NS], BF), "G1": ("sbuf", [128, 16 * NS], BF),
-    "NZ": ("sbuf", [128, 32 * NS], BF), "IND": ("sbuf", [128, 32 * NS], BF),
+    "win": ("sbuf", [128, WW], BF), "wout": ("sbuf", [128, WW], BF), "raw": ("sbuf", [128, W], BF),
+    "G0": ("sbuf", [128, 16 * NS + 16], BF), "G1": ("sbuf", [128, 16 * NS + 16], BF),
+    "IND": ("sbuf", [128, 32 * NS], BF), "GA": ("sbuf", [128, 32 * NS], BF),
     "ofs": ("sbuf", [128, V * 256], U16), "snd": ("sbuf", [128, V * 256], U16),
-    "rM": ("sbuf", [128, V * 256], BF), "sM": ("sbuf", [128, V * 256], BF),
-    "rST": ("sbuf", [128, V * 512], BF), "sST": ("sbuf", [128, V * 512], BF),
-    "hh": ("sbuf", [128, 2 * 16 * NS], F16), "bb": ("sbuf", [128, 2 * 16 * NS], BF),
-    "ii": ("sbuf", [128, 4 * NS], I32), "ff": ("sbuf", [128, 512], F32), "I32": ("sbuf", [128, 128], F32),
-    "ko": ("sbuf", [128, 16], U16), "so": ("sbuf", [128, 32], U16), "l3": ("sbuf", [128, 48], F32),
+    "rNM": ("sbuf", [128, V * 512], F16), "sNM": ("sbuf", [128, V * 512], F16),
+    "rST": ("sbuf", [128, V * 768], BF), "sST": ("sbuf", [128, V * 768], BF),
+    "hh": ("sbuf", [128, 2 * 8 * NS], F16), "bb": ("sbuf", [128, 2 * 16 * NS], BF),
+    "ii": ("sbuf", [128, 2 * NS], I32), "ff": ("sbuf", [128, 2 * 4 * NS], F32),
+    "ko": ("sbuf", [128, 16], U16), "so": ("sbuf", [128, 32], U16),
     "inN": ("sbuf", [128, 256], I32), "inM": ("sbuf", [128, 256], I32), "inO": ("sbuf", [128, 256], I32),
     "inW": ("sbuf", [128, 4], I32), "inT": ("sbuf", [128, 8], I32), "ic": ("sbuf", [128, 8], I32),
-    "ownN": ("sbuf", [128, 256], F16), "ownP": ("sbuf", [128, 256], F16),
-    "X": ("sbuf", [128, 144], F32), "QB": ("sbuf", [128, 128], F32), "col": ("sbuf", [128, 32], F32),
-    "Zo": ("sbuf", [128, 144], BF), "Zk": ("sbuf", [128, 144], BF), "Zh": ("sbuf", [128, 144], F16),
+    "inP": ("sbuf", [128, 256], BF), "ow": ("sbuf", [128, 512], F16),
+    "X": ("sbuf", [128, 128], BF), "XQ": ("sbuf", [128, 144], BF), "QB": ("sbuf", [128, 128], BF),
+    "col": ("sbuf", [128, 48], F32),
+    "Zo": ("sbuf", [128, 144], BF), "Zs": ("sbuf", [128, 144], BF), "Zh": ("sbuf", [128, 144], F16),
     "mb": ("sbuf", [128, 128 * len(MATS_BF)], BF), "mh": ("sbuf", [128, 128 * len(MATS_H)], F16),
-    "ones": ("sbuf", [128, 256], BF), "sm": ("sbuf", [128, 80], BF), "k1": ("sbuf", [128, 32], F32),
-    "thb": ("sbuf", [128, 8], BF), "Gm": ("sbuf", [128, 128], BF), "thc": ("sbuf", [128, 16], F32),
+    "ones": ("sbuf", [128, NS], BF), "sm": ("sbuf", [128, 32], BF), "k1": ("sbuf", [128, 16], F32),
+    "xs": ("sbuf", [128, 128], BF), "eh": ("sbuf", [128, 48], BF),
+    "thb": ("sbuf", [128, 8], BF), "thg": ("sbuf", [128, 128], BF), "thc": ("sbuf", [128, 16], F32),
     "oN": ("sbuf", [128, 256], F32), "oM": ("sbuf", [128, 256], F32), "oA": ("sbuf", [128, 256], F32),
-    "K0": ("psum", [128, 1024], BF) if CFG["pb_bf16"] else ("psum", [128, 512], F32),
 }
-for _k in range(1, 8):
+for _k in range(8):
     SCRATCH["K%d" % _k] = ("psum", [128, 512], F32)
 
-DMAS = ["dN", "dD", "dM", "dO", "dP0", "dP1", "dW", "dT", "oD", "oN0", "oN1", "oM0", "oM1", "oP0", "oP1", "oA0", "oA1"]
+DMAS = ["dN", "dM", "dO", "dP0", "dP1", "dW", "dT", "oN0", "oN1", "oM0", "oM1", "oP0", "oP1", "oA0", "oA1"] + \
+       ["dD%d" % i for i in range(8)] + ["oD%d" % i for i in range(4)]
 SEMAPHORES = ["sv", "ss", "st", "sg", "ls"] + DMAS + ["r%s%d%d" % (k, v, c) for k in "NMS" for v in range(1, V) for c in range(2)]
-DRAM = ("dep", "nam", "mrk", "own", "pic", "wt", "thr", "ydep", "ynam", "ymrk", "ypic", "ycut")
 
 
 def R(buf, c0, c1, st=1, p0=0, p1=128):
@@ -72,63 +88,109 @@ def is_ps(r):
     return r[0][0] == "K" and len(r[0]) == 2
 
 
-def build(cfg):
-    ops = []
-    n = cfg["ns"]
-    nc, nb = 256 // n, n // 16
-    lab = ["0"]
+def cut(r, i, s):
+    return R(r[0], r[3] + i * s * r[5], r[3] - r[3] % r[5] + (i + 1) * s * r[5], r[5])
 
-    def add(eng, cost, ins, outs, call, **kw):
-        o = dict(eng=eng, cost=cost, ins=[r for r in ins if isinstance(r, tuple)], outs=outs, call=call, k=len(ops), lat=0.0, kind="c", lab=lab[0])
-        o.update(kw)
-        ops.append(o)
-        return o
+
+def part(r, p0, p1):
+    return (r[0], p0, p1) + r[3:]
+
+
+def cost_of(c, cfg):
+    cy = cfg["cy"]
 
     def two(*rs):
         return all(dtype_of(r) in (BF, F16, U16) for r in rs)
 
-    def ts(out, a, s1, s2, o0, o1=None, ind=None):
-        c = max(64.0, width(out) * (0.5 if two(out, a) else 1.0)) + cfg["fix"]
-        if ind is not None:
-            c = 50 + width(out) * cfg["gam"]
-        add("v", c, [a, s1, s2, ind], [out], ("ts", out, a, s1, s2, o0, o1, ind))
+    k = c[0]
+    if k in ("ts", "cp"):
+        if c[-1] is not None:
+            return 50 + width(c[1]) * cfg["gam"] * cy
+        return max(cfg["mv"], width(c[1]) * (0.5 if two(c[1], c[2]) else 1.0)) * cy
+    if k == "cs":
+        return 50 + width(c[2]) * cfg["sig"] * cy
+    if k == "tt":
+        if c[5] is not None:
+            return 50 + width(c[1]) * cfg["gam"] * cy
+        if c[6] is not None:
+            return 50 + width(c[2]) * cfg["sig"] * cy
+        return max(cfg["mv"], width(c[1]) * (1.0 if is_ps(c[2]) or is_ps(c[3]) else cfg["t2"] if two(c[2], c[3]) else 2.0)) * cy
+    if k == "act":
+        if c[6] is not None:
+            return 65 + width(c[1]) * cfg["gam"] * cy
+        return max(64.0, width(c[1])) * cy + cfg["fs"]
+    if k == "mm":
+        return sum(max(min(64.0, width(l)), width(r)) for l, r in c[2]) * cfg["pe"]
+    if k == "mms":
+        return sum(max(min(64.0, width(m[1])), width(m[2])) for m in c[1]) * cfg["pe"] * cy / 0.83
+    if k == "ms":
+        return max(64.0, width(c[1]) * 0.5) * cy
+    if k == "iota":
+        return 130 + 2 * width(c[1]) * cy
+    if k == "dma":
+        return cfg["di"]
+    if k == "link":
+        return cfg["rf"] + width(c[1]) * cfg["rb"]
+    if k == "send":
+        return cfg["rissue"]
+    return 0.0
 
-    def tt(out, a, b, op, ind=None, sct=None):
-        if ind is not None:
-            c = 50 + width(out) * cfg["gam"]
-        elif sct is not None:
-            c = 50 + width(a) * cfg["sig"]
-        else:
-            ps = is_ps(a) or is_ps(b)
-            f = (cfg["tau"] if ps else cfg["tau2"]) if two(out, a, b) else (1.0 if ps else 2.0)
-            c = max(64.0, width(out) * f) + cfg["fix"]
-        add("v", c, [a, b, ind, sct], [out], ("tt", out, a, b, op, ind, sct))
+
+def build(cfg):
+    ops = []
+    n, nb, nc = NS, NB, 2
+    lab = ["0", -1]
+    loads = []
+
+    def add(eng, ins, outs, call, **kw):
+        o = dict(eng=eng, cost=cost_of(call, cfg) if call else 0.0, ins=[r for r in ins if isinstance(r, tuple)], outs=outs,
+                 call=call, k=len(ops), lat=0.0, kind="c", lab=lab[0], v=lab[1], after=[], soft=[])
+        o.update(kw)
+        ops.append(o)
+        return o
+
+    def ts(out, a, s1, s2, o0, o1=None):
+        return add("v", [a, s1, s2], [out], ("ts", out, a, s1, s2, o0, o1, None))
+
+    def tt(out, a, b, op, sct=None, ind=None):
+        return add("v", [a, b, sct, ind], [out], ("tt", out, a, b, op, ind, sct))
 
     def cp(out, a, ind=None):
-        c = max(64.0, width(out) * (0.5 if two(out, a) else 1.0)) + cfg["fix"]
-        if ind is not None:
-            c = 50 + width(out) * cfg["gam"]
-        add("v", c, [a, ind], [out], ("cp", out, a, ind))
+        return add("v", [a, ind], [out], ("cp", out, a, ind))
 
     def act(out, a, f, bias=0.0, scale=1.0, ind=None):
-        c = max(64.0, width(out)) + cfg["fix"]
-        if ind is not None:
-            c = 65 + width(out) * cfg["gam"]
-        add("s", c, [a, bias, scale, ind], [out], ("act", out, a, f, bias, scale, ind))
+        return add("s", [a, bias, scale, ind], [out], ("act", out, a, f, bias, scale, ind))
+
+    def lin(eng, out, a, scale, bias=0.0):
+        if eng == "s":
+            return act(out, a, AF.Identity if bias != 0.0 else AF.Copy, bias, scale)
+        return ts(out, a, scale, bias, AL.mult, AL.add)
 
     def mm(out, l, r, start, stop):
-        add("t", max(64.0, width(r)) * cfg["pe"] * (4 if dtype_of(r) == F32 else 1) + 5, [l, r], [out], ("mm", out, l, r, start, stop), start=start)
+        return grp(out, [(l, r)], start, stop)
 
     def grp(out, terms, first=True, end=True):
-        for i, (l, r) in enumerate(terms):
-            mm(out, l, r, first and i == 0, end and i == len(terms) - 1)
+        return add("t", [r for t in terms for r in t], [out], ("mm", out, terms, first, end))
+
+    def ms(r, val):
+        return add("v", [], [r], ("ms", r, val))
 
     def dma(q, sem, out, a, nbytes):
-        add(q, 60.0, [a], [out], ("dma", out, a), kind="d", sem=sem, lat=2000.0 + nbytes / 180.0)
+        o = add(q, [a], [out], ("dma", out, a), kind="d", sem=sem, lat=cfg["dlat"] + nbytes / cfg["dbw"], nbytes=nbytes)
+        if lab[1] < 0:
+            o["soft"] = [k for k in loads if ops[k]["eng"] == q][-1:]
+            loads.append(o["k"])
+        return o
 
     def send(sem, dst, src):
-        s = add("g", cfg["rissue"], [src], [], ("send", dst, src, sem), kind="r")
-        add("x", 0.0, [], [dst], None, kind="a", sem=sem, src=s["k"], lat=cfg["rlat"] + width(src) * 2)
+        s = add("g", [src], [], ("send", dst, src, sem), kind="r")
+        if cfg["rb"]:
+            add("x", [dst], [dst], ("link", dst), kind="a", sem=sem, src=s["k"], lat=cfg["rlat"])
+        else:
+            add("x", [], [dst], None, kind="a", sem=sem, src=s["k"], lat=cfg["rlat"] + width(src) * 2)
+
+    def iota(out, pat, base, cm):
+        add("g", [], [out], ("iota", out, pat, base, cm))
 
     def mb(name):
         i = MATS_BF.index(name)
@@ -145,375 +207,450 @@ def build(cfg):
     def zs(buf, a):
         return R(buf, 16 - a, 144 - a)
 
-    dma("y", "dN", R("inN", 0, 256), R("nam", 0, 256), 131072)
-    dma("y", "dD", R("win", 0, W), R("dep", 0, W), 1 << 20)
-    dma("s", "dT", R("inT", 0, 6, 1, 0, 8), R("thr", 0, 6, 1, 0, 8), 200)
-    dma("s", "dW", R("inW", 0, 1), ("wt",), 500)
-    dma("y", "dM", R("inM", 0, 256), R("mrk", 0, 256), 1200000)
-    dma("y", "dO", R("inO", 0, 256), R("own", 0, 256), 1300000)
+    nd = cfg["ndep"]
+    lq, oq = cfg["lq"], "yyyyyss" if cfg["oq"] == "old" else cfg["oq"]
+    for i in range(nd):
+        dma("y" if lq == "old" else lq[i], "dD%d" % i, R("raw", i * W // nd, (i + 1) * W // nd), R("dep", i * W // nd, (i + 1) * W // nd), (i + 1) * (1 << 20) // nd)
+    if lq == "old":
+        dma("y", "dN", R("inN", 0, 256), R("nam", 0, 256), 1180000)
+        dma("y", "dT", R("inT", 0, 6, 1, 0, 8), R("thr", 0, 6, 1, 0, 8), 1180000)
+        dma("y", "dW", R("inW", 0, 1), ("wt",), 1180000)
+        dma("y", "dM", R("inM", 0, 256), R("mrk", 0, 256), 1300000)
+        dma("y", "dO", R("inO", 0, 256), R("own", 0, 256), 1430000)
+        for c in range(nc):
+            dma("y", "dP%d" % c, R("rST", 3 * n * c + n, 3 * n * c + 2 * n), R("pic", n * c, n * c + n), 1500000)
+    else:
+        dma(lq[nd], "dN", R("inN", 0, 256), R("nam", 0, 256), 600000)
+        dma(lq[nd + 1], "dT", R("inT", 0, 6, 1, 0, 8), R("thr", 0, 6, 1, 0, 8), 600000)
+        dma(lq[nd + 2], "dM", R("inM", 0, 256), R("mrk", 0, 256), 600000)
+        dma(lq[nd + 3], "dP0", R("inP", 0, 256), R("pic", 0, 256), 600000)
+        dma(lq[nd + 4], "dO", R("inO", 0, 256), R("own", 0, 256), 600000)
+        dma(lq[nd + 5], "dW", R("inW", 0, 1), ("wt",), 600000)
+    X, BO, I = R("X", 0, 128), mb("BO"), mb("I")
+    iota(X, [[1, 128]], 0, -1)
+    iota(R("ic", 0, 1), [[1, 1]], 0, 1)
+    iota(R("QB", 0, 128), [[1, 8], [0, 16]], 0, 0)
+    iota(R("XQ", 0, 144), [[1, 144]], 0, 0)
+    ts(I, X, 0.0, None, AL.is_equal)
+    lab[0] = "n"
+    cp(R("ofs", 0, 256), R("inN", 0, 256))
+    lab[0] = "w"
+    for i, how in enumerate(cfg["enc"]):
+        s = W // len(cfg["enc"])
+        x, zt, kb, out = R("raw", i * s, (i + 1) * s), R("IND", i * s, (i + 1) * s), R("K%d" % (i % 8), 0, s), R("win", i * s, (i + 1) * s)
+        if how == "a":
+            act(kb, x, AF.Relu, Z, -Z)
+            tt(out, x, kb, AL.subtract)
+        else:
+            ts(zt, x, 0.0, -Z, AL.is_equal, AL.mult)
+            grp(kb, [(I, x), (I, zt)])
+            if how == "b":
+                act(out, kb, AF.Copy)
+            else:
+                cp(out, kb)
+    lab[0] = "0"
     for c in range(nc):
-        dma("y", "dP%d" % c, R("rST", 2 * n * c + n, 2 * n * c + 2 * n), R("pic", n * c, n * c + n), 1300000)
-        add("v", 94.0, [], [R("rST", 2 * n * c, 2 * n * c + n)], ("ms", R("rST", 2 * n * c, 2 * n * c + n), 0.0))
-    add("g", 130 + 2 * 144, [], [R("X", 0, 144)], ("iota", R("X", 0, 144), [[1, 144]], 0, 0))
-    add("g", 140, [], [R("ic", 0, 1)], ("iota", R("ic", 0, 1), [[1, 1]], 0, 1))
-    add("g", 140, [], [R("col", 0, 3)], ("iota", R("col", 0, 3), [[1, 3]], -1, 1))
-    add("g", 130 + 256, [], [R("QB", 0, 128)], ("iota", R("QB", 0, 128), [[1, 8], [0, 16]], 0, 0))
-    for r, val in ((R("ones", 0, n), 1.0), (R("win", W, W + n), 0.0), (R("sm", 16 + 2 * nb, 16 + 3 * nb), 0.0)):
-        add("v", 94.0, [], [r], ("ms", r, val))
-    cp(R("ofs", 0, 128), R("inN", 0, 128))
-    cp(R("ofs", 128, 256), R("inN", 128, 256))
-    X = R("X", 0, 128)
+        ms(R("G%d" % c, 16 * n, 16 * n + 16), 0.0)
+        ms(R("rST", 3 * n * c, 3 * n * c + n), 0.0)
+    ones = R("ones", 0, n)
+    ms(ones, 1.0)
+    cp(col("p"), R("ic", 0, 1))
     ts(R("ic", 1, 2), R("ic", 0, 1), 4, None, AL.arith_shift_right)
     ts(R("ic", 2, 3), R("ic", 0, 1), 15, None, AL.bitwise_and)
-    cp(R("col", 3, 5), R("ic", 1, 3))
-    ts(col("c16"), col("pg"), 16.0, 16.0, AL.mult, AL.add)
-    ts(col("m15"), col("pi"), 15.0, None, AL.is_equal)
-    ts(col("nl15"), col("pi"), 15.0, None, AL.is_lt)
-    ts(col("n0"), col("pi"), 0.0, None, AL.is_gt)
-    act(col("wk"), col("m15"), AF.Identity, -1.0, 16.0)
-    act(col("cm"), col("pi"), AF.Identity, 1.0 / 32, -1.0 / 16)
-    act(col("ch"), col("m15"), AF.Copy, 0.0, -0.5)
-    act(col("big"), col("m15"), AF.Copy, 0.0, 3.0 * 2 ** 22)
-    act(col("e15"), col("m15"), AF.Copy, 0.0, 4096.0)
-    ts(col("t1"), col("pi"), 8.0, -16.0, AL.is_ge, AL.mult)
-    ts(col("p8"), col("p"), col("t1"), 8.0, AL.add, AL.add)
-    ts(col("t2"), col("pi"), 6.0, None, AL.is_le)
-    tt(col("a16"), col("t2"), col("n0"), AL.mult)
-    k1 = 1.0 if cfg["clash"] == "s" else 0.0
-    if cfg["cum"] == "s":
-        act(col("bcum"), col("pi"), AF.Identity, k1, k1)
+    cp(R("col", 1, 3), R("ic", 1, 3))
+    pi = col("pi")
+    lin("s", col("c16"), col("pg"), 16.0, 16.0)
+    ts(col("m0"), pi, 0.0, None, AL.is_equal)
+    ts(col("m15"), pi, 15.0, None, AL.is_equal)
+    lin("s", col("n0"), col("m0"), -1.0, 1.0)
+    lin("s", col("nl15"), col("m15"), -1.0, 1.0)
+    ts(col("nl14"), pi, 14.0, None, AL.is_lt)
+    k1 = 1.0 if cfg["fl"][0] == "s" else 0.0
+    if cfg["fl"][1] == "s":
+        lin("v", col("bc"), pi, k1, k1)
     else:
-        act(col("bcum"), col("pi"), AF.Identity, 1.0 - k1, -k1)
-    k2 = 1.0 if cfg["ent"] == "s" else 0.0
-    if cfg["cp"] == "s":
-        act(col("bcp"), col("pi"), AF.Identity, 0.5 * k2 - 1.0, k2)
-    else:
-        act(col("bcp"), col("pi"), AF.Identity, 2.0 - 0.5 * k2, -k2)
-    ts(R("Zo", 0, 144), R("X", 0, 144), col("c16"), None, AL.is_equal)
-    ts(mb("I"), X, col("p"), None, AL.is_equal)
-    ts(mb("BO"), R("QB", 0, 128), col("pg"), None, AL.is_equal)
-    ts(mb("D1"), X, col("pp"), col("nl15"), AL.is_equal, AL.mult)
-    ts(mb("Ub"), X, col("pm"), col("n0"), AL.is_equal, AL.mult)
-    act(R("Zk", 0, 144), R("Zo", 0, 144), AF.Copy, 0.0, col("wk"))
-    cp(R("Zh", 0, 144), R("Zo", 0, 144))
-    ts(mb("M2"), X, col("p"), None, AL.is_ge)
-    tt(mb("Lin"), mb("M2"), mb("BO"), AL.mult)
-    ts(mb("M2"), mb("Lin"), 2.0, None, AL.mult)
-    tt(mb("M2"), mb("M2"), mb("I"), AL.subtract)
-    if k2:
-        act(mb("M2"), mb("M2"), AF.Copy, 0.0, 0.5)
-    act(mb("NI"), mb("I"), AF.Copy, 0.0, -1.0)
-    if cfg["dup"] == "f":
-        act(R("I32", 0, 128), mb("I"), AF.Copy)
-    if cfg["dup"] == "v":
-        cp(mh("Ih"), mb("I"))
-    act(mb("R15"), mb("BO"), AF.Copy, 0.0, col("m15"))
-    act(mb("R15n"), mb("R15"), AF.Copy, 0.0, -256.0)
-    act(mb("In"), mb("I"), AF.Copy, 0.0, -256.0)
-    tt(mb("Ma"), mb("R15"), mb("I"), AL.subtract)
-    tt(mb("Mf"), mb("I"), mb("D1"), AL.subtract)
-    act(mb("BOd"), mb("BO"), AF.Copy, 0.0, 1.0 / 16)
-    act(mb("R150"), zs("Zo", 0), AF.Copy, 0.0, col("m15"))
-    act(mb("Cm"), mb("I"), AF.Copy, 0.0, col("cm"))
-    act(mb("Ch"), mb("I"), AF.Copy, 0.0, col("ch"))
-    act(mb("Big"), mb("I"), AF.Copy, 0.0, col("big"))
+        lin("v", col("bc"), pi, -k1, 0.5 - k1)
+    ts(col("bg"), pi, -1.0, 0.0, AL.add, AL.max)
+    lin("v", col("bq"), col("m0"), 32.0, 1.0)
+    lin("s", col("cm"), pi, -1.0 / 16, 1152.0 - 15.0 / 32)
+    lin("s", col("cp"), pi, PBS, PA)
+    lin("s", col("a2"), col("nl15"), 2.0)
+    lin("s", col("aq"), col("m15"), -17.0, 2.0)
+    ts(col("wq"), col("nl14"), 32.0, col("m15"), AL.mult, AL.add)
+    lin("s", col("wcd"), col("m15"), 1.5 * ALPHA, -ALPHA)
+    lin("s", col("t1"), col("m15"), -BETA2)
+    ts(col("wce"), col("nl14"), -ALPHA, col("t1"), AL.mult, AL.add)
+    lin("s", col("wgi"), col("m0"), ALPHA + 2 * BETA, -BETA)
+    lin("s", col("wgd"), col("m0"), 0.5 * ALPHA + BETA, -BETA)
+    lin("s", col("wqd"), col("m0"), 0.25 - BETA - 0.5 * ALPHA, BETA + 0.5 * ALPHA)
+    lin("s", col("wss"), col("nl15"), -1.0)
+    lin("s", col("ch"), col("m15"), -0.5)
+    lin("s", col("e15"), col("m15"), 4096.0)
+    ts(col("t2"), pi, 8.0, -16.0, AL.is_ge, AL.mult)
+    lin("s", col("p8"), col("t2"), 1.0, 8.0)
+    ts(R("Zo", 0, 144), R("XQ", 0, 144), col("c16"), None, AL.is_equal)
+    ts(BO, R("QB", 0, 128), col("pg"), None, AL.is_equal)
+    ts(R("Zs", 0, 144), R("Zo", 0, 144), 1.0 / Z, None, AL.mult)
+    ts(R("Zh", 0, 144), R("Zo", 0, 144), 2.0, None, AL.mult)
+
+    def pat(out, src, a, w):
+        ts(out, src, a, w, AL.is_equal, AL.mult)
+
+    def scaled(out, src, w, eng="v"):
+        if eng == "s":
+            act(out, src, AF.Copy, 0.0, w)
+        else:
+            ts(out, src, w, None, AL.mult)
+
+    ts(mb("Mpar"), BO, col("m0"), -1.0, AL.mult, AL.mult)
+    ts(mb("t1"), BO, 256.0, -256.0, AL.mult, AL.add)
+    tt(mb("XD"), X, mb("t1"), AL.add)
+    ts(mb("Lin"), mb("XD"), 0.0, None, AL.is_ge)
+    ts(mb("Ls2"), mb("XD"), 1.0, col("bq"), AL.is_ge, AL.mult)
+    ts(mb("t3"), mb("XD"), -0.5, 0.5, AL.max, AL.add)
+    ts(mb("M2"), mb("t3"), 1.0, None, AL.min)
+    pat(mb("D1"), X, 1.0, col("nl15"))
+    tt(mb("t2"), I, mb("D1"), AL.subtract)
+    scaled(mb("Mf2"), mb("t2"), 0.5)
+    scaled(mb("GN"), mb("t2"), 0.5 * QSUM, "s")
+    scaled(mb("NI"), I, -1.0, "s")
+    ts(mb("RZ"), BO, col("m15"), Z, AL.mult, AL.mult)
+    ts(mb("RU"), BO, col("m15"), -ALPHA, AL.mult, AL.mult)
+    scaled(mb("I255"), I, 255.0 / 256, "s")
+    scaled(mb("IZ"), I, -0.5 * Z, "s")
+    scaled(mb("BOb"), BO, -PBS, "s")
+    scaled(mb("BOf"), BO, -PD, "s")
+    scaled(mb("BOg"), BO, 100.0, "s")
+    pat(mh("Sw"), X, col("p8"), 1.0)
+    pat(mb("t4"), X, col("p8"), -16 * 1152.0 * PBS)
+    scaled(mb("t5"), I, col("cp"), "s")
+    tt(mb("Cp"), mb("t4"), mb("t5"), AL.add)
+    pat(mb("DQ"), X, col("aq"), col("wq"))
+    scaled(mb("CI"), mb("D1"), ALPHA, "s")
+    scaled(mb("GE"), mb("D1"), BETA2, "s")
+    scaled(mb("GD"), I, col("wgd"), "s")
+    scaled(mb("QD"), I, col("wqd"), "s")
+    ts(mb("t6"), mb("RU"), 0.0, None, AL.is_equal)
+    tt(mb("X15"), X, mb("t6"), AL.mult)
+    pat(mb("CD"), mb("X15"), col("nl15"), col("wcd"))
+    pat(mb("CE"), mb("X15"), col("a2"), col("wce"))
+    lin("s", mb("t7"), mb("Mpar"), 1.0, 1.0)
+    tt(mb("X0"), X, mb("t7"), AL.mult)
+    pat(mb("GI"), mb("X0"), 0.0, col("wgi"))
+    scaled(mb("T0a"), zs("Zo", 0), -ALPHA, "s")
+    scaled(mb("T0w"), zs("Zo", 0), QSUM + BETA2, "s")
+    scaled(mb("Ch"), I, col("ch"), "s")
+    pat(mb("SS"), X, col("n0"), col("wss"))
+    tt(mb("SF"), zs("Zo", 0), zs("Zo", 1), AL.add)
     ts(R("ic", 4, 5), R("inW", 0, 1), 6, None, AL.arith_shift_right)
     ts(R("ic", 5, 6), R("inW", 0, 1), 63, None, AL.bitwise_and)
     ts(col("wa"), R("ic", 4, 5), 32.0, -64.0, AL.is_ge, AL.mult)
     ts(col("whs"), R("ic", 4, 5), col("wa"), 1.0 / 64, AL.add, AL.mult)
     ts(col("wls"), R("ic", 5, 6), 1.0 / 4096, None, AL.mult)
-    act(mb("Wh"), zs("Zo", 15), AF.Copy, 0.0, col("whs"))
-    act(mb("Wl"), zs("Zo", 15), AF.Copy, 0.0, col("wls"))
-    cp(mh("U"), mb("Ub"))
-    ts(mh("DI"), mb("Mf"), -1.0, None, AL.mult)
-    act(mb("DIb"), mb("Mf"), AF.Copy, 0.0, -1.0)
-    tt(mb("IUb"), mb("I"), mb("Ub"), AL.subtract)
-    cp(mh("IU"), mb("IUb"))
-    tt(mh("T0I"), zs("Zo", 0), mb("I"), AL.subtract)
-    ts(mh("NT0"), zs("Zo", 0), -1.0, None, AL.mult)
-    tt(mh("T0M"), mh("NT0"), mb("I"), AL.subtract)
-    cp(mh("BOh"), mb("BO"))
-    ts(mh("BOc"), mb("BO"), -1.0 / 32, None, AL.mult)
-    ts(mh("BOg"), mb("BO"), -100.0, None, AL.mult)
-    ts(mh("E15"), mb("I"), col("e15"), None, AL.mult)
-    ts(mh("Sw"), X, col("p8"), None, AL.is_equal)
-    jj = R("k1", 16, 16 + nb)
-    ts(jj, R("X", 0, nb), 16.0, col("pi"), AL.mult, AL.add)
-    act(R("sm", 0, nb), jj, AF.Copy, 0.0, 16.0)
-    act(R("sm", 16, 16 + nb), jj, AF.Copy, 0.0, -1.0)
-    act(R("sm", 16 + nb, 16 + 2 * nb), jj, AF.Copy, 0.0, -1.0)
-    act(R("k1", 0, nb), jj, AF.Identity, -2048.0, -1.0)
-    ts(R("sm", 64, 72), R("X", 0, 8), col("pg"), col("a16"), AL.is_equal, AL.mult)
-    Mpar = R("Gm", 0, 128)
-    cp(R("thb", 0, 6, 1, 0, 8), R("inT", 0, 6, 1, 0, 8))
-    ts(R("IND", 0, 128, 1, 0, 8), R("QB", 0, 128, 1, 0, 8), col("p", 8), None, AL.is_equal)
-    mm(R("K7", 0, 6), R("IND", 0, 128, 1, 0, 8), R("thb", 0, 6, 1, 0, 8), True, True)
-    if cfg["clash"] == "s":
-        act(R("thc", 0, 6), R("K7", 0, 6), AF.Identity, 0.5, -1.0)
+    scaled(mb("Wh"), zs("Zo", 15), col("whs"), "s")
+    scaled(mb("Wl"), zs("Zo", 15), col("wls"), "s")
+    pat(mh("U"), X, -1.0, col("n0"))
+    cp(mh("Ih"), I)
+    cp(mh("D"), mb("D1"))
+    pat(mh("D2"), X, 2.0, col("nl14"))
+    scaled(mh("E15"), I, col("e15"))
+    scaled(mh("Rh"), I, 16 * PBS)
+    if cfg["wire"] == "nm":
+        scaled(mh("I2"), I, 2.0)
     else:
-        act(R("thc", 0, 6), R("K7", 0, 6), AF.Copy)
-    ts(col("t1"), col("n0"), -1.0, None, AL.add)
-    act(Mpar, mb("BO"), AF.Copy, 0.0, col("t1"))
-    ts(R("ownN", 0, 256), R("inO", 0, 256), -1.0, 2048.0, AL.mult, AL.add)
-    mm(R("K7", 256, 512), mh("Sw"), R("ownN", 0, 256), True, True)
-    cp(R("ownP", 0, 256), R("K7", 256, 512))
-    act_or = cp
-    act_or(R("rM", 0, 256), R("inM", 0, 256))
-    ones = R("ones", 0, n)
+        scaled(mb("I2b"), I, 2.0)
+        cp(mb("Ub"), mh("U"))
+        cp(mb("D2b"), mh("D2"))
+    scaled(mh("BO2"), BO, 2.0)
+    ts(R("k1", 0, nb), R("XQ", 0, nb), 16.0, pi, AL.mult, AL.add)
+    lin("s", R("sm", 0, nb), R("k1", 0, nb), -16.0, -16.0)
+    ts(col("t3"), pi, 6.0, col("n0"), AL.is_le, AL.mult)
+    ts(R("sm", 16, 24), R("XQ", 0, 8), col("pg"), col("t3"), AL.is_equal, AL.mult)
+    if cfg["kx"] != "-":
+        ts(R("sm", 24, 32), R("XQ", 0, 8), col("pg"), None, AL.is_equal)
+        lin("s", col("ka"), pi, 16.0, 16.0)
+        iota(R("xs", 0, 128), [[0, nc], [-256, nb], [0, 8]], 0, 0)
+        ms(R("xs", 0, 128, 1, 0, 32), 0.0)
+        ms(R("eh", 0, 48, 1, 0, 33), 0.0)
+        cp(R("eh", 16, 32, 1, 0, 16), R("mb", I[3], I[3] + 16, 1, 0, 16))
+        ms(R("eh", 16, 32, 1, 32, 33), 1.0)
+    cp(R("thb", 0, 6, 1, 0, 8), R("inT", 0, 6, 1, 0, 8))
+    ts(R("thg", 0, 128, 1, 0, 8), R("QB", 0, 128, 1, 0, 8), col("p", 8), None, AL.is_equal)
+    mm(R("K3", 0, 6), R("thg", 0, 128, 1, 0, 8), R("thb", 0, 6, 1, 0, 8), True, True)
+    if cfg["fl"][0] == "s":
+        lin("v", R("thc", 0, 6), R("K3", 0, 6), -1.0, 0.5)
+    else:
+        cp(R("thc", 0, 6), R("K3", 0, 6))
+    for c in range(nc):
+        ts(R("ow", 2 * n * c, 2 * n * c + n), R("inO", n * c, n * c + n), -2048.0, 0.5, AL.add, AL.mult)
+        mm(R("K%d" % (3 + 4 * c), 0, n), mh("Sw"), R("ow", 2 * n * c, 2 * n * c + n), True, True)
+        cp(R("ow", 2 * n * c + n, 2 * n * c + 2 * n), R("K%d" % (3 + 4 * c), 0, n))
+        ts(R("rNM", 2 * n * c, 2 * n * c + n), R("ofs", n * c, n * c + n), -2048.0, None, AL.add)
+        ts(R("rNM", 2 * n * c + n, 2 * n * c + 2 * n) if cfg["wire"] == "nm" else R("rST", 3 * n * c + 2 * n, 3 * n * c + 3 * n),
+           R("inM", n * c, n * c + n), 0.25, None, AL.mult)
 
     for v in range(V):
         last = v == V - 1
-        gp = cfg["gp"]
+        lab[1] = v
         for c in range(nc):
-            gv = cfg["gv"][c if v == 0 else 2 + c]
-            s = n // gp
+            j = c if v == 0 else 2 + c
+            s = n // cfg["gp"][j]
             lab[0] = "g%d" % c
-            for i in range(gp):
+            for i in range(cfg["gp"][j]):
                 o = v * 256 + c * n + i * s
                 out = R("G%d" % c, 16 * i * s, 16 * (i + 1) * s)
-                if gv >> i & 1:
+                if cfg["gv"][j] >> i & 1:
                     cp(out, R("win", 0, W), ind=R("ofs", o, o + s))
                 else:
                     act(out, R("win", 0, W), AF.Copy, ind=R("ofs", o, o + s))
+        if last:
+            lab[0] = "o"
+            s = W // len(cfg["dec"])
+            for i, e in enumerate(cfg["dec"]):
+                if e == "s":
+                    act(R("wout", i * s, (i + 1) * s), R("win", i * s, (i + 1) * s), AF.Relu)
+                else:
+                    ts(R("wout", i * s, (i + 1) * s), R("win", i * s, (i + 1) * s), 0.0, None, AL.max)
         for c in range(nc):
             G = "G%d" % c
-            Gw = R(G, 0, 16 * n)
-            K1, K2, K3 = "K%d" % (1 + 3 * c), "K%d" % (2 + 3 * c), "K%d" % (3 + 3 * c)
+            Gw = R(G, 0, 16 * n + 16)
 
-            def ps(ka, kb, i):
-                return R(ka, i * n, (i + 1) * n) if (i + 1) * n <= 512 else R(kb, i * n - 512, (i + 1) * n - 512)
-
-            def cut(r, i, s):
-                return R(r[0], r[3] + i * s * r[5], r[3] - r[3] % r[5] + (i + 1) * s * r[5], r[5])
+            def ps(name, w=n, o=0):
+                q = cfg["bank"].get(name, name)
+                i = int(q[1]) * n + o
+                return R("K%d" % (4 * c + "ABCD".index(q[0])), i, i + w)
 
             def h(i, k=1):
-                return R("hh", (16 * c + i) * n, (16 * c + i + k) * n)
+                return R("hh", (8 * c + i) * n, (8 * c + i + k) * n)
 
-            def b(i):
-                return R("bb", (16 * c + i) * n, (16 * c + i + 1) * n)
+            def b(i, k=1):
+                return R("bb", (16 * c + i) * n, (16 * c + i + k) * n)
 
-            def row(r, buf=G, o=0):
-                return R(buf, o + r, o + 16 * n, 16)
+            def row(r):
+                return R(G, r, 16 * n, 16)
 
-            Nh, aN, sN, FN, FMN, Qn, Qp, FM, hd, cN, cP = [h(i) for i in range(11)]
-            aM, sM, cM = b(13), b(14), b(15)
-            clash, cum, ent, cpm, z, le, gt, xk, xk1, gate, y, cpr = [b(i) for i in range(12)]
-            PB, BB = R("K0", 2 * c * n, (2 * c + 1) * n), R("K0", (2 * c + 1) * n, (2 * c + 2) * n)
-            cnt1, cnt2 = R(K1, 0, n), R(K1, n, 2 * n)
-            pre1, koff, l3p, um, pre2 = R(K2, 0, n), R(K2, n, n + nb), R(K2, n + 16, n + 16 + 3 * nb), ps(K2, "K4", 2), ps(K2, "K4", 3)
-            oh = pre1
-            ma, mf, ms, mx = [ps(K3, "K5", i) for i in range(4)]
-            midN, midM, npr = ma, mf, ms
-            pd, pg_, pt, uh = [ps("K7", "K6", i) for i in range(4)]
+            def ind(r):
+                return R("IND", (16 * c + r) * n, (16 * c + r + 1) * n)
+
+            def big(r):
+                if cfg["za"]:
+                    return R("GA", 16 * c * n + r, 16 * (c + 1) * n, 16)
+                return R("GA", (16 * c + r) * n, (16 * c + r + 1) * n)
+
+            FN, rm, Qn, Qp, hd = [h(i) for i in range(5)]
+            clash, cum, FM, gt, y, ent, gg, qq, dec, xk, zle, zgt = [b(i) for i in range(12)]
+            acc = [R("ff", (4 * c + i) * n, (4 * c + i + 1) * n) for i in range(4)]
+            PB, BB, cnt1, cnt2 = ps("A0"), ps("A1"), ps("cnt1"), ps("B1")
+            if cfg["pbs"]:
+                PB = b(14)
+            if cfg["pes"] == "v":
+                BB = xk
             o = v * 256 + c * n
-            Min = R("rM", o, o + n)
-            Sin, Tin = R("rST", 2 * o, 2 * o + n), R("rST", 2 * o + n, 2 * o + 2 * n)
-            Sout, Tout = R("sST", 2 * o, 2 * o + n), R("sST", 2 * o + n, 2 * o + 2 * n)
+            Nh, Mq = R("rNM", 2 * o, 2 * o + n), R("rNM", 2 * o + n, 2 * o + 2 * n)
+            Sin, Tin = R("rST", 3 * o, 3 * o + n), R("rST", 3 * o + n, 3 * o + 2 * n)
+            Sout, Tout = R("sST", 3 * o, 3 * o + n), R("sST", 3 * o + n, 3 * o + 2 * n)
+            mq = mh
+            if v == 0 and lq != "old":
+                Tin = R("inP", o, o + n)
+            if cfg["wire"] != "nm":
+                Mq, mq = R("rST", 3 * o + 2 * n, 3 * o + 3 * n), lambda a: mb(dict(U="Ub", Ih="I", D="D1", D2="D2b", I2="I2b")[a])
+                if v > 0:
+                    lab[0] = "f%d" % c
+                    ts(Nh, R("ofs", o, o + n), -2048.0, None, AL.add)
             P = row(0)
-            nzo = 16 * n * c
-            lab[0] = "a%d" % c
-            Pc = b(12)
             s = n // cfg["tp"]
             for i in range(cfg["tp"]):
-                if cfg["pc"] == "s":
-                    act(cut(Pc, i, s), cut(P, i, s), AF.Copy)
-                else:
-                    cp(cut(Pc, i, s), cut(P, i, s))
-                if cfg["z"] == "s":
-                    act(cut(z, i, s), cut(P, i, s), AF.Relu, 256.0, -256.0)
-                else:
-                    ts(cut(z, i, s), cut(P, i, s), 0.0, 256.0, AL.is_equal, AL.mult)
-                tt(cut(PB, i, s), cut(Pc, i, s), cut(z, i, s), AL.add)
+                lab[0] = "b%d" % c
+                act(cut(PB, i, s), cut(P, i, s), AF.Abs)
+                lab[0] = "a%d" % c
                 for r in range(1, 16):
-                    ind = cut(R("IND", nzo + r * n, nzo + (r + 1) * n), i, s)
-                    tt(ind, cut(row(r), i, s), cut(PB, i, s), AL.is_gt)
-                    mm(cut(cnt1, i, s), zs("Zo", r), ind, r == 1, v == 0 and r == 15)
-                if v > 0:
-                    mm(cut(cnt1, i, s), Mpar, cut(Sin, i, s), False, True)
-            s = 16 * n // cfg["nzp"]
-            lab[0] = "z%d" % c
-            for i in range(cfg["nzp"]):
-                if i < cfg["nzs"][c]:
-                    act(R("NZ", nzo + i * s, nzo + (i + 1) * s), R(G, i * s, (i + 1) * s), AF.Sign, 0.0, -1.0)
-                else:
-                    ts(R("NZ", nzo + i * s, nzo + (i + 1) * s), R(G, i * s, (i + 1) * s), 1.0, -1.0, AL.min, AL.mult)
-            lab[0] = "l%d" % c
-            ts(Nh, R("ofs", o, o + n), -2048.0, None, AL.add)
+                    if v > 0 and r == cfg["par"]:
+                        mm(cut(cnt1, i, s), mb("Mpar"), cut(Sin, i, s), r == 1, False)
+                    tt(cut(ind(r), i, s), cut(row(r), i, s), cut(PB, i, s), AL.is_gt)
+                    mm(cut(cnt1, i, s), zs("Zo", r), cut(ind(r), i, s), r == 1 and (v == 0 or cfg["par"] > 1), r == 15)
+            if cfg["pes"] == "t":
+                grp(ps("Pe"), [(I, P)])
+            elif cfg["pes"] == "s":
+                act(ps("Pe"), P, AF.Copy)
+            lab[0] = "c%d" % c
+            if cfg["fl"][0] == "s":
+                act(clash, cnt1, AF.Sign, R("thc", v, v + 1))
+            else:
+                ts(clash, cnt1, R("thc", v, v + 1), None, AL.is_ge)
+            grp(ps("pre"), [(mb("Lin"), clash)])
+            if cfg["fl"][1] == "s":
+                act(cum, ps("pre"), AF.Sign, col("bc"))
+            else:
+                ts(cum, ps("pre"), col("bc"), None, AL.is_ge)
             lab[0] = "d%d" % c
-            th = R("thc", v, v + 1)
-            if cfg["clash"] == "s":
-                act(clash, cnt1, AF.Sign, th)
-            else:
-                ts(clash, cnt1, th, None, AL.is_ge)
-            grp(pre1, [(mb("Lin"), clash)])
-            if cfg["cum"] == "s":
-                act(cum, pre1, AF.Sign, col("bcum"))
-            else:
-                ts(cum, pre1, col("bcum"), None, AL.is_ge)
-            grp(koff, [(mb("I"), R("sm", 0, nb))] + [(zs("Zk", a), R("bb", cum[3] + a, cum[4], 16)) for a in range(16)])
-            grp(mf, [(mb("Mf"), cum)])
-            grp(ma, [(mb("Ma"), cum)])
-            grp(ms, [(mb("R15"), cum)])
             ko = R("ko", nb * c, nb * c + nb)
-            cp(ko, koff)
-            act(xk1, Gw, AF.Relu, -1.0, ind=ko)
-            act(xk, Gw, AF.Copy, ind=ko)
-            if cfg["fused_le"]:
-                tt(le, Gw, Pc, AL.is_le, ind=ko)
+            if cfg["kx"] == "-":
+                grp(ps("ko", nb), [(I, R("sm", 0, nb))] + [(zs("Zo", a), R("bb", cum[3] + a, cum[4], 16)) for a in range(16)])
+                lin(cfg["cv"][1], ko, ps("ko", nb), -1.0)
             else:
-                tt(le, xk, Pc, AL.is_le)
-            tt(BB, xk1, le, AL.mult)
-            tt(FM, mf, Min, AL.mult)
+                kp, kq = ps("ko", 8 * nb), ps("ko", nb, 8 * nb)
+                add("t", [cum, R("sm", 24, 32)], [part(kp, 0, 16)], ("mms", [
+                    (part(cut(kp, i, 8), 0, 16), cut(cum, i, 16), R("sm", 24, 32), True, True) for i in range(nb)]))
+                xs = R("xs", 64 * c, 64 * c + 8 * nb)
+                lin(cfg["kx"], part(xs, 0, 16), part(kp, 0, 16), 1.0)
+                add("t", [part(xs, 0, 33), R("eh", 0, 48, 1, 0, 33)], [kq], ("mms", [
+                    (part(kq, 32 * (i // 2), 32 * (i // 2) + 32), R("eh", 16 - 16 * (i % 2), 48 - 16 * (i % 2), 1, 0, 33),
+                     R("xs", xs[3] + i, xs[4], 8, 0, 33), i % 2 == 0, i % 2 == 1) for i in range(8)]))
+                lin(cfg["cv"][1], ko, kq, -1.0, col("ka"))
+            if cfg["pes"] == "v":
+                far, dec = dec, b(15)
+                act(dec, Gw, AF.Relu, ind=ko)
+                tt(gt, dec, P, AL.is_le)
+                tt(BB, dec, gt, AL.mult)
+            elif cfg["aux"][0] == "g":
+                act(dec, Gw, AF.Relu, ind=ko)
+            if cfg["pes"] != "v":
+                act(xk, Gw, AF.Copy, ind=ko)
+            if cfg["pes"] == "v":
+                pass
+            elif cfg["pes"] == "f":
+                tt(gt, Gw, P, AL.is_gt, ind=ko)
+            else:
+                tt(gt, xk, ps("Pe"), AL.is_gt)
+            lab[0] = "p%d" % c
+            grp(ps("nu"), [(mb("NI"), P), (mb("RZ"), cum)])
+            lab[0] = "d%d" % c
+            if cfg["pes"] != "v":
+                grp(BB, [(mb("I255"), xk)], True, False)
+                grp(BB, [(mb("IZ"), gt)], False)
+            lab[0] = "f%d" % c
+            grp(ps("FMp"), [(mq("I2"), Mq), (mb("Mf2"), cum)])
+            if cfg["fl"][2] == "s":
+                act(FM, ps("FMp"), AF.Relu, -1.0, 2.0)
+            else:
+                ts(FM, ps("FMp"), 0.75, None, AL.is_ge)
+            grp(ps("f"), [(mb("Mf2"), cum)])
+            tt(FN, ps("f"), Nh, AL.mult)
+            lab[0] = "z%d" % c
+            zr = cfg["zr"][c]
+            for r in range(1, zr + 1, 3):
+                grp(cnt2, [(zs("Zs", i), row(i)) for i in range(r, min(r + 3, zr + 1))], r == 1, False)
+            za = cfg["za"]
+            for i in range(za if zr == 0 else 0):
+                act(R("GA", (16 * c + i * 16 // za) * n, (16 * c + (i + 1) * 16 // za) * n), R(G, i * 16 // za * n, (i + 1) * 16 // za * n), AF.Abs)
+            for r in range(zr + 1, 1 if za else 16):
+                act(big(r), row(r), AF.Abs)
+            mm(cnt2, mb("BOg"), FM, zr == 0, False)
             lab[0] = "t%d" % c
             for r in range(1, 16):
-                mm(cnt2, zs("Zo", r), row(r, "NZ", nzo), r == 1, False)
-            mm(cnt2, mh("BOg"), FM, False, False)
-            for r in range(1, 16):
-                ind = R("IND", nzo + r * n, nzo + (r + 1) * n)
-                tt(ind, row(r), BB, AL.is_gt)
-                mm(cnt2, zs("Zo", r), ind, False, r == 15)
+                lastcmp = tt(ind(r), row(r) if r <= zr else big(r), BB, AL.is_lt)
+                mm(cnt2, zs("Zo", r), ind(r), False, r == 15)
             lab[0] = "m%d" % c
-            grp(um, [(mb("Cm"), ones), (mh("BOc"), FM), (mb("BOd"), xk)])
-            rm, rh = R("ii", 2 * c * n, (2 * c + 1) * n), R("ii", (2 * c + 1) * n, (2 * c + 2) * n)
-            if cfg["rnd"] == "s":
-                rm = R("ff", c * n, c * n + n)
-                act(rm, um, AF.Identity, 3.0 * 2 ** 22)
-                act(rm, rm, AF.Identity, -3.0 * 2 ** 22)
-            else:
-                cp(rm, um)
-            tt(oh, um, rm, AL.is_equal)
-            tt(Qn, oh, R("ownN", c * n, c * n + n), AL.mult)
-            tt(Qp, oh, R("ownP", c * n, c * n + n), AL.mult)
-            mark = len(ops)
-            grp(l3p, [(mb("I"), R("sm", 16, 16 + 3 * nb))] + [(zs("Zh", a), R("hh", Qn[3] + a, FM[4], 16)) for a in range(16)])
-            t3, o3 = R("l3", 24 * c, 24 * c + nb), 24 * c + nb
-            tt(t3, cut(l3p, 2, nb), R("k1", 0, nb), AL.mult)
-            tt(R("l3", o3, o3 + nb), t3, cut(l3p, 0, nb), AL.subtract)
-            tt(R("l3", o3 + nb, o3 + 2 * nb), t3, cut(l3p, 1, nb), AL.subtract)
+            if cfg["pes"] == "v":
+                pass
+            elif cfg["aux"][0] == "s":
+                act(dec, xk, AF.Relu)
+            elif cfg["aux"][0] == "v":
+                ts(dec, xk, 0.0, None, AL.max)
+            grp(ps("um"), [(BO, dec)])
+            lin(cfg["cv"][0], rm, ps("um"), 1.0 / 16, col("cm"))
+            grp(ps("pen"), [(mb("Cp"), ones), (mb("BOb"), dec), (mb("BOf"), FM)], True, False)
+            grp(ps("pen"), [(mh("Rh"), rm)], False)
+            tt(Qn, ps("pen"), R("ow", 2 * n * c, 2 * n * c + n), AL.min)
+            tt(Qp, ps("pen"), R("ow", 2 * n * c + n, 2 * n * c + 2 * n), AL.min)
+            lab[0] = "q%d" % c
+            grp(ps("l", 2 * nb, 16), [(zs("Zh", a), R("hh", Qn[3] + a, Qp[4], 16)) for a in range(16)])
             so = R("so", 16 * c, 16 * c + 2 * nb)
-            ts(so, R("l3", o3, o3 + 2 * nb), 4096.0, None, AL.add)
+            lin(cfg["cv"][2], so, ps("l", 2 * nb, 16), 1.0, QSUM + 2048.0)
             lab[0] = "s%d" % c
-            if cfg["gt"] == "s":
-                act(gt, le, AF.Identity, 1.0, -1.0)
-            else:
-                ts(gt, le, -1.0, 1.0, AL.mult, AL.add)
-            tt(R("win", 0, W + n), xk, gt, AL.mult, sct=cut(so, 0, nb))
-            tt(R("win", 0, W + n), xk, le, AL.mult, sct=cut(so, 1, nb))
-            held = []
-            if cfg["late"] >> c & 1:
-                held = ops[mark:]
-                del ops[mark:]
-            lab[0] = "l%d" % c
-            tt(FN, mf, Nh, AL.mult)
-            tt(aN, ma, Nh, AL.mult)
-            tt(sN, ms, Nh, AL.mult)
-            for i, (dst, msk) in enumerate(((aM, ma), (sM, ms))):
-                if cfg["mk"][i] == "s":
-                    grp(mx, [(mb("I"), Min), (mb(("Ma", "R15")[i]), cum)])
-                    act(dst, mx, AF.Relu, -1.0)
+            if cfg["pes"] == "v":
+                tt(far, dec, BB, AL.subtract)
+                if not last:
+                    ts(b(10, 2), b(8, 2), 0.0, -Z, AL.is_equal, AL.mult)
+                    tt(R("win", 0, WW), b(8, 2), b(10, 2), AL.add, sct=so)
                 else:
-                    tt(dst, msk, Min, AL.mult)
-            if cfg["fmn"] == "p":
-                grp(mf, [(mh("BOh"), FM)])
-                tt(FMN, mf, FN, AL.mult)
+                    add("v", [b(8, 2), so], [R("wout", 0, WW)], ("cs", R("wout", 0, WW), b(8, 2), so))
+            elif not last:
+                lin(cfg["aux"][1], zle, gt, Z, -Z)
+                lin(cfg["aux"][2], zgt, gt, -Z)
+                tt(R("win", 0, WW), b(8, 2), b(10, 2), AL.add, sct=so)
             else:
-                tt(FMN, FM, Nh, AL.mult)
+                lin(cfg["aux"][1], zle, gt, -1.0, 1.0)
+                tt(R("wout", 0, WW), dec, gt, AL.mult, sct=cut(so, 0, nb))
+                tt(R("wout", 0, WW), dec, zle, AL.mult, sct=cut(so, 1, nb))
             lab[0] = "p%d" % c
-            if cfg["xor"] == "s":
-                grp(mx, [(mb("NI"), Sin), (zs("Zh", 0), FM), (zs("Zh", v + 1), FM)])
-                act(Sout, mx, AF.Abs)
+            if cfg["mg"][1] == "1":
+                tt(ps("Sg", n, n), Tin, ps("nu"), AL.min)
+                grp(ps("Sg"), [(mb("SS"), Sin), (mb("SF"), FM)])
+                act(R("sST", 3 * o, 3 * o + 2 * n), ps("Sg", 2 * n), AF.Abs)
             else:
-                grp(mx, [(zs("Zh", 0), FM), (zs("Zh", v + 1), FM)])
-                tt(Sout, mx, Sin, AL.not_equal)
-            if cfg["he"]:
-                lab[0] = "h%d" % c
-                grp(pt, [(mb("I"), Tin), (mb("In"), Pc)])
-                act(cpr, pt, AF.Relu)
-                grp(uh, [(mb("Ch"), ones), (mb("Wh"), Pc), (mb("Wl"), Pc), (mb("Wh"), cpr), (mb("Wl"), cpr), (mb("Big"), cum)])
-                ts(rh, uh, 2.0 ** -13, None, AL.add)
-                tt(hd, uh, rh, AL.subtract)
-                lab[0] = "p%d" % c
-            grp(pd, [(mb("I"), Pc), (mb("R15n"), cum)])
-            if cfg["gate"] == "s":
-                act(gate, pd, AF.Relu)
-            else:
-                ts(gate, pd, 0.0, None, AL.max)
-            grp(pg_, [(mb("I"), Tin), (mb("In"), gate)])
-            if cfg["y"] == "s":
-                act(y, pg_, AF.Relu)
-            else:
-                ts(y, pg_, 0.0, None, AL.max)
-            if cfg["to"] == "s":
-                grp(pt, [(mb("I"), gate), (mb("I"), y)])
-                act(Tout, pt, AF.Copy)
-            else:
-                tt(Tout, gate, y, AL.add)
+                tt(y, Tin, ps("nu"), AL.min)
+                act(Tout, y, AF.Abs)
+                grp(ps("Sg"), [(mb("SS"), Sin), (mb("SF"), FM)])
+                act(Sout, ps("Sg"), AF.Abs)
             if not last:
-                send("rS%d%d" % (v + 1, c), R("rST", 2 * (o + 256), 2 * (o + 256) + 2 * n), R("sST", 2 * o, 2 * o + 2 * n))
+                if cfg["wire"] != "2":
+                    send("rS%d%d" % (v + 1, c), R("rST", 3 * (o + 256), 3 * (o + 256) + 2 * n), R("sST", 3 * o, 3 * o + 2 * n))
             else:
-                dma("y", "oP%d" % c, R("ypic", c * n, c * n + n), Tout, 32768)
-            if not cfg["he"]:
-                grp(uh, [(mb("Ch"), ones), (mb("Wh"), Tout), (mb("Wl"), Tout), (mb("Big"), cum)])
-                ts(rh, uh, 2.0 ** -13, None, AL.add)
-                tt(hd, uh, rh, AL.subtract)
+                dma(oq[c], "oP%d" % c, R("ypic", c * n, c * n + n), Tout, 32768)
+            lab[0] = "h%d" % c
+            grp(ps("uh"), [(mb("Ch"), ones), (mb("Wh"), Tout), (mb("Wl"), Tout)])
+            rh = R("ii", c * n, c * n + n)
+            lin(cfg["rh"], rh, ps("uh"), 1.0, 2.0 ** -13)
+            tt(hd, ps("uh"), rh, AL.subtract)
             if last:
-                grp(R("K7", 0, n, 1, 0, 8), [(R("sm", 64, 72), Sout)])
-                act(R("oA", c * n, c * n + n, 1, 0, 8), R("K7", 0, n, 1, 0, 8), AF.Copy)
-                dma("y", "oA%d" % c, R("ycut", c * n, c * n + n, 1, 0, 8), R("oA", c * n, c * n + n, 1, 0, 8), 4096)
+                a8 = R(ps("Sg")[0], ps("Sg")[3], ps("Sg")[4], 1, 0, 8)
+                grp(a8, [(R("sm", 16, 24), Sout)])
+                act(R("oA", c * n, c * n + n, 1, 0, 8), a8, AF.Copy)
+                if cfg["oq"] == "old":
+                    dma("y", "oA%d" % c, R("ycut", c * n, c * n + n, 1, 0, 8), R("oA", c * n, c * n + n, 1, 0, 8), 4096)
+                elif c == nc - 1:
+                    dma(oq[2], "oA0", R("ycut", 0, 256, 1, 0, 8), R("oA", 0, 256, 1, 0, 8), 8192)
+            lab[0] = "u%d" % c
+            grp(ps("U"), [(mh("U"), Nh), (mq("U"), Mq), (mb("RU"), cum), (mh("E15"), hd)])
+            lin(cfg["ce"], acc[0], ps("U"), 1.0)
             lab[0] = "l%d" % c
-            grp(npr, [(mh("BOh"), Qp)])
-            grp(midM, [(mb("Ub"), Min), (mb("R150"), cum), (mh("T0M"), FM), (mb("DIb"), aM), (mb("IUb"), sM)])
-            terms = [(mh("U"), Nh), (mh("T0I"), FN), (mh("DI"), aN), (mh("IU"), sN), (mh("NT0"), FMN), (mh("NT0"), Qn), (mh("E15"), hd)]
-            grp(midN, terms)
-            act(aM, midM, AF.Copy)
-            if cfg["dup"] == "f":
-                act(R("ff", 256 + c * n, 256 + c * n + n), midN, AF.Copy)
-                terms = [(R("I32", 0, 128), R("ff", 256 + c * n, 256 + c * n + n))]
-            elif cfg["dup"] == "v":
-                cp(Nh, midN)
-                terms = [(mh("Ih"), Nh)]
-            grp(mx, terms, True, False)
+            grp(ps("cI"), [(mh("Ih"), Nh), (mq("Ih"), Mq), (mb("CI"), cum)], True, False)
+            grp(ps("cD"), [(mh("D"), Nh), (mq("D"), Mq), (mb("CD"), cum), (zs("Zh", 0), FN), (mb("T0a"), FM)], True, False)
+            e = grp(ps("cE"), [(mh("D2"), Nh), (mq("D2"), Mq), (mb("CE"), cum), (zs("Zh", 0), Qn), (mb("T0w"), FM)], True, False)
+            if cfg["bank"]["cE"][0] == "A" and cfg["pes"] != "v":
+                e["after"].append(lastcmp["k"])
             lab[0] = "e%d" % c
-            if cfg["ent"] == "s":
-                act(ent, cnt2, AF.Sign, -102.5, -1.0)
+            act(ent, cnt2, AF.Sign, -102.5)
+            grp(ps("gp"), [(mb("D1"), cum), (mb("M2"), ent)])
+            grp(ps("qp"), [(mb("DQ"), cum), (mb("Ls2"), ent)])
+            if cfg["mg"][0] == "1":
+                act(b(6, 2), ps("gp", 2 * n), AF.Sign, col("bg"))
             else:
-                ts(ent, cnt2, -103.0, None, AL.is_le)
-            grp(pre2, [(mb("D1"), cum), (mb("M2"), ent)])
-            if cfg["cp"] == "s":
-                act(cpr, pre2, AF.Relu, col("bcp"))
-                act(cpm, cpr, AF.Sign)
-            else:
-                ts(cpm, pre2, col("bcp"), None, AL.is_ge)
-            tt(cN, midN, cpm, AL.mult)
-            tt(cP, npr, cpm, AL.mult)
-            grp(mx, [(mh("DI"), cN), (mh("DI"), cP)], False)
-            midN = mx
+                act(gg, ps("gp"), AF.Sign, col("bg"))
+                act(qq, ps("qp"), AF.Sign, col("bg"))
+            grp(ps("cI"), [(mb("GI"), gg)], False)
+            grp(ps("cE"), [(mb("GE"), gg)], False)
+            grp(ps("cN"), [(mh("BO2"), Qp), (mb("GN"), gg)])
+            grp(ps("cD"), [(mb("GD"), gg), (mb("QD"), qq)], False)
+            tt(acc[1], acc[0], ps("cI"), AL.max)
+            tt(acc[2], acc[1], ps("cE"), AL.max)
+            tt(acc[3], acc[2], ps("cN"), AL.max)
+            tt(ps("acc"), acc[3], ps("cD"), AL.max)
+            nam = R("snd", o, o + n)
+            lin(cfg["cv"][3], nam, ps("acc"), 1.0, 2048.0)
+            Nq, Mo = R("sNM", 2 * o, 2 * o + n), R("sNM", 2 * o + n, 2 * o + 2 * n)
+            if cfg["wire"] != "nm":
+                Mo = R("sST", 3 * o + 2 * n, 3 * o + 3 * n)
             if not last:
-                ts(R("snd", o, o + n), midN, 2048.0, None, AL.add)
-                send("rN%d%d" % (v + 1, c), R("ofs", o + 256, o + 256 + n), R("snd", o, o + n))
+                send("rN%d%d" % (v + 1, c), R("ofs", o + 256, o + 256 + n), nam)
             else:
-                ts(R("oN", c * n, c * n + n), midN, 2048.0, None, AL.add)
-                dma("y", "oN%d" % c, R("ynam", c * n, c * n + n), R("oN", c * n, c * n + n), 65536)
-            ops.extend(held)
+                cp(R("oN", c * n, c * n + n), nam)
+                dma(oq[3 + c], "oN%d" % c, R("ynam", c * n, c * n + n), R("oN", c * n, c * n + n), 65536)
             lab[0] = "k%d" % c
-            if cfg["mk"][2] == "s":
-                grp(midM, [(mb("I"), aM), (mb("I"), cpm)])
-                act(cM, midM, AF.Relu, -1.0)
-            else:
-                tt(cM, midM, cpm, AL.mult)
-            grp(midM, [(mb("I"), aM), (mb("DIb"), cM)])
+            lin(cfg["cv"][4], Nq, nam, 1.0, -2048.0)
+            tt(Mo, ps("acc"), Nq, AL.subtract)
             if not last:
-                act(R("sM", o, o + n), midM, AF.Copy)
-                send("rM%d%d" % (v + 1, c), R("rM", o + 256, o + 256 + n), R("sM", o, o + n))
+                if cfg["wire"] == "nm":
+                    send("rM%d%d" % (v + 1, c), R("rNM", 2 * (o + 256), 2 * (o + 256) + 2 * n), R("sNM", 2 * o, 2 * o + 2 * n))
+                else:
+                    i = 0 if cfg["wire"] == "2" else 2 * n
+                    send("rM%d%d" % (v + 1, c), R("rST", 3 * (o + 256) + i, 3 * (o + 256) + 3 * n), R("sST", 3 * o + i, 3 * o + 3 * n))
             else:
-                act(R("oM", c * n, c * n + n), midM, AF.Copy)
-                dma("s", "oM%d" % c, R("ymrk", c * n, c * n + n), R("oM", c * n, c * n + n), 65536)
+                ts(R("oM", c * n, c * n + n), Mo, 4.0, None, AL.mult)
+                dma(oq[5 + c], "oM%d" % c, R("ymrk", c * n, c * n + n), R("oM", c * n, c * n + n), 65536)
         if last:
-            dma("y", "oD", R("ydep", 0, W), R("win", 0, W), 1 << 20)
-    for k, o in enumerate(ops):
-        o["k"] = k
-        if o["kind"] == "a":
-            o["src"] = k - 1
+            dma("y", "oD0", R("ydep", 0, W), R("wout", 0, W), 1 << 20)
     return ops
 
 
@@ -523,6 +660,47 @@ def overlap(a, b):
     if a[2] <= b[1] or b[2] <= a[1] or a[4] <= b[3] or b[4] <= a[3]:
         return False
     return True
+
+
+def depend(ops):
+    touch = {}
+    lastmm = {}
+    for o in ops:
+        deps = set(o["after"] + o["soft"])
+        for r in o["ins"]:
+            for (k, w, q) in touch.get(r[0], ()):
+                if w and overlap(r, q):
+                    deps.add(k)
+        for r in o["outs"]:
+            lst = touch.setdefault(r[0], [])
+            for (k, w, q) in lst:
+                if overlap(r, q):
+                    deps.add(k)
+            if r[5] == 1:
+                lst[:] = [e for e in lst if not (r[1] <= e[2][1] and e[2][2] <= r[2] and r[3] <= e[2][3] and e[2][4] <= r[4])]
+        for r in o["ins"]:
+            if len(r) > 1:
+                touch.setdefault(r[0], []).append((o["k"], False, r))
+        for r in o["outs"]:
+            touch[r[0]].append((o["k"], True, r))
+        if o["eng"] == "t":
+            bank = o["outs"][0][0]
+            if bank in lastmm:
+                deps.add(lastmm[bank])
+            lastmm[bank] = o["k"]
+        if o["kind"] == "a":
+            deps = {o["src"]}
+        deps.discard(o["k"])
+        o["base"] = deps
+        o["banks"] = {r[0] for r in o["ins"] + o["outs"] if is_ps(r)}
+
+
+def hop(a, b, cfg):
+    if a["k"] in b["soft"]:
+        return -a["lat"]
+    if a["eng"] == b["eng"] and a["kind"] == "c":
+        return 0.0 if a["eng"] == "t" else cfg["shop"]
+    return 0.0 if b["kind"] == "a" else cfg["hop"] + (cfg["ht"] if a["eng"] == "t" else 0.0)
 
 
 def place(ops, seq, pre, gap):
@@ -550,7 +728,7 @@ def place(ops, seq, pre, gap):
         o = ops[k]
         t = max([t0[d] + w for d, w in pre[k] if d >= 0] + [w for d, w in pre[k] if d < 0] + [0.0])
         c = o["cost"]
-        if o["kind"] != "a":
+        if c > 0.0:
             while True:
                 t1 = clear(o["eng"], None, t, c, 0.0)
                 for bk in o["banks"]:
@@ -568,14 +746,77 @@ def place(ops, seq, pre, gap):
     return t0
 
 
-def tighten(ops, base, hop, cfg):
-    fw = [[(d, ops[d]["cost"] + ops[d]["lat"] + hop(ops[d], o)) for d in base[o["k"]]] for o in ops]
+def follow(ops, key, fw, bw, cfg):
+    free = {e: 0.0 for e in "vstgyx"}
+    left = [len(o["base"]) for o in ops]
+    rt = [0.0] * len(ops)
+    t0 = [0.0] * len(ops)
+    ready = [o["k"] for o in ops if not o["base"]]
+    bank = {}
+    while ready:
+        est = {}
+        for k in ready:
+            o = ops[k]
+            t = max(rt[k], free[o["eng"]])
+            for b in o["banks"]:
+                for e, f in bank.get(b, {}).items():
+                    if e != o["eng"]:
+                        t = max(t, f + cfg["hop"])
+            est[k] = t
+        best = min(ready, key=lambda k: (est[k], -key[k]))
+        lim, e0 = est[best] + cfg["slack"], ops[best]["eng"]
+        for k in ready:
+            if ops[k]["eng"] == e0 and est[k] <= lim and key[k] > key[best]:
+                best = k
+        o = ops[best]
+        ready.remove(best)
+        t0[best] = est[best]
+        if o["cost"] > 0.0:
+            free[o["eng"]] = t0[best] + o["cost"]
+        for b in o["banks"]:
+            bank.setdefault(b, {})[o["eng"]] = t0[best] + o["cost"]
+        for s, w in bw[best]:
+            if s >= 0:
+                left[s] -= 1
+                if left[s] == 0:
+                    rt[s] = max(t0[d] + w2 for d, w2 in fw[s])
+                    ready.append(s)
+    return t0
+
+
+def arrange(ops, cfg):
+    fw = [[(d, ops[d]["cost"] + ops[d]["lat"] + hop(ops[d], o, cfg)) for d in o["base"]] for o in ops]
     bw = [[(-1, o["lat"])] for o in ops]
     for o in ops:
-        for d in base[o["k"]]:
-            bw[d].append((o["k"], o["cost"] + ops[d]["lat"] + hop(ops[d], o)))
-    t0 = [o["t0"] for o in ops]
-    best = (max(o["fin"] for o in ops), t0)
+        for d in o["base"]:
+            bw[d].append((o["k"], o["cost"] + ops[d]["lat"] + hop(ops[d], o, cfg)))
+    pri = [0.0] * len(ops)
+    nxt = {}
+    for o in reversed(ops):
+        pri[o["k"]] = o["cost"] + max(pri[s] - ops[s]["cost"] + w if s >= 0 else w for s, w in bw[o["k"]])
+        if o["lab"][0] in cfg["runs"]:
+            run = (o["eng"], o["lab"], o["v"])
+            pri[o["k"]] = max(pri[o["k"]], o["cost"] + nxt.get(run, 0.0))
+            nxt[run] = pri[o["k"]]
+    key = [pri[o["k"]] + cfg["off"].get(o["lab"], 0.0) for o in ops]
+    if cfg["period"]:
+        prev = {}
+        for o in ops:
+            t = max([cfg["off"].get(o["lab"], 0.0) + cfg["period"] * o["v"] if o["v"] >= 0 else cfg["off"].get(o["lab"], 0.0)] +
+                    [w - key[d] for d, w in fw[o["k"]] if ops[d]["v"] == o["v"]])
+            if o["lab"][0] in cfg["runs"]:
+                run = (o["eng"], o["lab"], o["v"])
+                t = max(t, prev.get(run, t))
+                prev[run] = t + o["cost"]
+            key[o["k"]] = -t
+    if cfg["slack"] < 0:
+        for o in ops:
+            for d in o["base"]:
+                key[o["k"]] = min(key[o["k"]], key[d])
+        t0 = place(ops, sorted(range(len(ops)), key=lambda k: (-key[k], k)), fw, cfg["hop"])
+    else:
+        t0 = follow(ops, key, fw, bw, cfg)
+    best = (max(t0[o["k"]] + o["cost"] + o["lat"] for o in ops), t0)
     for _ in range(cfg["fbi"]):
         u = place(ops, sorted(range(len(ops)), key=lambda k: (-(t0[k] + ops[k]["cost"]), -k)), bw, cfg["hop"])
         t0 = place(ops, sorted(range(len(ops)), key=lambda k: (-(u[k] + ops[k]["cost"]), k)), fw, cfg["hop"])
@@ -587,7 +828,7 @@ def tighten(ops, base, hop, cfg):
     for o in order:
         o["t0"] = best[1][o["k"]]
         o["fin"] = o["t0"] + o["cost"] + o["lat"]
-        o["deps"] = set(base[o["k"]])
+        o["deps"] = set(o["base"])
         for k in o["banks"]:
             for e, q in bank.get(k, {}).items():
                 if e != o["eng"]:
@@ -598,93 +839,8 @@ def tighten(ops, base, hop, cfg):
 
 def schedule(cfg):
     ops = build(cfg)
-    touch = {}
-    lastmm = {}
-    for o in ops:
-        deps = set()
-        for r in o["ins"]:
-            for (k, w, q) in touch.get(r[0], ()):
-                if w and overlap(r, q):
-                    deps.add(k)
-        for r in o["outs"]:
-            lst = touch.setdefault(r[0], [])
-            for (k, w, q) in lst:
-                if overlap(r, q):
-                    deps.add(k)
-            if r[5] == 1:
-                lst[:] = [e for e in lst if not (r[1] <= e[2][1] and e[2][2] <= r[2] and r[3] <= e[2][3] and e[2][4] <= r[4])]
-        for r in o["ins"]:
-            if len(r) > 1:
-                touch.setdefault(r[0], []).append((o["k"], False, r))
-        for r in o["outs"]:
-            touch[r[0]].append((o["k"], True, r))
-        if o["eng"] == "t":
-            bank = o["outs"][0][0]
-            if bank in lastmm:
-                deps.add(lastmm[bank])
-            lastmm[bank] = o["k"]
-        if o["kind"] == "a":
-            deps = {o["src"]}
-        deps.discard(o["k"])
-        o["deps"] = deps
-        o["banks"] = {r[0] for r in o["ins"] + o["outs"] if is_ps(r)}
-    succ = [[] for _ in ops]
-    for o in ops:
-        for d in o["deps"]:
-            succ[d].append(o["k"])
-    base = [set(o["deps"]) for o in ops]
-
-    def hop(a, b):
-        if a["eng"] == b["eng"] and a["kind"] == "c":
-            return 0.0 if a["eng"] == "t" else cfg["shop"]
-        return 0.0 if b["kind"] == "a" else cfg["hop"]
-
-    for o in reversed(ops):
-        o["pri"] = o["cost"] + o["lat"] + max([hop(o, ops[s]) + ops[s]["pri"] for s in succ[o["k"]]] + [0.0])
-    for o in ops:
-        o["pri"] += cfg["off"].get(o["lab"], 0.0)
-    free = {e: 0.0 for e in "vstgyx"}
-    left = [len(o["deps"]) for o in ops]
-    ready = [o for o in ops if not o["deps"]]
-    for o in ready:
-        o["rt"] = 0.0
-    bank = {}
-    order = []
-    while ready:
-        best = None
-        for o in ready:
-            t = max(o["rt"], free[o["eng"]]) if o["kind"] != "a" else o["rt"]
-            for k in o["banks"]:
-                for e, q in bank.get(k, {}).items():
-                    if e != o["eng"]:
-                        t = max(t, q["fin"] + cfg["hop"])
-            o["est"] = t
-            if best is None or t < best["est"]:
-                best = o
-        t0, e0 = best["est"], best["eng"]
-        for o in ready:
-            if o["eng"] == e0 and o["est"] <= t0 + cfg["slack"] and o["pri"] > best["pri"]:
-                best = o
-        o = best
-        ready.remove(o)
-        for k in o["banks"]:
-            for e, q in bank.get(k, {}).items():
-                if e != o["eng"]:
-                    o["deps"].add(q["k"])
-            bank.setdefault(k, {})[o["eng"]] = o
-        o["t0"] = o["est"]
-        if o["kind"] != "a":
-            free[o["eng"]] = o["t0"] + o["cost"]
-        o["fin"] = o["t0"] + o["cost"] + o["lat"]
-        order.append(o)
-        for s in succ[o["k"]]:
-            left[s] -= 1
-            if left[s] == 0:
-                q = ops[s]
-                q["rt"] = max(ops[d]["fin"] + hop(ops[d], q) for d in q["deps"])
-                ready.append(q)
-    if cfg["fbi"]:
-        order = tighten(ops, base, hop, cfg)
+    depend(ops)
+    order = arrange(ops, cfg)
     cnt = {e: 0 for e in "vstg"}
     known = {e: {} for e in "vstgy"}
     for o in order:
@@ -695,7 +851,7 @@ def schedule(cfg):
         waits = {}
         for d in sorted(o["deps"], key=lambda d: -ops[d]["fin"]):
             q = ops[d]
-            if q["kind"] == "r" or (e == "t" and q["eng"] == "t"):
+            if q["kind"] == "r" or (e == "t" and q["eng"] == "t") or d in o["soft"]:
                 continue
             s, val = q["sig"]
             if known[e].get(s, 0) >= val:
@@ -756,6 +912,8 @@ def rank_program(g, core, T, topo):
                 i = q.tensor_scalar(A(c[1]), A(c[2], c[7]), A(c[3]), A(c[4]), c[5], c[6])
         elif c[0] == "tt":
             i = q.tensor_tensor(A(c[1], c[6]), A(c[2], c[5]), A(c[3]), c[4])
+        elif c[0] == "cs":
+            i = q.tensor_copy(A(c[1], c[3]), A(c[2]))
         elif c[0] == "cp":
             i = q.tensor_copy(A(c[1]), A(c[2], c[3]))
         elif c[0] == "act":
@@ -764,7 +922,11 @@ def rank_program(g, core, T, topo):
             else:
                 i = q.activation(A(c[1]), A(c[2], c[6]), c[3], bias=A(c[4]), scale=A(c[5]))
         elif c[0] == "mm":
-            i = q.matmul(A(c[1]), A(c[2]), A(c[3]), c[4], c[5])
+            for j, (l, r) in enumerate(c[2]):
+                i = q.matmul(A(c[1]), A(l), A(r), c[3] and j == 0, c[4] and j == len(c[2]) - 1)
+        elif c[0] == "mms":
+            for m in c[1]:
+                i = q.matmul(A(m[0]), A(m[1]), A(m[2]), m[3], m[4])
         elif c[0] == "ms":
             i = q.memset(A(c[1]), c[2])
         elif c[0] == "iota":

@@ -15,7 +15,7 @@ QSUM = 522240.0
 ALPHA, BETA, BETA2 = 10240.0, 3072.0, 6144.0
 
 CFG = dict(
-    gp=(4, 4, 4, 4), gv=(10, 0, 2, 4), tp=2, enc="bbcbbbcb", dec="ssss", aux="sss", ndep=4, zr=(15, 15), pes="t", runs="gatw", period=0, cv="svvvv", kx="-", fl="sss", mg="11", ce="s", wire="nm", par=1, lq="old", oq="old", di=60.0, rf=0.0, rb=0.0, t2=2.0, ht=0.0, za=0, rh="v", pbs=0, mv=64.0,
+    gp=(4, 4, 4, 4), gv=(10, 0, 2, 4), tp=2, enc="bbcbbbcb", dec="ssss", aux="sss", ndep=4, zr=(15, 15), pes="t", runs="gatw", period=0, cv="svvvv", kx="-", fl="sss", mg="11", ce="s", wire="nm", par=1, lq="old", oq="old", di=60.0, rf=0.0, rb=0.0, t2=2.0, ht=0.0, za=0, rh="v", pbs=0, mv=64.0, fin="", cs="v",
     cy=0.83, gam=1.56, sig=3.8, pe=0.5, fs=90.0, hop=110.0, shop=40.0, rissue=600.0, rlat=1800.0, dlat=1500.0, dbw=200.0,
     slack=80.0, fbi=1, off={},
     bank=dict(cnt1="C1", Pe="D1", FMp="C1", f="C2", um="C0", pen="C1", l="C3", ko="C3", pre="C0", uh="D0", Sg="D1", U="D2",
@@ -34,6 +34,7 @@ CFG.update({'gp': (4, 4, 4, 4), 'gv': (5, 0, 3, 0), 'tp': 2, 'enc': 'babbabba', 
 CFG.update(pbs=1)
 CFG.update(dict(hop=120.0, shop=120.0, ht=130.0, fs=20.0, rlat=2050.0, pe=0.49, rissue=400.0, gam=1.6, sig=3.6, cy=0.84, dbw=220.0, dlat=400.0, di=60.0, mv=85.0))
 CFG.update({'gp': (4, 4, 4, 4), 'gv': (10, 2, 10, 8), 'tp': 1, 'enc': 'babbabba', 'dec': 'vsss', 'pes': 'v', 'period': 15500, 'cv': 'ssssv', 'fl': 'vss', 'mg': '11', 'ce': 's', 'wire': 'nm', 'par': 1, 'slack': 0, 'fbi': 1, 'off': {'g0': 200.0, 'b0': 700.0, 'a0': -2100.0, 'z0': 1200.0, 'c0': 700.0, 'd0': 1700.0, 'f0': 5000.0, 'p0': 5500.0, 't0': 4700.0, 'm0': 2100.0, 'q0': 7300.0, 's0': 11200.0, 'h0': 4600.0, 'u0': 6300.0, 'l0': 5200.0, 'e0': 7600.0, 'k0': 10900.0, 'g1': 5900.0, 'b1': 5500.0, 'a1': 7700.0, 'z1': 7600.0, 'c1': 6100.0, 'd1': 10000.0, 'f1': 9800.0, 'p1': 11200.0, 't1': 12400.0, 'm1': 9300.0, 'q1': 10200.0, 's1': 17000.0, 'h1': 9300.0, 'u1': 8400.0, 'l1': 11600.0, 'e1': 12000.0, 'k1': 11200.0, '0': -4700.0, 'w': -9400.0, 'n': -13500.0, 'o': 9000.0}, 'bank': {'cnt1': 'C1', 'Pe': 'D1', 'FMp': 'C1', 'f': 'C2', 'um': 'A0', 'pen': 'C1', 'l': 'C3', 'ko': 'C3', 'pre': 'C0', 'uh': 'D0', 'Sg': 'D1', 'U': 'A1', 'cI': 'C2', 'cD': 'D3', 'cE': 'A2', 'cN': 'B0', 'acc': 'C0', 'nu': 'A3', 'gp': 'B2', 'qp': 'B3'}})
+CFG.update({'gp': (4, 4, 4, 8), 'gv': (3, 2, 5, 3), 'enc': 'babbabba', 'dec': 'ssvs', 'aux': 'pss', 'ndep': 8, 'zr': (15, 0), 'period': 16000, 'cv': 'svssv', 'fl': 'sss', 'mg': '01', 'wire': 'nm', 'par': 1, 'lq': 'ysysysysysyyyy', 'za': 4, 'rh': 's', 'fin': 's', 'cs': 's', 'slack': 0, 'fbi': 2, 'off': {'g0': 1000.0, 'b0': 1400.0, 'a0': -8300.0, 'z0': 2000.0, 'c0': 3500.0, 'd0': 3600.0, 'f0': 7100.0, 'p0': -3400.0, 't0': 6600.0, 'm0': 3500.0, 'q0': 6000.0, 's0': 5800.0, 'h0': 7500.0, 'u0': 300.0, 'l0': 4500.0, 'e0': 500.0, 'k0': 15400.0, 'g1': 6000.0, 'b1': 3900.0, 'a1': 9700.0, 'z1': 6700.0, 'c1': 6100.0, 'd1': 9400.0, 'f1': 14400.0, 'p1': 12300.0, 't1': 9600.0, 'm1': 9800.0, 'q1': 6100.0, 's1': 15600.0, 'h1': 10300.0, 'u1': 9600.0, 'l1': 10800.0, 'e1': 9700.0, 'k1': 14100.0, '0': -4000.0, 'w': -6900.0, 'n': -12100.0, 'o': 11400.0}, 'bank': {'cnt1': 'C1', 'Pe': 'D1', 'FMp': 'C1', 'f': 'A1', 'um': 'A0', 'pen': 'C1', 'l': 'C3', 'ko': 'D3', 'pre': 'C0', 'uh': 'A0', 'Sg': 'D1', 'U': 'A1', 'cI': 'C2', 'cD': 'D3', 'cE': 'A2', 'cN': 'B0', 'acc': 'A0', 'nu': 'A3', 'gp': 'B2', 'qp': 'B3'}})
 
 MATS_BF = ["I", "NI", "BO", "Mpar", "Lin", "Mf2", "RZ", "I255", "IZ", "BOb", "BOf", "Cp", "BOg", "D1", "M2", "Ls2", "DQ",
            "RU", "CI", "CD", "CE", "GI", "GE", "GD", "QD", "GN", "T0a", "T0w", "Wh", "Wl", "Ch", "SS", "SF",
@@ -297,7 +298,7 @@ def build(cfg):
         ts(out, src, a, w, AL.is_equal, AL.mult)
 
     def scaled(out, src, w, eng="v"):
-        if eng == "s":
+        if eng == "s" or cfg["cs"] == "s":
             act(out, src, AF.Copy, 0.0, w)
         else:
             ts(out, src, w, None, AL.mult)
@@ -316,8 +317,9 @@ def build(cfg):
     scaled(mb("NI"), I, -1.0, "s")
     ts(mb("RZ"), BO, col("m15"), Z, AL.mult, AL.mult)
     ts(mb("RU"), BO, col("m15"), -ALPHA, AL.mult, AL.mult)
-    scaled(mb("I255"), I, 255.0 / 256, "s")
-    scaled(mb("IZ"), I, -0.5 * Z, "s")
+    if not cfg["fin"]:
+        scaled(mb("I255"), I, 255.0 / 256, "s")
+        scaled(mb("IZ"), I, -0.5 * Z, "s")
     scaled(mb("BOb"), BO, -PBS, "s")
     scaled(mb("BOf"), BO, -PD, "s")
     scaled(mb("BOg"), BO, 100.0, "s")
@@ -498,9 +500,16 @@ def build(cfg):
                      R("xs", xs[3] + i, xs[4], 8, 0, 33), i % 2 == 0, i % 2 == 1) for i in range(8)]))
                 lin(cfg["cv"][1], ko, kq, -1.0, col("ka"))
             if cfg["pes"] == "v":
-                far, dec = dec, b(15)
-                act(dec, Gw, AF.Relu, ind=ko)
-                tt(gt, dec, P, AL.is_le)
+                if cfg["aux"][0] == "p" and not last:
+                    lab[0] = "b%d" % c
+                    act(b(15), P, AF.Relu)
+                    lab[0] = "d%d" % c
+                    act(dec, Gw, AF.Relu, ind=ko)
+                    tt(gt, dec, b(15), AL.is_le)
+                else:
+                    far, dec = dec, b(15)
+                    act(dec, Gw, AF.Relu, ind=ko)
+                    tt(gt, dec, P, AL.is_le)
                 tt(BB, dec, gt, AL.mult)
             elif cfg["aux"][0] == "g":
                 act(dec, Gw, AF.Relu, ind=ko)
@@ -558,7 +567,11 @@ def build(cfg):
             so = R("so", 16 * c, 16 * c + 2 * nb)
             lin(cfg["cv"][2], so, ps("l", 2 * nb, 16), 1.0, QSUM + 2048.0)
             lab[0] = "s%d" % c
-            if cfg["pes"] == "v":
+            if cfg["pes"] == "v" and cfg["aux"][0] == "p" and not last:
+                lin(cfg["aux"][1], zle, gt, -Z)
+                ts(zgt, BB, 0.0, -Z, AL.is_equal, AL.mult)
+                tt(R("win", 0, WW), b(8, 2), b(10, 2), AL.add, sct=so)
+            elif cfg["pes"] == "v":
                 tt(far, dec, BB, AL.subtract)
                 if not last:
                     ts(b(10, 2), b(8, 2), 0.0, -Z, AL.is_equal, AL.mult)
@@ -627,6 +640,14 @@ def build(cfg):
             tt(acc[2], acc[1], ps("cE"), AL.max)
             tt(acc[3], acc[2], ps("cN"), AL.max)
             tt(ps("acc"), acc[3], ps("cD"), AL.max)
+            if last and cfg["fin"]:
+                oN, oM = R("oN", c * n, c * n + n), R("oM", c * n, c * n + n)
+                ts(oN, ps("acc"), 3.0 * 2 ** 22, 2048.0 - 3.0 * 2 ** 22, AL.add, AL.add)
+                dma(oq[3 + c], "oN%d" % c, R("ynam", c * n, c * n + n), oN, 65536)
+                tt(acc[0], ps("acc"), oN, AL.subtract)
+                lin(cfg["fin"], oM, acc[0], 4.0, 8192.0)
+                dma(oq[5 + c], "oM%d" % c, R("ymrk", c * n, c * n + n), oM, 65536)
+                continue
             nam = R("snd", o, o + n)
             lin(cfg["cv"][3], nam, ps("acc"), 1.0, 2048.0)
             Nq, Mo = R("sNM", 2 * o, 2 * o + n), R("sNM", 2 * o + n, 2 * o + 2 * n)
@@ -802,7 +823,8 @@ def arrange(ops, cfg):
     if cfg["period"]:
         prev = {}
         for o in ops:
-            t = max([cfg["off"].get(o["lab"], 0.0) + cfg["period"] * o["v"] if o["v"] >= 0 else cfg["off"].get(o["lab"], 0.0)] +
+            own = cfg["off"].get({0: "X", V - 1: "Y"}.get(o["v"], "-") + o["lab"], 0.0)
+            t = max([cfg["off"].get(o["lab"], 0.0) + own + cfg["period"] * max(o["v"], 0)] +
                     [w - key[d] for d, w in fw[o["k"]] if ops[d]["v"] == o["v"]])
             if o["lab"][0] in cfg["runs"]:
                 run = (o["eng"], o["lab"], o["v"])

from concourse.bass import DstId, RemoteDMATransfer
from concourse.mybir import dt, AluOpType, AxisListType, ActivationFunctionType

AL = AluOpType
AF = ActivationFunctionType
V = 6
W = 4096
NS = 128
NB = NS // 16
F32, BF, F16, I32, U16 = "float32", "bfloat16", "float16", "int32", "uint16"
Z = 2.0 ** 18
WW = W + 7680
PA, PBS, PD = 1280.0, 2304.0, 256.0
QSUM = 522240.0
ALPHA, BETA, BETA2 = 10240.0, 3072.0, 6144.0

CFG = dict(
    gp=(4, 4, 4, 4), gv=(10, 0, 2, 4), tp=2, enc="bbcbbbcb", dec="ssss", aux="sss", ndep=4, zr=(15, 15), pes="t", runs="gatw", period=0, cv="svvvv", kx="-", fl="sss", mg="11", ce="s", wire="nm", par=1, lq="old", oq="old", di=60.0, rf=0.0, rb=0.0, t2=2.0, ht=0.0, za=0, rh="v", pbs=0, mv=64.0, fin="", cs="v",
    cy=0.83, gam=1.56, sig=3.8, pe=0.5, fs=90.0, hop=110.0, shop=40.0, rissue=600.0, rlat=1800.0, dlat=1500.0, dbw=200.0,
    slack=80.0, fbi=1, off={},
    bank=dict(cnt1="C1", Pe="D1", FMp="C1", f="C2", um="C0", pen="C1", l="C3", ko="C3", pre="C0", uh="D0", Sg="D1", U="D2",
              cI="C2", cD="D3", cE="A2", cN="B0", acc="D0", nu="A3", gp="B2", qp="B3"),
)

CFG.update({'gp': (4, 4, 4, 4), 'gv': (5, 5, 10, 5), 'tp': 2, 'enc': 'bbcbbcab', 'dec': 'ssss', 'aux': 'sss', 'ndep': 4, 'zr': (15, 0), 'pes': 't', 'runs': 'gatwz', 'period': 15000, 'cv': 'ssssv', 'kx': 'v', 'slack': -1, 'fbi': 2, 'off': {'g0': -1000.0, 'b0': 800.0, 'a0': 300.0, 'z0': 400.0, 'c0': -4300.0, 'd0': -4700.0, 'f0': 3900.0, 'p0': -4000.0, 't0': 5300.0, 'm0': 3900.0, 'q0': 400.0, 's0': -100.0, 'h0': 5700.0, 'u0': 6100.0, 'l0': -2800.0, 'e0': 7300.0, 'k0': 5700.0, 'g1': 2600.0, 'b1': -500.0, 'a1': 500.0, 'z1': 5000.0, 'c1': 4000.0, 'd1': 3000.0, 'f1': 8500.0, 'p1': 5000.0, 't1': -300.0, 'm1': 7700.0, 'q1': -1000.0, 's1': 9600.0, 'h1': 5600.0, 'u1': 6000.0, 'l1': 12300.0, 'e1': -7900.0, 'k1': -1000.0, '0': -6400.0, 'w': -20400.0, 'n': -10900.0, 'o': 5400.0}})
CFG.update({'gp': (4, 4, 4, 4), 'gv': (9, 2, 2, 1), 'tp': 1, 'enc': 'bbcbbcab', 'dec': 'ssss', 'aux': 'ssv', 'ndep': 4, 'zr': (15, 15), 'pes': 's', 'runs': 'gatwz', 'period': 16000, 'cv': 'ssvvv', 'kx': 'v', 'fl': 'vvs', 'mg': '11', 'ce': 's', 'fs': 90.0, 'slack': -1, 'fbi': 1, 'off': {'g0': -800.0, 'b0': 1300.0, 'a0': -1000.0, 'z0': -4700.0, 'c0': -6600.0, 'd0': -2100.0, 'f0': 5800.0, 'p0': -1500.0, 't0': 4600.0, 'm0': 3800.0, 'q0': -3800.0, 's0': 700.0, 'h0': 3000.0, 'u0': 4200.0, 'l0': -1000.0, 'e0': 7600.0, 'k0': 3000.0, 'g1': 2600.0, 'b1': 1800.0, 'a1': -2100.0, 'z1': 700.0, 'c1': 6300.0, 'd1': 7400.0, 'f1': 8600.0, 'p1': 4800.0, 't1': -1200.0, 'm1': 6700.0, 'q1': -500.0, 's1': 1400.0, 'h1': 2000.0, 'u1': 6300.0, 'l1': 9900.0, 'e1': -12500.0, 'k1': 4000.0, '0': -14700.0, 'w': -19400.0, 'n': -9200.0, 'o': 5400.0}})
CFG.update(dict(pe=0.44, hop=120.0, shop=100.0, rissue=600.0, rlat=1200.0, fs=50.0, rf=600.0, rb=4.0, di=900.0, dbw=200.0))
CFG.update({'gp': (4, 4, 4, 4), 'gv': (3, 2, 2, 1), 'tp': 2, 'enc': 'bbcbbcab', 'dec': 'ssss', 'aux': 'vss', 'ndep': 2, 'zr': (15, 15), 'pes': 't', 'runs': 'gatwz', 'period': 16000, 'cv': 'ssvvv', 'kx': 'v', 'fl': 'vvs', 'mg': '11', 'ce': 's', 'wire': '2', 'par': 15, 'lq': 'ysyggggg', 'oq': 'gggsyyg', 'di': 900.0, 'rf': 600.0, 'rb': 4.0, 'fs': 50.0, 'slack': -1, 'fbi': 1, 'off': {'g0': -1600.0, 'b0': 1500.0, 'a0': -1200.0, 'z0': -2600.0, 'c0': -4600.0, 'd0': -4500.0, 'f0': 6100.0, 'p0': -3600.0, 't0': 5500.0, 'm0': 2000.0, 'q0': -6100.0, 's0': -1100.0, 'h0': 2900.0, 'u0': 3400.0, 'l0': -4900.0, 'e0': 5800.0, 'k0': 6200.0, 'g1': 2600.0, 'b1': 4000.0, 'a1': -6000.0, 'z1': -400.0, 'c1': -2600.0, 'd1': 6800.0, 'f1': 9100.0, 'p1': 6300.0, 't1': -1600.0, 'm1': 7000.0, 'q1': -5200.0, 's1': 1100.0, 'h1': 4700.0, 'u1': 6000.0, 'l1': 8500.0, 'e1': -17600.0, 'k1': 5400.0, '0': -11800.0, 'w': -18100.0, 'n': -7900.0, 'o': 6800.0}})
CFG.update(dict(pe=0.44, hop=160.0, shop=160.0, rissue=500.0, rlat=2900.0, fs=70.0, rf=0.0, rb=2.0, di=60.0, dbw=400.0, gam=1.38, sig=2.8, t2=1.0, kx="-"))
CFG.update({'gp': (4, 4, 4, 4), 'gv': (10, 2, 3, 1), 'tp': 1, 'aux': 'gss', 'pes': 's', 'period': 17000, 'cv': 'sssvv', 'fl': 'vvs', 'mg': '01', 'ce': 's', 'wire': '3', 'par': 8, 'slack': 40, 'fbi': 1, 'off': {'g0': -5000.0, 'b0': 2200.0, 'a0': -1500.0, 'z0': -1600.0, 'c0': -4100.0, 'd0': -5400.0, 'f0': 4800.0, 'p0': -3200.0, 't0': 7000.0, 'm0': 2600.0, 'q0': -8400.0, 's0': -3300.0, 'h0': 4600.0, 'u0': 4100.0, 'l0': -6600.0, 'e0': 4900.0, 'k0': 9200.0, 'g1': 3100.0, 'b1': 4800.0, 'a1': -1000.0, 'z1': 1500.0, 'c1': -4900.0, 'd1': 700.0, 'f1': 8000.0, 'p1': 7300.0, 't1': 2900.0, 'm1': 7000.0, 'q1': -6500.0, 's1': 6100.0, 'h1': 4200.0, 'u1': 4300.0, 'l1': 6000.0, 'e1': -24400.0, 'k1': 5400.0, '0': -9700.0, 'w': -17800.0, 'n': -6400.0, 'o': 4400.0}})
CFG.update({'lq': 'ysysyyyy', 'oq': 'yyysyys', 'di': 200.0, 'dbw': 330.0, 'gv': (9, 2, 3, 4), 'fbi': 2, 'off': {'g0': -4200.0, 'b0': 2200.0, 'a0': -4300.0, 'z0': -4900.0, 'c0': 1000.0, 'd0': -300.0, 'f0': 4300.0, 'p0': -5900.0, 't0': 5600.0, 'm0': 5600.0, 'q0': -11500.0, 's0': -2500.0, 'h0': -1900.0, 'u0': 2800.0, 'l0': -1900.0, 'e0': -1200.0, 'k0': 8000.0, 'g1': 3100.0, 'b1': 3600.0, 'a1': -3400.0, 'z1': 2000.0, 'c1': -5400.0, 'd1': 1700.0, 'f1': 7500.0, 'p1': 3800.0, 't1': 1900.0, 'm1': 9100.0, 'q1': -7000.0, 's1': 5700.0, 'h1': 4400.0, 'u1': 2700.0, 'l1': 7900.0, 'e1': -23700.0, 'k1': 3000.0, '0': -8200.0, 'w': -14900.0, 'n': -9600.0, 'o': 9300.0}})
CFG.update(dict(hop=90.0, shop=100.0, ht=50.0, fs=66.0, rlat=3000.0, pe=0.46, rissue=650.0, gam=1.22, sig=2.0, cy=0.96, dbw=200.0, dlat=400.0, di=60.0))
CFG.update({'gp': (4, 4, 4, 4), 'gv': (5, 0, 3, 0), 'tp': 2, 'enc': 'babbabba', 'aux': 'vvs', 'ndep': 4, 'zr': (15, 15), 'pes': 't', 'period': 16000, 'cv': 'svsvv', 'fl': 'vvs', 'mg': '11', 'ce': 's', 'wire': '3', 'par': 1, 'lq': 'ysysysyyyy', 'za': 2, 'slack': 0, 'fbi': 1, 'off': {'g0': 0.0, 'b0': -2900.0, 'a0': 2400.0, 'z0': 300.0, 'c0': -1000.0, 'd0': -2100.0, 'f0': 4700.0, 'p0': 5200.0, 't0': 4900.0, 'm0': 4100.0, 'q0': 4200.0, 's0': 11300.0, 'h0': 7100.0, 'u0': 9800.0, 'l0': 3800.0, 'e0': 5600.0, 'k0': 11700.0, 'g1': 6000, 'b1': 7900.0, 'a1': 6200.0, 'z1': 11100.0, 'c1': 10200.0, 'd1': 11500.0, 'f1': 10800.0, 'p1': 10200.0, 't1': 10700.0, 'm1': 12800.0, 'q1': 13700.0, 's1': 19100.0, 'h1': 13800.0, 'u1': 8400.0, 'l1': 11700.0, 'e1': 15100.0, 'k1': 13000.0, '0': -4600.0, 'w': -14100.0, 'n': -18700.0, 'o': 6600.0}})
CFG.update(pbs=1)
CFG.update(dict(hop=120.0, shop=120.0, ht=130.0, fs=20.0, rlat=2050.0, pe=0.49, rissue=400.0, gam=1.6, sig=3.6, cy=0.84, dbw=220.0, dlat=400.0, di=60.0, mv=85.0))
CFG.update({'gp': (4, 4, 4, 4), 'gv': (10, 2, 10, 8), 'tp': 1, 'enc': 'babbabba', 'dec': 'vsss', 'pes': 'v', 'period': 15500, 'cv': 'ssssv', 'fl': 'vss', 'mg': '11', 'ce': 's', 'wire': 'nm', 'par': 1, 'slack': 0, 'fbi': 1, 'off': {'g0': 200.0, 'b0': 700.0, 'a0': -2100.0, 'z0': 1200.0, 'c0': 700.0, 'd0': 1700.0, 'f0': 5000.0, 'p0': 5500.0, 't0': 4700.0, 'm0': 2100.0, 'q0': 7300.0, 's0': 11200.0, 'h0': 4600.0, 'u0': 6300.0, 'l0': 5200.0, 'e0': 7600.0, 'k0': 10900.0, 'g1': 5900.0, 'b1': 5500.0, 'a1': 7700.0, 'z1': 7600.0, 'c1': 6100.0, 'd1': 10000.0, 'f1': 9800.0, 'p1': 11200.0, 't1': 12400.0, 'm1': 9300.0, 'q1': 10200.0, 's1': 17000.0, 'h1': 9300.0, 'u1': 8400.0, 'l1': 11600.0, 'e1': 12000.0, 'k1': 11200.0, '0': -4700.0, 'w': -9400.0, 'n': -13500.0, 'o': 9000.0}, 'bank': {'cnt1': 'C1', 'Pe': 'D1', 'FMp': 'C1', 'f': 'C2', 'um': 'A0', 'pen': 'C1', 'l': 'C3', 'ko': 'C3', 'pre': 'C0', 'uh': 'D0', 'Sg': 'D1', 'U': 'A1', 'cI': 'C2', 'cD': 'D3', 'cE': 'A2', 'cN': 'B0', 'acc': 'C0', 'nu': 'A3', 'gp': 'B2', 'qp': 'B3'}})
CFG.update({'gp': (4, 4, 4, 8), 'gv': (3, 2, 5, 3), 'enc': 'babbabba', 'dec': 'ssvs', 'aux': 'pss', 'ndep': 8, 'zr': (15, 0), 'period': 16000, 'cv': 'svssv', 'fl': 'sss', 'mg': '01', 'wire': 'nm', 'par': 1, 'lq': 'ysysysysysyyyy', 'za': 4, 'rh': 's', 'fin': 's', 'cs': 's', 'slack': 0, 'fbi': 2, 'off': {'g0': 1000.0, 'b0': 1400.0, 'a0': -8300.0, 'z0': 2000.0, 'c0': 3500.0, 'd0': 3600.0, 'f0': 7100.0, 'p0': -3400.0, 't0': 6600.0, 'm0': 3500.0, 'q0': 6000.0, 's0': 5800.0, 'h0': 7500.0, 'u0': 300.0, 'l0': 4500.0, 'e0': 500.0, 'k0': 15400.0, 'g1': 6000.0, 'b1': 3900.0, 'a1': 9700.0, 'z1': 6700.0, 'c1': 6100.0, 'd1': 9400.0, 'f1': 14400.0, 'p1': 12300.0, 't1': 9600.0, 'm1': 9800.0, 'q1': 6100.0, 's1': 15600.0, 'h1': 10300.0, 'u1': 9600.0, 'l1': 10800.0, 'e1': 9700.0, 'k1': 14100.0, '0': -4000.0, 'w': -6900.0, 'n': -12100.0, 'o': 11400.0}, 'bank': {'cnt1': 'C1', 'Pe': 'D1', 'FMp': 'C1', 'f': 'A1', 'um': 'A0', 'pen': 'C1', 'l': 'C3', 'ko': 'D3', 'pre': 'C0', 'uh': 'A0', 'Sg': 'D1', 'U': 'A1', 'cI': 'C2', 'cD': 'D3', 'cE': 'A2', 'cN': 'B0', 'acc': 'A0', 'nu': 'A3', 'gp': 'B2', 'qp': 'B3'}})

MATS_BF = ["I", "NI", "BO", "Mpar", "Lin", "Mf2", "RZ", "I255", "IZ", "BOb", "BOf", "Cp", "BOg", "D1", "M2", "Ls2", "DQ",
           "RU", "CI", "CD", "CE", "GI", "GE", "GD", "QD", "GN", "T0a", "T0w", "Wh", "Wl", "Ch", "SS", "SF",
           "X0", "X15", "XD", "t1", "t2", "t3", "t4", "t5", "t6", "t7", "Ub", "D2b", "I2b"]
MATS_H = ["U", "Ih", "D", "D2", "E15", "Rh", "I2", "BO2", "Sw"]
COLS = ["p", "pg", "pi", "c16", "m0", "m15", "n0", "nl15", "nl14", "bc", "bg", "bq", "cm", "cp", "a2", "aq",
        "wq", "wcd", "wce", "wgi", "wgd", "wqd", "wss", "wa", "whs", "wls", "p8", "t1", "t2", "t3", "ch", "e15", "ka"]

SCRATCH = {
    "win": ("sbuf", [128, WW], BF), "wout": ("sbuf", [128, WW], BF), "raw": ("sbuf", [128, W], BF),
    "G0": ("sbuf", [128, 16 * NS + 16], BF), "G1": ("sbuf", [128, 16 * NS + 16], BF),
    "IND": ("sbuf", [128, 32 * NS], BF), "GA": ("sbuf", [128, 32 * NS], BF),
    "ofs": ("sbuf", [128, V * 256], U16), "snd": ("sbuf", [128, V * 256], U16),
    "rNM": ("sbuf", [128, V * 512], F16), "sNM": ("sbuf", [128, V * 512], F16),
    "rST": ("sbuf", [128, V * 768], BF), "sST": ("sbuf", [128, V * 768], BF),
    "hh": ("sbuf", [128, 2 * 8 * NS], F16), "bb": ("sbuf", [128, 2 * 16 * NS], BF),
    "ii": ("sbuf", [128, 2 * NS], I32), "ff": ("sbuf", [128, 2 * 4 * NS], F32),
    "ko": ("sbuf", [128, 16], U16), "so": ("sbuf", [128, 32], U16),
    "inN": ("sbuf", [128, 256], I32), "inM": ("sbuf", [128, 256], I32), "inO": ("sbuf", [128, 256], I32),
    "inW": ("sbuf", [128, 4], I32), "inT": ("sbuf", [128, 8], I32), "ic": ("sbuf", [128, 8], I32),
    "inP": ("sbuf", [128, 256], BF), "ow": ("sbuf", [128, 512], F16),
    "X": ("sbuf", [128, 128], BF), "XQ": ("sbuf", [128, 144], BF), "QB": ("sbuf", [128, 128], BF),
    "col": ("sbuf", [128, 48], F32),
    "Zo": ("sbuf", [128, 144], BF), "Zs": ("sbuf", [128, 144], BF), "Zh": ("sbuf", [128, 144], F16),
    "mb": ("sbuf", [128, 128 * len(MATS_BF)], BF), "mh": ("sbuf", [128, 128 * len(MATS_H)], F16),
    "ones": ("sbuf", [128, NS], BF), "sm": ("sbuf", [128, 32], BF), "k1": ("sbuf", [128, 16], F32),
    "xs": ("sbuf", [128, 128], BF), "eh": ("sbuf", [128, 48], BF),
    "thb": ("sbuf", [128, 8], BF), "thg": ("sbuf", [128, 128], BF), "thc": ("sbuf", [128, 16], F32),
    "oN": ("sbuf", [128, 256], F32), "oM": ("sbuf", [128, 256], F32), "oA": ("sbuf", [128, 256], F32),
}
for _k in range(8):
    SCRATCH["K%d" % _k] = ("psum", [128, 512], F32)

DMAS = ["dN", "dM", "dO", "dP0", "dP1", "dW", "dT", "oN0", "oN1", "oM0", "oM1", "oP0", "oP1", "oA0", "oA1"] + \
       ["dD%d" % i for i in range(8)] + ["oD%d" % i for i in range(4)]
SEMAPHORES = ["sv", "ss", "st", "sg", "ls"] + DMAS + ["r%s%d%d" % (k, v, c) for k in "NMS" for v in range(1, V) for c in range(2)]


def R(buf, c0, c1, st=1, p0=0, p1=128):
    return (buf, p0, p1, c0, c1, st)


def width(r):
    return (r[4] - r[3] + r[5] - 1) // r[5]


def dtype_of(r):
    return SCRATCH[r[0]][2]


def is_ps(r):
    return r[0][0] == "K" and len(r[0]) == 2


def cut(r, i, s):
    return R(r[0], r[3] + i * s * r[5], r[3] - r[3] % r[5] + (i + 1) * s * r[5], r[5])


def part(r, p0, p1):
    return (r[0], p0, p1) + r[3:]


def cost_of(c, cfg):
    cy = cfg["cy"]

    def two(*rs):
        return all(dtype_of(r) in (BF, F16, U16) for r in rs)

    k = c[0]
    if k in ("ts", "cp"):
        if c[-1] is not None:
            return 50 + width(c[1]) * cfg["gam"] * cy
        return max(cfg["mv"], width(c[1]) * (0.5 if two(c[1], c[2]) else 1.0)) * cy
    if k == "cs":
        return 50 + width(c[2]) * cfg["sig"] * cy
    if k == "tt":
        if c[5] is not None:
            return 50 + width(c[1]) * cfg["gam"] * cy
        if c[6] is not None:
            return 50 + width(c[2]) * cfg["sig"] * cy
        return max(cfg["mv"], width(c[1]) * (1.0 if is_ps(c[2]) or is_ps(c[3]) else cfg["t2"] if two(c[2], c[3]) else 2.0)) * cy
    if k == "act":
        if c[6] is not None:
            return 65 + width(c[1]) * cfg["gam"] * cy
        return max(64.0, width(c[1])) * cy + cfg["fs"]
    if k == "mm":
        return sum(max(min(64.0, width(l)), width(r)) for l, r in c[2]) * cfg["pe"]
    if k == "mms":
        return sum(max(min(64.0, width(m[1])), width(m[2])) for m in c[1]) * cfg["pe"] * cy / 0.83
    if k == "ms":
        return max(64.0, width(c[1]) * 0.5) * cy
    if k == "iota":
        return 130 + 2 * width(c[1]) * cy
    if k == "dma":
        return cfg["di"]
    if k == "link":
        return cfg["rf"] + width(c[1]) * cfg["rb"]
    if k == "send":
        return cfg["rissue"]
    return 0.0


def build(cfg):
    ops = []
    n, nb, nc = NS, NB, 2
    lab = ["0", -1]
    loads = []

    def add(eng, ins, outs, call, **kw):
        o = dict(eng=eng, cost=cost_of(call, cfg) if call else 0.0, ins=[r for r in ins if isinstance(r, tuple)], outs=outs,
                 call=call, k=len(ops), lat=0.0, kind="c", lab=lab[0], v=lab[1], after=[], soft=[])
        o.update(kw)
        ops.append(o)
        return o

    def ts(out, a, s1, s2, o0, o1=None):
        return add("v", [a, s1, s2], [out], ("ts", out, a, s1, s2, o0, o1, None))

    def tt(out, a, b, op, sct=None, ind=None):
        return add("v", [a, b, sct, ind], [out], ("tt", out, a, b, op, ind, sct))

    def cp(out, a, ind=None):
        return add("v", [a, ind], [out], ("cp", out, a, ind))

    def act(out, a, f, bias=0.0, scale=1.0, ind=None):
        return add("s", [a, bias, scale, ind], [out], ("act", out, a, f, bias, scale, ind))

    def lin(eng, out, a, scale, bias=0.0):
        if eng == "s":
            return act(out, a, AF.Identity if bias != 0.0 else AF.Copy, bias, scale)
        return ts(out, a, scale, bias, AL.mult, AL.add)

    def mm(out, l, r, start, stop):
        return grp(out, [(l, r)], start, stop)

    def grp(out, terms, first=True, end=True):
        return add("t", [r for t in terms for r in t], [out], ("mm", out, terms, first, end))

    def ms(r, val):
        return add("v", [], [r], ("ms", r, val))

    def dma(q, sem, out, a, nbytes):
        o = add(q, [a], [out], ("dma", out, a), kind="d", sem=sem, lat=cfg["dlat"] + nbytes / cfg["dbw"], nbytes=nbytes)
        if lab[1] < 0:
            o["soft"] = [k for k in loads if ops[k]["eng"] == q][-1:]
            loads.append(o["k"])
        return o

    def send(sem, dst, src):
        s = add("g", [src], [], ("send", dst, src, sem), kind="r")
        if cfg["rb"]:
            add("x", [dst], [dst], ("link", dst), kind="a", sem=sem, src=s["k"], lat=cfg["rlat"])
        else:
            add("x", [], [dst], None, kind="a", sem=sem, src=s["k"], lat=cfg["rlat"] + width(src) * 2)

    def iota(out, pat, base, cm):
        add("g", [], [out], ("iota", out, pat, base, cm))

    def mb(name):
        i = MATS_BF.index(name)
        return R("mb", 128 * i, 128 * i + 128)

    def mh(name):
        i = MATS_H.index(name)
        return R("mh", 128 * i, 128 * i + 128)

    def col(name, p1=128):
        i = COLS.index(name)
        return R("col", i, i + 1, 1, 0, p1)

    def zs(buf, a):
        return R(buf, 16 - a, 144 - a)

    nd = cfg["ndep"]
    lq, oq = cfg["lq"], "yyyyyss" if cfg["oq"] == "old" else cfg["oq"]
    for i in range(nd):
        dma("y" if lq == "old" else lq[i], "dD%d" % i, R("raw", i * W // nd, (i + 1) * W // nd), R("dep", i * W // nd, (i + 1) * W // nd), (i + 1) * (1 << 20) // nd)
    if lq == "old":
        dma("y", "dN", R("inN", 0, 256), R("nam", 0, 256), 1180000)
        dma("y", "dT", R("inT", 0, 6, 1, 0, 8), R("thr", 0, 6, 1, 0, 8), 1180000)
        dma("y", "dW", R("inW", 0, 1), ("wt",), 1180000)
        dma("y", "dM", R("inM", 0, 256), R("mrk", 0, 256), 1300000)
        dma("y", "dO", R("inO", 0, 256), R("own", 0, 256), 1430000)
        for c in range(nc):
            dma("y", "dP%d" % c, R("rST", 3 * n * c + n, 3 * n * c + 2 * n), R("pic", n * c, n * c + n), 1500000)
    else:
        dma(lq[nd], "dN", R("inN", 0, 256), R("nam", 0, 256), 600000)
        dma(lq[nd + 1], "dT", R("inT", 0, 6, 1, 0, 8), R("thr", 0, 6, 1, 0, 8), 600000)
        dma(lq[nd + 2], "dM", R("inM", 0, 256), R("mrk", 0, 256), 600000)
        dma(lq[nd + 3], "dP0", R("inP", 0, 256), R("pic", 0, 256), 600000)
        dma(lq[nd + 4], "dO", R("inO", 0, 256), R("own", 0, 256), 600000)
        dma(lq[nd + 5], "dW", R("inW", 0, 1), ("wt",), 600000)
    X, BO, I = R("X", 0, 128), mb("BO"), mb("I")
    iota(X, [[1, 128]], 0, -1)
    iota(R("ic", 0, 1), [[1, 1]], 0, 1)
    iota(R("QB", 0, 128), [[1, 8], [0, 16]], 0, 0)
    iota(R("XQ", 0, 144), [[1, 144]], 0, 0)
    ts(I, X, 0.0, None, AL.is_equal)
    lab[0] = "n"
    cp(R("ofs", 0, 256), R("inN", 0, 256))
    lab[0] = "w"
    for i, how in enumerate(cfg["enc"]):
        s = W // len(cfg["enc"])
        x, zt, kb, out = R("raw", i * s, (i + 1) * s), R("IND", i * s, (i + 1) * s), R("K%d" % (i % 8), 0, s), R("win", i * s, (i + 1) * s)
        if how == "a":
            act(kb, x, AF.Relu, Z, -Z)
            tt(out, x, kb, AL.subtract)
        else:
            ts(zt, x, 0.0, -Z, AL.is_equal, AL.mult)
            grp(kb, [(I, x), (I, zt)])
            if how == "b":
                act(out, kb, AF.Copy)
            else:
                cp(out, kb)
    lab[0] = "0"
    for c in range(nc):
        ms(R("G%d" % c, 16 * n, 16 * n + 16), 0.0)
        ms(R("rST", 3 * n * c, 3 * n * c + n), 0.0)
    ones = R("ones", 0, n)
    ms(ones, 1.0)
    cp(col("p"), R("ic", 0, 1))
    ts(R("ic", 1, 2), R("ic", 0, 1), 4, None, AL.arith_shift_right)
    ts(R("ic", 2, 3), R("ic", 0, 1), 15, None, AL.bitwise_and)
    cp(R("col", 1, 3), R("ic", 1, 3))
    pi = col("pi")
    lin("s", col("c16"), col("pg"), 16.0, 16.0)
    ts(col("m0"), pi, 0.0, None, AL.is_equal)
    ts(col("m15"), pi, 15.0, None, AL.is_equal)
    lin("s", col("n0"), col("m0"), -1.0, 1.0)
    lin("s", col("nl15"), col("m15"), -1.0, 1.0)
    ts(col("nl14"), pi, 14.0, None, AL.is_lt)
    k1 = 1.0 if cfg["fl"][0] == "s" else 0.0
    if cfg["fl"][1] == "s":
        lin("v", col("bc"), pi, k1, k1)
    else:
        lin("v", col("bc"), pi, -k1, 0.5 - k1)
    ts(col("bg"), pi, -1.0, 0.0, AL.add, AL.max)
    lin("v", col("bq"), col("m0"), 32.0, 1.0)
    lin("s", col("cm"), pi, -1.0 / 16, 1152.0 - 15.0 / 32)
    lin("s", col("cp"), pi, PBS, PA)
    lin("s", col("a2"), col("nl15"), 2.0)
    lin("s", col("aq"), col("m15"), -17.0, 2.0)
    ts(col("wq"), col("nl14"), 32.0, col("m15"), AL.mult, AL.add)
    lin("s", col("wcd"), col("m15"), 1.5 * ALPHA, -ALPHA)
    lin("s", col("t1"), col("m15"), -BETA2)
    ts(col("wce"), col("nl14"), -ALPHA, col("t1"), AL.mult, AL.add)
    lin("s", col("wgi"), col("m0"), ALPHA + 2 * BETA, -BETA)
    lin("s", col("wgd"), col("m0"), 0.5 * ALPHA + BETA, -BETA)
    lin("s", col("wqd"), col("m0"), 0.25 - BETA - 0.5 * ALPHA, BETA + 0.5 * ALPHA)
    lin("s", col("wss"), col("nl15"), -1.0)
    lin("s", col("ch"), col("m15"), -0.5)
    lin("s", col("e15"), col("m15"), 4096.0)
    ts(col("t2"), pi, 8.0, -16.0, AL.is_ge, AL.mult)
    lin("s", col("p8"), col("t2"), 1.0, 8.0)
    ts(R("Zo", 0, 144), R("XQ", 0, 144), col("c16"), None, AL.is_equal)
    ts(BO, R("QB", 0, 128), col("pg"), None, AL.is_equal)
    ts(R("Zs", 0, 144), R("Zo", 0, 144), 1.0 / Z, None, AL.mult)
    ts(R("Zh", 0, 144), R("Zo", 0, 144), 2.0, None, AL.mult)

    def pat(out, src, a, w):
        ts(out, src, a, w, AL.is_equal, AL.mult)

    def scaled(out, src, w, eng="v"):
        if eng == "s" or cfg["cs"] == "s":
            act(out, src, AF.Copy, 0.0, w)
        else:
            ts(out, src, w, None, AL.mult)

    ts(mb("Mpar"), BO, col("m0"), -1.0, AL.mult, AL.mult)
    ts(mb("t1"), BO, 256.0, -256.0, AL.mult, AL.add)
    tt(mb("XD"), X, mb("t1"), AL.add)
    ts(mb("Lin"), mb("XD"), 0.0, None, AL.is_ge)
    ts(mb("Ls2"), mb("XD"), 1.0, col("bq"), AL.is_ge, AL.mult)
    ts(mb("t3"), mb("XD"), -0.5, 0.5, AL.max, AL.add)
    ts(mb("M2"), mb("t3"), 1.0, None, AL.min)
    pat(mb("D1"), X, 1.0, col("nl15"))
    tt(mb("t2"), I, mb("D1"), AL.subtract)
    scaled(mb("Mf2"), mb("t2"), 0.5)
    scaled(mb("GN"), mb("t2"), 0.5 * QSUM, "s")
    scaled(mb("NI"), I, -1.0, "s")
    ts(mb("RZ"), BO, col("m15"), Z, AL.mult, AL.mult)
    ts(mb("RU"), BO, col("m15"), -ALPHA, AL.mult, AL.mult)
    if not cfg["fin"]:
        scaled(mb("I255"), I, 255.0 / 256, "s")
        scaled(mb("IZ"), I, -0.5 * Z, "s")
    scaled(mb("BOb"), BO, -PBS, "s")
    scaled(mb("BOf"), BO, -PD, "s")
    scaled(mb("BOg"), BO, 100.0, "s")
    pat(mh("Sw"), X, col("p8"), 1.0)
    pat(mb("t4"), X, col("p8"), -16 * 1152.0 * PBS)
    scaled(mb("t5"), I, col("cp"), "s")
    tt(mb("Cp"), mb("t4"), mb("t5"), AL.add)
    pat(mb("DQ"), X, col("aq"), col("wq"))
    scaled(mb("CI"), mb("D1"), ALPHA, "s")
    scaled(mb("GE"), mb("D1"), BETA2, "s")
    scaled(mb("GD"), I, col("wgd"), "s")
    scaled(mb("QD"), I, col("wqd"), "s")
    ts(mb("t6"), mb("RU"), 0.0, None, AL.is_equal)
    tt(mb("X15"), X, mb("t6"), AL.mult)
    pat(mb("CD"), mb("X15"), col("nl15"), col("wcd"))
    pat(mb("CE"), mb("X15"), col("a2"), col("wce"))
    lin("s", mb("t7"), mb("Mpar"), 1.0, 1.0)
    tt(mb("X0"), X, mb("t7"), AL.mult)
    pat(mb("GI"), mb("X0"), 0.0, col("wgi"))
    scaled(mb("T0a"), zs("Zo", 0), -ALPHA, "s")
    scaled(mb("T0w"), zs("Zo", 0), QSUM + BETA2, "s")
    scaled(mb("Ch"), I, col("ch"), "s")
    pat(mb("SS"), X, col("n0"), col("wss"))
    tt(mb("SF"), zs("Zo", 0), zs("Zo", 1), AL.add)
    ts(R("ic", 4, 5), R("inW", 0, 1), 6, None, AL.arith_shift_right)
    ts(R("ic", 5, 6), R("inW", 0, 1), 63, None, AL.bitwise_and)
    ts(col("wa"), R("ic", 4, 5), 32.0, -64.0, AL.is_ge, AL.mult)
    ts(col("whs"), R("ic", 4, 5), col("wa"), 1.0 / 64, AL.add, AL.mult)
    ts(col("wls"), R("ic", 5, 6), 1.0 / 4096, None, AL.mult)
    scaled(mb("Wh"), zs("Zo", 15), col("whs"), "s")
    scaled(mb("Wl"), zs("Zo", 15), col("wls"), "s")
    pat(mh("U"), X, -1.0, col("n0"))
    cp(mh("Ih"), I)
    cp(mh("D"), mb("D1"))
    pat(mh("D2"), X, 2.0, col("nl14"))
    scaled(mh("E15"), I, col("e15"))
    scaled(mh("Rh"), I, 16 * PBS)
    if cfg["wire"] == "nm":
        scaled(mh("I2"), I, 2.0)
    else:
        scaled(mb("I2b"), I, 2.0)
        cp(mb("Ub"), mh("U"))
        cp(mb("D2b"), mh("D2"))
    scaled(mh("BO2"), BO, 2.0)
    ts(R("k1", 0, nb), R("XQ", 0, nb), 16.0, pi, AL.mult, AL.add)
    lin("s", R("sm", 0, nb), R("k1", 0, nb), -16.0, -16.0)
    ts(col("t3"), pi, 6.0, col("n0"), AL.is_le, AL.mult)
    ts(R("sm", 16, 24), R("XQ", 0, 8), col("pg"), col("t3"), AL.is_equal, AL.mult)
    if cfg["kx"] != "-":
        ts(R("sm", 24, 32), R("XQ", 0, 8), col("pg"), None, AL.is_equal)
        lin("s", col("ka"), pi, 16.0, 16.0)
        iota(R("xs", 0, 128), [[0, nc], [-256, nb], [0, 8]], 0, 0)
        ms(R("xs", 0, 128, 1, 0, 32), 0.0)
        ms(R("eh", 0, 48, 1, 0, 33), 0.0)
        cp(R("eh", 16, 32, 1, 0, 16), R("mb", I[3], I[3] + 16, 1, 0, 16))
        ms(R("eh", 16, 32, 1, 32, 33), 1.0)
    cp(R("thb", 0, 6, 1, 0, 8), R("inT", 0, 6, 1, 0, 8))
    ts(R("thg", 0, 128, 1, 0, 8), R("QB", 0, 128, 1, 0, 8), col("p", 8), None, AL.is_equal)
    mm(R("K3", 0, 6), R("thg", 0, 128, 1, 0, 8), R("thb", 0, 6, 1, 0, 8), True, True)
    if cfg["fl"][0] == "s":
        lin("v", R("thc", 0, 6), R("K3", 0, 6), -1.0, 0.5)
    else:
        cp(R("thc", 0, 6), R("K3", 0, 6))
    for c in range(nc):
        ts(R("ow", 2 * n * c, 2 * n * c + n), R("inO", n * c, n * c + n), -2048.0, 0.5, AL.add, AL.mult)
        mm(R("K%d" % (3 + 4 * c), 0, n), mh("Sw"), R("ow", 2 * n * c, 2 * n * c + n), True, True)
        cp(R("ow", 2 * n * c + n, 2 * n * c + 2 * n), R("K%d" % (3 + 4 * c), 0, n))
        ts(R("rNM", 2 * n * c, 2 * n * c + n), R("ofs", n * c, n * c + n), -2048.0, None, AL.add)
        ts(R("rNM", 2 * n * c + n, 2 * n * c + 2 * n) if cfg["wire"] == "nm" else R("rST", 3 * n * c + 2 * n, 3 * n * c + 3 * n),
           R("inM", n * c, n * c + n), 0.25, None, AL.mult)

    for v in range(V):
        last = v == V - 1
        lab[1] = v
        for c in range(nc):
            j = c if v == 0 else 2 + c
            s = n // cfg["gp"][j]
            lab[0] = "g%d" % c
            for i in range(cfg["gp"][j]):
                o = v * 256 + c * n + i * s
                out = R("G%d" % c, 16 * i * s, 16 * (i + 1) * s)
                if cfg["gv"][j] >> i & 1:
                    cp(out, R("win", 0, W), ind=R("ofs", o, o + s))
                else:
                    act(out, R("win", 0, W), AF.Copy, ind=R("ofs", o, o + s))
        if last:
            lab[0] = "o"
            s = W // len(cfg["dec"])
            for i, e in enumerate(cfg["dec"]):
                if e == "s":
                    act(R("wout", i * s, (i + 1) * s), R("win", i * s, (i + 1) * s), AF.Relu)
                else:
                    ts(R("wout", i * s, (i + 1) * s), R("win", i * s, (i + 1) * s), 0.0, None, AL.max)
        for c in range(nc):
            G = "G%d" % c
            Gw = R(G, 0, 16 * n + 16)

            def ps(name, w=n, o=0):
                q = cfg["bank"].get(name, name)
                i = int(q[1]) * n + o
                return R("K%d" % (4 * c + "ABCD".index(q[0])), i, i + w)

            def h(i, k=1):
                return R("hh", (8 * c + i) * n, (8 * c + i + k) * n)

            def b(i, k=1):
                return R("bb", (16 * c + i) * n, (16 * c + i + k) * n)

            def row(r):
                return R(G, r, 16 * n, 16)

            def ind(r):
                return R("IND", (16 * c + r) * n, (16 * c + r + 1) * n)

            def big(r):
                if cfg["za"]:
                    return R("GA", 16 * c * n + r, 16 * (c + 1) * n, 16)
                return R("GA", (16 * c + r) * n, (16 * c + r + 1) * n)

            FN, rm, Qn, Qp, hd = [h(i) for i in range(5)]
            clash, cum, FM, gt, y, ent, gg, qq, dec, xk, zle, zgt = [b(i) for i in range(12)]
            acc = [R("ff", (4 * c + i) * n, (4 * c + i + 1) * n) for i in range(4)]
            PB, BB, cnt1, cnt2 = ps("A0"), ps("A1"), ps("cnt1"), ps("B1")
            if cfg["pbs"]:
                PB = b(14)
            if cfg["pes"] == "v":
                BB = xk
            o = v * 256 + c * n
            Nh, Mq = R("rNM", 2 * o, 2 * o + n), R("rNM", 2 * o + n, 2 * o + 2 * n)
            Sin, Tin = R("rST", 3 * o, 3 * o + n), R("rST", 3 * o + n, 3 * o + 2 * n)
            Sout, Tout = R("sST", 3 * o, 3 * o + n), R("sST", 3 * o + n, 3 * o + 2 * n)
            mq = mh
            if v == 0 and lq != "old":
                Tin = R("inP", o, o + n)
            if cfg["wire"] != "nm":
                Mq, mq = R("rST", 3 * o + 2 * n, 3 * o + 3 * n), lambda a: mb(dict(U="Ub", Ih="I", D="D1", D2="D2b", I2="I2b")[a])
                if v > 0:
                    lab[0] = "f%d" % c
                    ts(Nh, R("ofs", o, o + n), -2048.0, None, AL.add)
            P = row(0)
            s = n // cfg["tp"]
            for i in range(cfg["tp"]):
                lab[0] = "b%d" % c
                act(cut(PB, i, s), cut(P, i, s), AF.Abs)
                lab[0] = "a%d" % c
                for r in range(1, 16):
                    if v > 0 and r == cfg["par"]:
                        mm(cut(cnt1, i, s), mb("Mpar"), cut(Sin, i, s), r == 1, False)
                    tt(cut(ind(r), i, s), cut(row(r), i, s), cut(PB, i, s), AL.is_gt)
                    mm(cut(cnt1, i, s), zs("Zo", r), cut(ind(r), i, s), r == 1 and (v == 0 or cfg["par"] > 1), r == 15)
            if cfg["pes"] == "t":
                grp(ps("Pe"), [(I, P)])
            elif cfg["pes"] == "s":
                act(ps("Pe"), P, AF.Copy)
            lab[0] = "c%d" % c
            if cfg["fl"][0] == "s":
                act(clash, cnt1, AF.Sign, R("thc", v, v + 1))
            else:
                ts(clash, cnt1, R("thc", v, v + 1), None, AL.is_ge)
            grp(ps("pre"), [(mb("Lin"), clash)])
            if cfg["fl"][1] == "s":
                act(cum, ps("pre"), AF.Sign, col("bc"))
            else:
                ts(cum, ps("pre"), col("bc"), None, AL.is_ge)
            lab[0] = "d%d" % c
            ko = R("ko", nb * c, nb * c + nb)
            if cfg["kx"] == "-":
                grp(ps("ko", nb), [(I, R("sm", 0, nb))] + [(zs("Zo", a), R("bb", cum[3] + a, cum[4], 16)) for a in range(16)])
                lin(cfg["cv"][1], ko, ps("ko", nb), -1.0)
            else:
                kp, kq = ps("ko", 8 * nb), ps("ko", nb, 8 * nb)
                add("t", [cum, R("sm", 24, 32)], [part(kp, 0, 16)], ("mms", [
                    (part(cut(kp, i, 8), 0, 16), cut(cum, i, 16), R("sm", 24, 32), True, True) for i in range(nb)]))
                xs = R("xs", 64 * c, 64 * c + 8 * nb)
                lin(cfg["kx"], part(xs, 0, 16), part(kp, 0, 16), 1.0)
                add("t", [part(xs, 0, 33), R("eh", 0, 48, 1, 0, 33)], [kq], ("mms", [
                    (part(kq, 32 * (i // 2), 32 * (i // 2) + 32), R("eh", 16 - 16 * (i % 2), 48 - 16 * (i % 2), 1, 0, 33),
                     R("xs", xs[3] + i, xs[4], 8, 0, 33), i % 2 == 0, i % 2 == 1) for i in range(8)]))
                lin(cfg["cv"][1], ko, kq, -1.0, col("ka"))
            if cfg["pes"] == "v":
                if cfg["aux"][0] == "p" and not last:
                    lab[0] = "b%d" % c
                    act(b(15), P, AF.Relu)
                    lab[0] = "d%d" % c
                    act(dec, Gw, AF.Relu, ind=ko)
                    tt(gt, dec, b(15), AL.is_le)
                else:
                    far, dec = dec, b(15)
                    act(dec, Gw, AF.Relu, ind=ko)
                    tt(gt, dec, P, AL.is_le)
                tt(BB, dec, gt, AL.mult)
            elif cfg["aux"][0] == "g":
                act(dec, Gw, AF.Relu, ind=ko)
            if cfg["pes"] != "v":
                act(xk, Gw, AF.Copy, ind=ko)
            if cfg["pes"] == "v":
                pass
            elif cfg["pes"] == "f":
                tt(gt, Gw, P, AL.is_gt, ind=ko)
            else:
                tt(gt, xk, ps("Pe"), AL.is_gt)
            lab[0] = "p%d" % c
            grp(ps("nu"), [(mb("NI"), P), (mb("RZ"), cum)])
            lab[0] = "d%d" % c
            if cfg["pes"] != "v":
                grp(BB, [(mb("I255"), xk)], True, False)
                grp(BB, [(mb("IZ"), gt)], False)
            lab[0] = "f%d" % c
            grp(ps("FMp"), [(mq("I2"), Mq), (mb("Mf2"), cum)])
            if cfg["fl"][2] == "s":
                act(FM, ps("FMp"), AF.Relu, -1.0, 2.0)
            else:
                ts(FM, ps("FMp"), 0.75, None, AL.is_ge)
            grp(ps("f"), [(mb("Mf2"), cum)])
            tt(FN, ps("f"), Nh, AL.mult)
            lab[0] = "z%d" % c
            zr = cfg["zr"][c]
            for r in range(1, zr + 1, 3):
                grp(cnt2, [(zs("Zs", i), row(i)) for i in range(r, min(r + 3, zr + 1))], r == 1, False)
            za = cfg["za"]
            for i in range(za if zr == 0 else 0):
                act(R("GA", (16 * c + i * 16 // za) * n, (16 * c + (i + 1) * 16 // za) * n), R(G, i * 16 // za * n, (i + 1) * 16 // za * n), AF.Abs)
            for r in range(zr + 1, 1 if za else 16):
                act(big(r), row(r), AF.Abs)
            mm(cnt2, mb("BOg"), FM, zr == 0, False)
            lab[0] = "t%d" % c
            for r in range(1, 16):
                lastcmp = tt(ind(r), row(r) if r <= zr else big(r), BB, AL.is_lt)
                mm(cnt2, zs("Zo", r), ind(r), False, r == 15)
            lab[0] = "m%d" % c
            if cfg["pes"] == "v":
                pass
            elif cfg["aux"][0] == "s":
                act(dec, xk, AF.Relu)
            elif cfg["aux"][0] == "v":
                ts(dec, xk, 0.0, None, AL.max)
            grp(ps("um"), [(BO, dec)])
            lin(cfg["cv"][0], rm, ps("um"), 1.0 / 16, col("cm"))
            grp(ps("pen"), [(mb("Cp"), ones), (mb("BOb"), dec), (mb("BOf"), FM)], True, False)
            grp(ps("pen"), [(mh("Rh"), rm)], False)
            tt(Qn, ps("pen"), R("ow", 2 * n * c, 2 * n * c + n), AL.min)
            tt(Qp, ps("pen"), R("ow", 2 * n * c + n, 2 * n * c + 2 * n), AL.min)
            lab[0] = "q%d" % c
            grp(ps("l", 2 * nb, 16), [(zs("Zh", a), R("hh", Qn[3] + a, Qp[4], 16)) for a in range(16)])
            so = R("so", 16 * c, 16 * c + 2 * nb)
            lin(cfg["cv"][2], so, ps("l", 2 * nb, 16), 1.0, QSUM + 2048.0)
            lab[0] = "s%d" % c
            if cfg["pes"] == "v" and cfg["aux"][0] == "p" and not last:
                lin(cfg["aux"][1], zle, gt, -Z)
                ts(zgt, BB, 0.0, -Z, AL.is_equal, AL.mult)
                tt(R("win", 0, WW), b(8, 2), b(10, 2), AL.add, sct=so)
            elif cfg["pes"] == "v":
                tt(far, dec, BB, AL.subtract)
                if not last:
                    ts(b(10, 2), b(8, 2), 0.0, -Z, AL.is_equal, AL.mult)
                    tt(R("win", 0, WW), b(8, 2), b(10, 2), AL.add, sct=so)
                else:
                    add("v", [b(8, 2), so], [R("wout", 0, WW)], ("cs", R("wout", 0, WW), b(8, 2), so))
            elif not last:
                lin(cfg["aux"][1], zle, gt, Z, -Z)
                lin(cfg["aux"][2], zgt, gt, -Z)
                tt(R("win", 0, WW), b(8, 2), b(10, 2), AL.add, sct=so)
            else:
                lin(cfg["aux"][1], zle, gt, -1.0, 1.0)
                tt(R("wout", 0, WW), dec, gt, AL.mult, sct=cut(so, 0, nb))
                tt(R("wout", 0, WW), dec, zle, AL.mult, sct=cut(so, 1, nb))
            lab[0] = "p%d" % c
            if cfg["mg"][1] == "1":
                tt(ps("Sg", n, n), Tin, ps("nu"), AL.min)
                grp(ps("Sg"), [(mb("SS"), Sin), (mb("SF"), FM)])
                act(R("sST", 3 * o, 3 * o + 2 * n), ps("Sg", 2 * n), AF.Abs)
            else:
                tt(y, Tin, ps("nu"), AL.min)
                act(Tout, y, AF.Abs)
                grp(ps("Sg"), [(mb("SS"), Sin), (mb("SF"), FM)])
                act(Sout, ps("Sg"), AF.Abs)
            if not last:
                if cfg["wire"] != "2":
                    send("rS%d%d" % (v + 1, c), R("rST", 3 * (o + 256), 3 * (o + 256) + 2 * n), R("sST", 3 * o, 3 * o + 2 * n))
            else:
                dma(oq[c], "oP%d" % c, R("ypic", c * n, c * n + n), Tout, 32768)
            lab[0] = "h%d" % c
            grp(ps("uh"), [(mb("Ch"), ones), (mb("Wh"), Tout), (mb("Wl"), Tout)])
            rh = R("ii", c * n, c * n + n)
            lin(cfg["rh"], rh, ps("uh"), 1.0, 2.0 ** -13)
            tt(hd, ps("uh"), rh, AL.subtract)
            if last:
                a8 = R(ps("Sg")[0], ps("Sg")[3], ps("Sg")[4], 1, 0, 8)
                grp(a8, [(R("sm", 16, 24), Sout)])
                act(R("oA", c * n, c * n + n, 1, 0, 8), a8, AF.Copy)
                if cfg["oq"] == "old":
                    dma("y", "oA%d" % c, R("ycut", c * n, c * n + n, 1, 0, 8), R("oA", c * n, c * n + n, 1, 0, 8), 4096)
                elif c == nc - 1:
                    dma(oq[2], "oA0", R("ycut", 0, 256, 1, 0, 8), R("oA", 0, 256, 1, 0, 8), 8192)
            lab[0] = "u%d" % c
            grp(ps("U"), [(mh("U"), Nh), (mq("U"), Mq), (mb("RU"), cum), (mh("E15"), hd)])
            lin(cfg["ce"], acc[0], ps("U"), 1.0)
            lab[0] = "l%d" % c
            grp(ps("cI"), [(mh("Ih"), Nh), (mq("Ih"), Mq), (mb("CI"), cum)], True, False)
            grp(ps("cD"), [(mh("D"), Nh), (mq("D"), Mq), (mb("CD"), cum), (zs("Zh", 0), FN), (mb("T0a"), FM)], True, False)
            e = grp(ps("cE"), [(mh("D2"), Nh), (mq("D2"), Mq), (mb("CE"), cum), (zs("Zh", 0), Qn), (mb("T0w"), FM)], True, False)
            if cfg["bank"]["cE"][0] == "A" and cfg["pes"] != "v":
                e["after"].append(lastcmp["k"])
            lab[0] = "e%d" % c
            act(ent, cnt2, AF.Sign, -102.5)
            grp(ps("gp"), [(mb("D1"), cum), (mb("M2"), ent)])
            grp(ps("qp"), [(mb("DQ"), cum), (mb("Ls2"), ent)])
            if cfg["mg"][0] == "1":
                act(b(6, 2), ps("gp", 2 * n), AF.Sign, col("bg"))
            else:
                act(gg, ps("gp"), AF.Sign, col("bg"))
                act(qq, ps("qp"), AF.Sign, col("bg"))
            grp(ps("cI"), [(mb("GI"), gg)], False)
            grp(ps("cE"), [(mb("GE"), gg)], False)
            grp(ps("cN"), [(mh("BO2"), Qp), (mb("GN"), gg)])
            grp(ps("cD"), [(mb("GD"), gg), (mb("QD"), qq)], False)
            tt(acc[1], acc[0], ps("cI"), AL.max)
            tt(acc[2], acc[1], ps("cE"), AL.max)
            tt(acc[3], acc[2], ps("cN"), AL.max)
            tt(ps("acc"), acc[3], ps("cD"), AL.max)
            if last and cfg["fin"]:
                oN, oM = R("oN", c * n, c * n + n), R("oM", c * n, c * n + n)
                ts(oN, ps("acc"), 3.0 * 2 ** 22, 2048.0 - 3.0 * 2 ** 22, AL.add, AL.add)
                dma(oq[3 + c], "oN%d" % c, R("ynam", c * n, c * n + n), oN, 65536)
                tt(acc[0], ps("acc"), oN, AL.subtract)
                lin(cfg["fin"], oM, acc[0], 4.0, 8192.0)
                dma(oq[5 + c], "oM%d" % c, R("ymrk", c * n, c * n + n), oM, 65536)
                continue
            nam = R("snd", o, o + n)
            lin(cfg["cv"][3], nam, ps("acc"), 1.0, 2048.0)
            Nq, Mo = R("sNM", 2 * o, 2 * o + n), R("sNM", 2 * o + n, 2 * o + 2 * n)
            if cfg["wire"] != "nm":
                Mo = R("sST", 3 * o + 2 * n, 3 * o + 3 * n)
            if not last:
                send("rN%d%d" % (v + 1, c), R("ofs", o + 256, o + 256 + n), nam)
            else:
                cp(R("oN", c * n, c * n + n), nam)
                dma(oq[3 + c], "oN%d" % c, R("ynam", c * n, c * n + n), R("oN", c * n, c * n + n), 65536)
            lab[0] = "k%d" % c
            lin(cfg["cv"][4], Nq, nam, 1.0, -2048.0)
            tt(Mo, ps("acc"), Nq, AL.subtract)
            if not last:
                if cfg["wire"] == "nm":
                    send("rM%d%d" % (v + 1, c), R("rNM", 2 * (o + 256), 2 * (o + 256) + 2 * n), R("sNM", 2 * o, 2 * o + 2 * n))
                else:
                    i = 0 if cfg["wire"] == "2" else 2 * n
                    send("rM%d%d" % (v + 1, c), R("rST", 3 * (o + 256) + i, 3 * (o + 256) + 3 * n), R("sST", 3 * o + i, 3 * o + 3 * n))
            else:
                ts(R("oM", c * n, c * n + n), Mo, 4.0, None, AL.mult)
                dma(oq[5 + c], "oM%d" % c, R("ymrk", c * n, c * n + n), R("oM", c * n, c * n + n), 65536)
        if last:
            dma("y", "oD0", R("ydep", 0, W), R("wout", 0, W), 1 << 20)
    return ops


def overlap(a, b):
    if a[0] != b[0] or len(a) == 1:
        return False
    if a[2] <= b[1] or b[2] <= a[1] or a[4] <= b[3] or b[4] <= a[3]:
        return False
    return True


def depend(ops):
    touch = {}
    lastmm = {}
    for o in ops:
        deps = set(o["after"] + o["soft"])
        for r in o["ins"]:
            for (k, w, q) in touch.get(r[0], ()):
                if w and overlap(r, q):
                    deps.add(k)
        for r in o["outs"]:
            lst = touch.setdefault(r[0], [])
            for (k, w, q) in lst:
                if overlap(r, q):
                    deps.add(k)
            if r[5] == 1:
                lst[:] = [e for e in lst if not (r[1] <= e[2][1] and e[2][2] <= r[2] and r[3] <= e[2][3] and e[2][4] <= r[4])]
        for r in o["ins"]:
            if len(r) > 1:
                touch.setdefault(r[0], []).append((o["k"], False, r))
        for r in o["outs"]:
            touch[r[0]].append((o["k"], True, r))
        if o["eng"] == "t":
            bank = o["outs"][0][0]
            if bank in lastmm:
                deps.add(lastmm[bank])
            lastmm[bank] = o["k"]
        if o["kind"] == "a":
            deps = {o["src"]}
        deps.discard(o["k"])
        o["base"] = deps
        o["banks"] = {r[0] for r in o["ins"] + o["outs"] if is_ps(r)}


def hop(a, b, cfg):
    if a["k"] in b["soft"]:
        return -a["lat"]
    if a["eng"] == b["eng"] and a["kind"] == "c":
        return 0.0 if a["eng"] == "t" else cfg["shop"]
    return 0.0 if b["kind"] == "a" else cfg["hop"] + (cfg["ht"] if a["eng"] == "t" else 0.0)


def place(ops, seq, pre, gap):
    t0 = [0.0] * len(ops)
    lines = {}

    def clear(key, eng, t, c, m):
        a = lines.get(key)
        if not a:
            return t
        lo, hi = 0, len(a)
        while lo < hi:
            mid = (lo + hi) // 2
            if a[mid][1] + m <= t:
                lo = mid + 1
            else:
                hi = mid
        while lo < len(a) and a[lo][0] < t + c + m:
            if a[lo][2] != eng and a[lo][1] + m > t:
                t = a[lo][1] + m
            lo += 1
        return t

    for k in seq:
        o = ops[k]
        t = max([t0[d] + w for d, w in pre[k] if d >= 0] + [w for d, w in pre[k] if d < 0] + [0.0])
        c = o["cost"]
        if c > 0.0:
            while True:
                t1 = clear(o["eng"], None, t, c, 0.0)
                for bk in o["banks"]:
                    t1 = clear(bk, o["eng"], t1, c, gap)
                if t1 == t:
                    break
                t = t1
            for key in [o["eng"]] + list(o["banks"]):
                a = lines.setdefault(key, [])
                i = len(a)
                while i and a[i - 1][0] > t:
                    i -= 1
                a.insert(i, (t, t + c, o["eng"]))
        t0[k] = t
    return t0


def follow(ops, key, fw, bw, cfg):
    free = {e: 0.0 for e in "vstgyx"}
    left = [len(o["base"]) for o in ops]
    rt = [0.0] * len(ops)
    t0 = [0.0] * len(ops)
    ready = [o["k"] for o in ops if not o["base"]]
    bank = {}
    while ready:
        est = {}
        for k in ready:
            o = ops[k]
            t = max(rt[k], free[o["eng"]])
            for b in o["banks"]:
                for e, f in bank.get(b, {}).items():
                    if e != o["eng"]:
                        t = max(t, f + cfg["hop"])
            est[k] = t
        best = min(ready, key=lambda k: (est[k], -key[k]))
        lim, e0 = est[best] + cfg["slack"], ops[best]["eng"]
        for k in ready:
            if ops[k]["eng"] == e0 and est[k] <= lim and key[k] > key[best]:
                best = k
        o = ops[best]
        ready.remove(best)
        t0[best] = est[best]
        if o["cost"] > 0.0:
            free[o["eng"]] = t0[best] + o["cost"]
        for b in o["banks"]:
            bank.setdefault(b, {})[o["eng"]] = t0[best] + o["cost"]
        for s, w in bw[best]:
            if s >= 0:
                left[s] -= 1
                if left[s] == 0:
                    rt[s] = max(t0[d] + w2 for d, w2 in fw[s])
                    ready.append(s)
    return t0


def arrange(ops, cfg):
    fw = [[(d, ops[d]["cost"] + ops[d]["lat"] + hop(ops[d], o, cfg)) for d in o["base"]] for o in ops]
    bw = [[(-1, o["lat"])] for o in ops]
    for o in ops:
        for d in o["base"]:
            bw[d].append((o["k"], o["cost"] + ops[d]["lat"] + hop(ops[d], o, cfg)))
    pri = [0.0] * len(ops)
    nxt = {}
    for o in reversed(ops):
        pri[o["k"]] = o["cost"] + max(pri[s] - ops[s]["cost"] + w if s >= 0 else w for s, w in bw[o["k"]])
        if o["lab"][0] in cfg["runs"]:
            run = (o["eng"], o["lab"], o["v"])
            pri[o["k"]] = max(pri[o["k"]], o["cost"] + nxt.get(run, 0.0))
            nxt[run] = pri[o["k"]]
    key = [pri[o["k"]] + cfg["off"].get(o["lab"], 0.0) for o in ops]
    if cfg["period"]:
        prev = {}
        for o in ops:
            own = cfg["off"].get({0: "X", V - 1: "Y"}.get(o["v"], "-") + o["lab"], 0.0)
            t = max([cfg["off"].get(o["lab"], 0.0) + own + cfg["period"] * max(o["v"], 0)] +
                    [w - key[d] for d, w in fw[o["k"]] if ops[d]["v"] == o["v"]])
            if o["lab"][0] in cfg["runs"]:
                run = (o["eng"], o["lab"], o["v"])
                t = max(t, prev.get(run, t))
                prev[run] = t + o["cost"]
            key[o["k"]] = -t
    if cfg["slack"] < 0:
        for o in ops:
            for d in o["base"]:
                key[o["k"]] = min(key[o["k"]], key[d])
        t0 = place(ops, sorted(range(len(ops)), key=lambda k: (-key[k], k)), fw, cfg["hop"])
    else:
        t0 = follow(ops, key, fw, bw, cfg)
    best = (max(t0[o["k"]] + o["cost"] + o["lat"] for o in ops), t0)
    for _ in range(cfg["fbi"]):
        u = place(ops, sorted(range(len(ops)), key=lambda k: (-(t0[k] + ops[k]["cost"]), -k)), bw, cfg["hop"])
        t0 = place(ops, sorted(range(len(ops)), key=lambda k: (-(u[k] + ops[k]["cost"]), k)), fw, cfg["hop"])
        end = max(t0[o["k"]] + o["cost"] + o["lat"] for o in ops)
        if end < best[0]:
            best = (end, t0)
    order = sorted(ops, key=lambda o: (best[1][o["k"]], o["k"]))
    bank = {}
    for o in order:
        o["t0"] = best[1][o["k"]]
        o["fin"] = o["t0"] + o["cost"] + o["lat"]
        o["deps"] = set(o["base"])
        for k in o["banks"]:
            for e, q in bank.get(k, {}).items():
                if e != o["eng"]:
                    o["deps"].add(q["k"])
            bank.setdefault(k, {})[o["eng"]] = o
    return order


def schedule(cfg):
    ops = build(cfg)
    depend(ops)
    order = arrange(ops, cfg)
    cnt = {e: 0 for e in "vstg"}
    known = {e: {} for e in "vstgy"}
    for o in order:
        if o["kind"] == "a":
            o["sig"], o["clock"] = (o["sem"], 1), {}
            continue
        e = o["eng"]
        waits = {}
        for d in sorted(o["deps"], key=lambda d: -ops[d]["fin"]):
            q = ops[d]
            if q["kind"] == "r" or (e == "t" and q["eng"] == "t") or d in o["soft"]:
                continue
            s, val = q["sig"]
            if known[e].get(s, 0) >= val:
                continue
            waits[s] = max(waits.get(s, 0), val)
            known[e][s] = val
            for s2, v2 in q["clock"].items():
                if known[e].get(s2, 0) < v2:
                    known[e][s2] = v2
        o["waits"] = waits
        o["clock"] = dict(known[e])
        if o["kind"] == "c":
            cnt[e] += 1
            o["sig"] = ("s" + e, cnt[e])
        elif o["kind"] == "d":
            o["sig"] = (o["sem"], 16)
    return order, cnt


PLAN = []


def rank_program(g, core, T, topo):
    rank = T.rank_of(core)
    if rank is None:
        return
    if not PLAN:
        PLAN.append(schedule(CFG))
    order, cnt = PLAN[0]
    nxt = T.cores[(rank + 1) % len(T.cores)]
    prv = T.cores[(rank - 1) % len(T.cores)]
    rid, pid = topo.addr(nxt)[:2]
    mask = topo.mask(core, nxt)
    nout = len(topo.engines(core, nxt))
    nin = len(topo.engines(prv, core))
    Q = {"v": g.vector, "s": g.scalar, "t": g.tensor, "g": g, "y": g.sync}

    def A(r, ind=None):
        if not isinstance(r, tuple):
            return r
        if len(r) == 1:
            return T[r[0]][:]
        a = T[r[0]][r[1]:r[2], r[3]:r[4]] if r[5] == 1 else T[r[0]][r[1]:r[2], r[3]:r[4]:r[5]]
        return a if ind is None else a.indirect(A(ind))

    sends = 0
    for o in order:
        if o["kind"] == "a":
            continue
        q = Q[o["eng"]]
        for s, val in o["waits"].items():
            q.wait_ge(T.sem[s], val * nin if s[0] == "r" else val)
        c = o["call"]
        if c[0] == "ts":
            if c[6] is None:
                i = q.tensor_scalar(A(c[1]), A(c[2], c[7]), A(c[3]), None, c[5])
            else:
                i = q.tensor_scalar(A(c[1]), A(c[2], c[7]), A(c[3]), A(c[4]), c[5], c[6])
        elif c[0] == "tt":
            i = q.tensor_tensor(A(c[1], c[6]), A(c[2], c[5]), A(c[3]), c[4])
        elif c[0] == "cs":
            i = q.tensor_copy(A(c[1], c[3]), A(c[2]))
        elif c[0] == "cp":
            i = q.tensor_copy(A(c[1]), A(c[2], c[3]))
        elif c[0] == "act":
            if c[3] == AF.Copy:
                i = q.activation(A(c[1]), A(c[2], c[6]), c[3], scale=A(c[5]))
            else:
                i = q.activation(A(c[1]), A(c[2], c[6]), c[3], bias=A(c[4]), scale=A(c[5]))
        elif c[0] == "mm":
            for j, (l, r) in enumerate(c[2]):
                i = q.matmul(A(c[1]), A(l), A(r), c[3] and j == 0, c[4] and j == len(c[2]) - 1)
        elif c[0] == "mms":
            for m in c[1]:
                i = q.matmul(A(m[0]), A(m[1]), A(m[2]), m[3], m[4])
        elif c[0] == "ms":
            i = q.memset(A(c[1]), c[2])
        elif c[0] == "iota":
            if dtype_of(c[1]) == I32:
                i = q.iota(A(c[1]), c[2], c[3], c[4])
            else:
                i = q.iota(A(c[1]), c[2], c[3], c[4], allow_small_or_imprecise_dtypes=True)
        elif c[0] == "dma":
            q.dma_start(A(c[1]), A(c[2])).then_inc(T.sem[o["sem"]], 16)
            continue
        else:
            q.remote_dma(A(c[1]), A(c[2]), T.sem[c[3]], T.sem.ls, pid, rid, mask)
            sends += 1
            continue
        i.then_inc(T.sem[o["sig"][0]], 1)
    g.wait_ge(T.sem.ls, sends * nout)
    for e in "vstg":
        g.wait_ge(T.sem["s" + e], cnt[e])
    for o in order:
        if o["kind"] == "d":
            g.wait_ge(T.sem[o["sem"]], 16)
